import numpy as np
import ml_dtypes


def mxq(x, axis, fmt="e4m3"):
    dtype, down = {"e4m3": (ml_dtypes.float8_e4m3fn, 7), "e5m2": (ml_dtypes.float8_e5m2, 14)}[fmt]
    v = np.moveaxis(np.asarray(x, np.float32).astype(ml_dtypes.bfloat16).astype(np.float64), axis, -1)
    blocks = v.reshape(v.shape[:-1] + (-1, 32))
    amax = np.abs(blocks).max(-1, keepdims=True)
    byte = np.maximum(np.where(amax > 0, np.frexp(amax)[1] - 1 + 127, 0) - down, 1)
    scale = np.exp2(byte - 127.0)
    codes = (blocks / scale).astype(np.float32).astype(dtype).astype(np.float64)
    return np.moveaxis((codes * scale).reshape(v.shape), -1, axis)


WIDE = False


def mx_kscale(k):
    if not WIDE:
        return np.ones(k)
    levels = np.array([18, -18])
    if k % 512:
        return np.exp2(np.random.permutation(np.resize(levels, k // 32))).repeat(32)
    a = np.empty((k // 512, 16))
    for p in range(k // 512):
        a[p, :8] = np.random.permutation(np.resize(levels, 8))
        for g in range(8):
            far = levels[np.abs(levels - a[p, g]) >= 10]
            a[p, g + 8] = far[np.random.randint(len(far))]
    return np.exp2(a.ravel()).repeat(32)


def f64(x):
    return np.asarray(x).astype(np.float64)


def striped(idx):
    return np.tile(np.asarray(idx).reshape(-1, 16).T, (8, 1)).astype(np.uint16)


def unstriped(offs):
    return offs[:16].T.reshape(-1).astype(np.int64)


E2M1 = np.array([0.0, 0.5, 1.0, 1.5, 2.0, 3.0, 4.0, 6.0, -0.0, -0.5, -1.0, -1.5, -2.0, -3.0, -4.0, -6.0])


def pack_weight(w, fmt):
    k, n = w.shape
    w = f64(np.asarray(w, np.float32).astype(ml_dtypes.bfloat16)).reshape(k // 32, 32, n)
    amax = np.abs(w).max(1)
    if fmt == "e4m3":
        byte = np.frexp(amax)[1] - 1 + 127 - 7
    else:
        mant, ex = np.frexp(amax / 6.0)
        byte = np.where(mant > 0.5, ex, ex - 1) + 127
    byte = np.clip(np.where(amax > 0, byte, 1), 1, 254)
    scaled = (w * np.exp2(127.0 - byte)[:, None, :]).reshape(k, n).astype(np.float32)
    by_word = np.ascontiguousarray(scaled.reshape(k // 512, 128, 4, n).transpose(0, 1, 3, 2))
    if fmt == "e4m3":
        words = by_word.astype(ml_dtypes.float8_e4m3fn).view(np.uint8)
    else:
        c = by_word.astype(ml_dtypes.float4_e2m1fn).view(np.uint8) & 0xF
        words = (c[..., 0::2] | (c[..., 1::2] << 4)).reshape(k // 512, 128, 2 * n)
    return np.ascontiguousarray(words), np.ascontiguousarray(byte.astype(np.uint8).reshape(k // 512, 16, n))


def unpack_weight(words, scales, fmt):
    g, _, n = scales.shape
    words = np.ascontiguousarray(words).reshape(g, 128, n, -1)
    if fmt == "e4m3":
        vals = words.view(ml_dtypes.float8_e4m3fn).astype(np.float64)
    else:
        nib = np.empty((g, 128, n, 4), np.uint8)
        nib[..., 0::2] = words & 0xF
        nib[..., 1::2] = words >> 4
        vals = E2M1[nib]
    vals = vals * np.repeat(np.exp2(scales.astype(np.float64) - 127.0), 8, axis=1)[..., None]
    return vals.transpose(0, 1, 3, 2).reshape(g * 512, n)


B, N, T, D, R = 1, 512, 2048, 1024, 512


def setup_inputs():
    n = np.random.standard_normal
    idx = np.random.permutation(T)[:B * N]
    s = mx_kscale(D)[:, None]
    z = mx_kscale(R)[:, None]
    q = n((B, D, R))
    do = n((B, D, R))
    cp = pack_weight(n((D, T)) * (1.00 / np.sqrt(D)) / s, "e2m1")
    return {
        "qT": (q * s).astype(np.float32),
        "c_words": np.ascontiguousarray(cp[0].reshape(1, 2, 128, T, 2).transpose(0, 2, 3, 1, 4)).reshape(1, 128, T, 4),
        "c_scales": cp[1],
        "doT": (do * s).astype(np.float32),
        "rw": (np.random.uniform(0.5, 1.5, (B, R, 1)) * 1.0 / np.sqrt(R) * z).astype(np.float32),
        "qm": (q.transpose(0, 2, 1) / z).astype(np.float32),
        "dom": (do.transpose(0, 2, 1) / z).astype(np.float32),
        "offs": striped(idx),
    }


def reference(qT, c_words, c_scales, doT, rw, qm, dom, offs):
    idx = unstriped(offs)
    c = unpack_weight(c_words.reshape(1, 128, T, 2, 2).transpose(0, 3, 1, 2, 4).reshape(2, 128, 2 * T), c_scales, "e2m1")
    pick = lambda x: x[:, idx].reshape(x.shape[0], B, N).transpose(1, 0, 2)
    cq = pick(c)
    a = mxq(f64(qT), 1, "e4m3").transpose(0, 2, 1) @ cq
    p = 1.0 / (1.0 + np.exp(-a))
    dp = mxq(f64(doT), 1, "e5m2").transpose(0, 2, 1) @ cq
    ds = f64(rw) * dp * p * (1.0 - p)
    dk = mxq(f64(qm), 1, "e4m3").transpose(0, 2, 1) @ mxq(ds, 1, "e5m2")
    dv = mxq(f64(dom), 1, "e5m2").transpose(0, 2, 1) @ mxq(f64(rw) * p, 1, "e4m3")
    gc = np.zeros((D, T))
    gc[:, idx] = (dk + dv).transpose(1, 0, 2).reshape(D, B * N)
    return gc

@@ -1,0 +1,188 @@
+from contextlib import ExitStack
+
+import concourse.mybir as mybir
+
+N, T, D, R = 512, 2048, 1024, 512
+FLOPS = 4 * 2 * D * R * N
+
+F32 = mybir.dt.float32
+BF16 = mybir.dt.bfloat16
+I32 = mybir.dt.int32
+U32 = mybir.dt.uint32
+U16 = mybir.dt.uint16
+U8 = mybir.dt.uint8
+E4M3 = mybir.dt.float8_e4m3fn_x4
+E5M2 = mybir.dt.float8_e5m2_x4
+E2M1 = mybir.dt.float4_e2m1fn_x4
+MULT = mybir.AluOpType.mult
+ADD = mybir.AluOpType.add
+SUB = mybir.AluOpType.subtract
+SIGMOID = mybir.ActivationFunctionType.Sigmoid
+COPY = mybir.ActivationFunctionType.Copy
+
+P = 128
+PACK = 4
+K_PASS = P * PACK
+PASSES = D // K_PASS
+WINDOWS = 3
+D_CHUNKS = (256, 256, 512)
+D_STEP = 256
+SHARE = 88
+
+
+def tile_attend_gat_sig_c_kernel(tc, qT, c_words, c_scales, doT, rw, qm, dom, offs, out):
+    nc = tc.nc
+    with ExitStack() as ctx:
+        sb = ctx.enter_context(tc.tile_pool(name="sb", bufs=1))
+        ps = ctx.enter_context(tc.psum_pool(name="ps", bufs=1))
+
+        def tile(name, shape, dtype):
+            return sb.tile(shape, dtype, name=name, align_bytes=64)
+
+        def bank(b, name):
+            return ps.tile([P, N], F32, name=name, tag="bank%d" % b)
+
+        offsets = sb.tile([P, N // 16], U16, name="offsets")
+        nc.sync.dma_start(offsets[:], offs)
+
+        def load_rows(name, rows):
+            raw = tile(name, [P, PACK, rows.shape[1]], F32)
+            nc.sync.dma_start(out=raw[:], in_=rows.rearrange("(p j) w -> p j w", j=PACK))
+            return raw
+
+        q_raw = [load_rows("q_raw0", qT[0, 0:K_PASS, :])]
+
+        pool_scales = tile("pool_scales", [P, PASSES * T // 4], I32)
+        nc.vector.memset(pool_scales[:], 0)
+        warm_in = tile("warm_in", [P, 1], F32)
+        warm_out = tile("warm_out", [P, 1], F32)
+        nc.vector.memset(warm_in[:], 0.0)
+        scale_rows = c_scales.bitcast(I32)
+        for quad in range(4):
+            nc.scalar.dma_start(
+                out=pool_scales[32 * quad : 32 * quad + 4, :].rearrange("f (o t) -> f o t", o=PASSES),
+                in_=scale_rows[:, 4 * quad : 4 * quad + 4, :].rearrange("o f t -> f o t"),
+            )
+        gate = tile("gate", [P, PACK], F32)
+        nc.scalar.dma_start(out=gate[:], in_=rw[0].rearrange("(p t) o -> p (t o)", t=PACK))
+        nc.scalar.activation(out=warm_out[:], in_=warm_in[:], func=SIGMOID)
+
+        pool_words = tile("pool_words", [P, T], I32)
+        nc.sync.dma_start(out=pool_words[:], in_=c_words[0].rearrange("p t b -> p (t b)").bitcast(I32))
+        q_raw.append(load_rows("q_raw1", qT[0, K_PASS:D, :]))
+        do_raw = [load_rows("do_raw%d" % o, doT[0, o * K_PASS : (o + 1) * K_PASS, :]) for o in range(PASSES)]
+        qm_raw, dom_raw = [], []
+        d0 = 0
+        for c, width in enumerate(D_CHUNKS):
+            dom_c = load_rows("dom_raw%d" % c, dom[0, :, d0 : d0 + width])
+            qm_c = load_rows("qm_raw%d" % c, qm[0, :, d0 : d0 + width])
+            for s0 in range(0, width, D_STEP):
+                dom_raw.append(dom_c[:, :, s0 : s0 + D_STEP])
+                qm_raw.append(qm_c[:, :, s0 : s0 + D_STEP])
+            d0 += width
+
+        windows = [tile("window%d" % w, [P, T], F32) for w in range(WINDOWS)]
+        for window in windows:
+            nc.vector.memset(window[:], 0.0)
+
+        neg_gate = tile("neg_gate", [P, PACK], F32)
+        nc.gpsimd.tensor_scalar(neg_gate[:], gate[:], -1.0, 0.0, MULT, ADD)
+
+        c_sc = [tile("c_sc%d" % o, [P, N], U8) for o in range(PASSES)]
+        for o in range(PASSES):
+            nc.vector.tensor_copy(c_sc[o][:], pool_scales[:].bitcast(U8)[:, o * T : (o + 1) * T].indirect(offsets[:]))
+        word_pairs = tile("word_pairs", [P, N], U32)
+        nc.vector.tensor_copy(word_pairs[:], pool_words[:].bitcast(U32).indirect(offsets[:]))
+        c_codes = tile("c_codes", [P, PASSES * 2 * N], U8)
+        nc.vector.tensor_copy(
+            c_codes[:].bitcast(U16).rearrange("p (o n) -> p o n", o=PASSES),
+            word_pairs[:].bitcast(U16).rearrange("p (n o) -> p o n", o=PASSES),
+        )
+
+        def quantize(name, grouped, fmt):
+            words = grouped.shape[1] // PACK
+            codes = tile(name + "_codes", [P, words], U32)
+            scales = tile(name + "_scales", [P, words], U8)
+            nc.vector.quantize_mx(out=codes[:].bitcast(fmt), scales=scales[:], in_=grouped)
+            return codes, scales
+
+        def group_queries(name, raw, share):
+            grouped = tile(name, [P, PACK * R], BF16)
+            dst = grouped[:].rearrange("p (t m j) -> p m j t", t=PACK, j=PACK)
+            src = raw[:].rearrange("p j (m t) -> p m j t", t=PACK)
+            if share > 0:
+                nc.vector.tensor_copy(dst[:, 0:share], src[:, 0:share])
+            if share < P:
+                nc.scalar.copy(dst[:, share:P], src[:, share:P])
+            return grouped[:]
+
+        def interleave(name, copy, rows):
+            grouped = tile(name, [P, PACK * rows.shape[2]], BF16)
+            copy(
+                grouped[:].rearrange("p (c i t) -> p c t i", i=4, t=PACK),
+                rows.rearrange("p t (c i) -> p c t i", i=4),
+            )
+            return grouped[:]
+
+        def score_pass(banks, operand, fmt, o):
+            codes, scales = operand
+            for t in range(PACK):
+                cols = slice(t * P, (t + 1) * P)
+                nc.tensor.matmul_mx(
+                    out=banks[t][:],
+                    lhsT=codes[:, cols].bitcast(fmt),
+                    lhsT_scale=scales[:, cols],
+                    rhs=c_codes[:, o * 2 * N : (o + 1) * 2 * N].bitcast(E2M1),
+                    rhs_scale=c_sc[o][:],
+                    start=(o == 0),
+                    stop=(o == PASSES - 1),
+                )
+
+        a_banks = [bank(t, "a%d" % t) for t in range(PACK)]
+        dp_banks = [bank(PACK + t, "dp%d" % t) for t in range(PACK)]
+        for o, share in enumerate((0, SHARE)):
+            q_mx = quantize("q%d" % o, group_queries("q_bf%d" % o, q_raw[o], share), E4M3)
+            score_pass(a_banks, q_mx, E4M3, o)
+        prob = tile("prob", [P, PACK, N], F32)
+        for t in range(PACK):
+            nc.scalar.activation(out=prob[:, t, :], in_=a_banks[t][:], func=SIGMOID)
+        for o, share in enumerate((P, SHARE)):
+            do_mx = quantize("do%d" % o, group_queries("do_bf%d" % o, do_raw[o], share), E5M2)
+            score_pass(dp_banks, do_mx, E5M2, o)
+
+        neg_slope = tile("neg_slope", [P, PACK, N], F32)
+        ds_rows = tile("ds_rows", [P, PACK, N], BF16)
+        pw_rows = tile("pw_rows", [P, PACK, N], BF16)
+        for t in range(PACK):
+            nc.vector.scalar_tensor_tensor(neg_slope[:, t, :], prob[:, t, :], 1.0, prob[:, t, :], SUB, MULT)
+        for t in range(PACK):
+            nc.vector.scalar_tensor_tensor(
+                ds_rows[:, t, :], dp_banks[t][:], neg_gate[:, t : t + 1], neg_slope[:, t, :], MULT, MULT
+            )
+        for t in range(PACK):
+            nc.scalar.activation(out=pw_rows[:, t, :], in_=prob[:, t, :], func=COPY, scale=gate[:, t : t + 1])
+        pw_bf = interleave("pw_bf", nc.scalar.copy, pw_rows[:])
+        ds_bf = interleave("ds_bf", nc.vector.tensor_copy, ds_rows[:])
+        ds_codes, ds_scales = quantize("ds", ds_bf, E5M2)
+        pw_codes, pw_scales = quantize("pw", pw_bf, E4M3)
+
+        for c in range(D // D_STEP):
+            dom_codes, dom_scales = quantize("dom%d" % c, interleave("dom_bf%d" % c, nc.scalar.copy, dom_raw[c]), E5M2)
+            qm_codes, qm_scales = quantize("qm%d" % c, interleave("qm_bf%d" % c, nc.scalar.copy, qm_raw[c]), E4M3)
+            for s in range(D_STEP // P):
+                b = c * (D_STEP // P) + s
+                cols = slice(s * P, (s + 1) * P)
+                acc = bank(b, "grad%d" % b)
+                nc.tensor.matmul_mx(
+                    out=acc[:], lhsT=dom_codes[:, cols].bitcast(E5M2), lhsT_scale=dom_scales[:, cols],
+                    rhs=pw_codes[:].bitcast(E4M3), rhs_scale=pw_scales[:], start=True, stop=False,
+                )
+                nc.tensor.matmul_mx(
+                    out=acc[:], lhsT=qm_codes[:, cols].bitcast(E4M3), lhsT_scale=qm_scales[:, cols],
+                    rhs=ds_codes[:].bitcast(E5M2), rhs_scale=ds_scales[:], start=False, stop=True,
+                )
+                grad = tile("grad_sb%d" % b, [P, N], F32)
+                nc.scalar.copy(grad[:], acc[:])
+                window = windows[b % WINDOWS]
+                nc.vector.tensor_copy(window[:].indirect(offsets[:]), grad[:])
+                nc.sync.dma_start(out=out[b * P : (b + 1) * P, :], in_=window[:])

@@ -24,20 +24,27 @@ P = 128
 PACK = 4
 K_PASS = P * PACK
 PASSES = D // K_PASS
-WINDOWS = 3
-D_CHUNKS = (256, 256, 512)
-D_STEP = 256
-SHARE = 88
+LOAD_WIDTHS = (256, 256, 512)
+STEP_WIDTHS = ((128, 128), (256,), (256, 256))
+Q_SHARES = (104, 24)
+DO_SHARES = (64, 112)
+DS_SHARE = 112
+PW_SHARE = 48
+FIRST_SHARE = 0
+PW_ROWS_ON_VECTOR = 0
+COPIES_ON_VECTOR = 0
+AHEAD = 0
 
 
 def tile_attend_gat_sig_c_kernel(tc, qT, c_words, c_scales, doT, rw, qm, dom, offs, out):
     nc = tc.nc
     with ExitStack() as ctx:
         sb = ctx.enter_context(tc.tile_pool(name="sb", bufs=1))
+        stage = ctx.enter_context(tc.tile_pool(name="stage", bufs=4))
         ps = ctx.enter_context(tc.psum_pool(name="ps", bufs=1))
 
-        def tile(name, shape, dtype):
-            return sb.tile(shape, dtype, name=name, align_bytes=64)
+        def tile(name, shape, dtype, tag=None):
+            return sb.tile(shape, dtype, name=name, tag=tag or name, align_bytes=64)
 
         def bank(b, name):
             return ps.tile([P, N], F32, name=name, tag="bank%d" % b)
@@ -46,17 +53,18 @@ def tile_attend_gat_sig_c_kernel(tc, qT, c_words, c_scales, doT, rw, qm, dom, of
         nc.sync.dma_start(offsets[:], offs)
 
         def load_rows(name, rows):
-            raw = tile(name, [P, PACK, rows.shape[1]], F32)
+            raw = stage.tile([P, PACK, rows.shape[1]], F32, name=name, tag="staged", align_bytes=64)
             nc.sync.dma_start(out=raw[:], in_=rows.rearrange("(p j) w -> p j w", j=PACK))
             return raw
 
-        q_raw = [load_rows("q_raw0", qT[0, 0:K_PASS, :])]
+        pool_words = stage.tile([P, T], I32, name="pool_words", tag="staged", align_bytes=64)
+        nc.sync.dma_start(out=pool_words[:], in_=c_words[0].rearrange("p t b -> p (t b)").bitcast(I32))
 
         pool_scales = tile("pool_scales", [P, PASSES * T // 4], I32)
-        nc.vector.memset(pool_scales[:], 0)
+        nc.gpsimd.memset(pool_scales[:], 0)
         warm_in = tile("warm_in", [P, 1], F32)
         warm_out = tile("warm_out", [P, 1], F32)
-        nc.vector.memset(warm_in[:], 0.0)
+        nc.gpsimd.memset(warm_in[:], 0.0)
         scale_rows = c_scales.bitcast(I32)
         for quad in range(4):
             nc.scalar.dma_start(
@@ -67,30 +75,29 @@ def tile_attend_gat_sig_c_kernel(tc, qT, c_words, c_scales, doT, rw, qm, dom, of
         nc.scalar.dma_start(out=gate[:], in_=rw[0].rearrange("(p t) o -> p (t o)", t=PACK))
         nc.scalar.activation(out=warm_out[:], in_=warm_in[:], func=SIGMOID)
 
-        pool_words = tile("pool_words", [P, T], I32)
-        nc.sync.dma_start(out=pool_words[:], in_=c_words[0].rearrange("p t b -> p (t b)").bitcast(I32))
-        q_raw.append(load_rows("q_raw1", qT[0, K_PASS:D, :]))
+        q_raw = [load_rows("q_raw%d" % o, qT[0, o * K_PASS : (o + 1) * K_PASS, :]) for o in range(PASSES)]
         do_raw = [load_rows("do_raw%d" % o, doT[0, o * K_PASS : (o + 1) * K_PASS, :]) for o in range(PASSES)]
         qm_raw, dom_raw = [], []
         d0 = 0
-        for c, width in enumerate(D_CHUNKS):
+        for c, width in enumerate(LOAD_WIDTHS):
             dom_c = load_rows("dom_raw%d" % c, dom[0, :, d0 : d0 + width])
             qm_c = load_rows("qm_raw%d" % c, qm[0, :, d0 : d0 + width])
-            for s0 in range(0, width, D_STEP):
-                dom_raw.append(dom_c[:, :, s0 : s0 + D_STEP])
-                qm_raw.append(qm_c[:, :, s0 : s0 + D_STEP])
+            s0 = 0
+            for step in STEP_WIDTHS[c]:
+                dom_raw.append(dom_c[:, :, s0 : s0 + step])
+                qm_raw.append(qm_c[:, :, s0 : s0 + step])
+                s0 += step
             d0 += width
 
-        windows = [tile("window%d" % w, [P, T], F32) for w in range(WINDOWS)]
-        for window in windows:
-            nc.vector.memset(window[:], 0.0)
+        windows = [tile("window%d" % w, [P, T], F32) for w in range(3)]
+        nc.gpsimd.memset(windows[0][:], 0.0)
+        for window in windows[1:]:
+            nc.vector.memset(window[:, 0 : T // 2 - 1], 0.0)
+            nc.vector.memset(window[:, T // 2 - 1 : T], 0.0)
 
         neg_gate = tile("neg_gate", [P, PACK], F32)
         nc.gpsimd.tensor_scalar(neg_gate[:], gate[:], -1.0, 0.0, MULT, ADD)
 
-        c_sc = [tile("c_sc%d" % o, [P, N], U8) for o in range(PASSES)]
-        for o in range(PASSES):
-            nc.vector.tensor_copy(c_sc[o][:], pool_scales[:].bitcast(U8)[:, o * T : (o + 1) * T].indirect(offsets[:]))
         word_pairs = tile("word_pairs", [P, N], U32)
         nc.vector.tensor_copy(word_pairs[:], pool_words[:].bitcast(U32).indirect(offsets[:]))
         c_codes = tile("c_codes", [P, PASSES * 2 * N], U8)
@@ -98,6 +105,7 @@ def tile_attend_gat_sig_c_kernel(tc, qT, c_words, c_scales, doT, rw, qm, dom, of
             c_codes[:].bitcast(U16).rearrange("p (o n) -> p o n", o=PASSES),
             word_pairs[:].bitcast(U16).rearrange("p (n o) -> p o n", o=PASSES),
         )
+        c_sc = [tile("c_sc%d" % o, [P, N], U8) for o in range(PASSES)]
 
         def quantize(name, grouped, fmt):
             words = grouped.shape[1] // PACK
@@ -106,21 +114,27 @@ def tile_attend_gat_sig_c_kernel(tc, qT, c_words, c_scales, doT, rw, qm, dom, of
             nc.vector.quantize_mx(out=codes[:].bitcast(fmt), scales=scales[:], in_=grouped)
             return codes, scales
 
-        def group_queries(name, raw, share):
-            grouped = tile(name, [P, PACK * R], BF16)
-            dst = grouped[:].rearrange("p (t m j) -> p m j t", t=PACK, j=PACK)
-            src = raw[:].rearrange("p j (m t) -> p m j t", t=PACK)
+        def shared_copy(dst, src, share):
             if share > 0:
                 nc.vector.tensor_copy(dst[:, 0:share], src[:, 0:share])
-            if share < P:
-                nc.scalar.copy(dst[:, share:P], src[:, share:P])
+            if share < dst.shape[1]:
+                nc.scalar.copy(dst[:, share:], src[:, share:])
+
+        def group_queries(name, raw, share):
+            grouped = tile(name, [P, PACK * R], BF16)
+            shared_copy(
+                grouped[:].rearrange("p (t m j) -> p m t j", t=PACK, j=PACK),
+                raw[:].rearrange("p j (m t) -> p m t j", t=PACK),
+                share,
+            )
             return grouped[:]
 
-        def interleave(name, copy, rows):
+        def interleave(name, rows, share):
             grouped = tile(name, [P, PACK * rows.shape[2]], BF16)
-            copy(
+            shared_copy(
                 grouped[:].rearrange("p (c i t) -> p c t i", i=4, t=PACK),
                 rows.rearrange("p t (c i) -> p c t i", i=4),
+                share,
             )
             return grouped[:]
 
@@ -140,38 +154,55 @@ def tile_attend_gat_sig_c_kernel(tc, qT, c_words, c_scales, doT, rw, qm, dom, of
 
         a_banks = [bank(t, "a%d" % t) for t in range(PACK)]
         dp_banks = [bank(PACK + t, "dp%d" % t) for t in range(PACK)]
-        for o, share in enumerate((0, SHARE)):
+        for o, share in enumerate(Q_SHARES):
+            nc.vector.tensor_copy(c_sc[o][:], pool_scales[:].bitcast(U8)[:, o * T : (o + 1) * T].indirect(offsets[:]))
             q_mx = quantize("q%d" % o, group_queries("q_bf%d" % o, q_raw[o], share), E4M3)
             score_pass(a_banks, q_mx, E4M3, o)
         prob = tile("prob", [P, PACK, N], F32)
         for t in range(PACK):
             nc.scalar.activation(out=prob[:, t, :], in_=a_banks[t][:], func=SIGMOID)
-        for o, share in enumerate((P, SHARE)):
+        for o, share in enumerate(DO_SHARES):
             do_mx = quantize("do%d" % o, group_queries("do_bf%d" % o, do_raw[o], share), E5M2)
             score_pass(dp_banks, do_mx, E5M2, o)
 
         neg_slope = tile("neg_slope", [P, PACK, N], F32)
         ds_rows = tile("ds_rows", [P, PACK, N], BF16)
         pw_rows = tile("pw_rows", [P, PACK, N], BF16)
+        operands = {}
+
+        def query_operands(c):
+            if c < len(dom_raw) and c not in operands:
+                share = FIRST_SHARE if c == 0 else 0
+                dom_mx = quantize("dom%d" % c, interleave("dom_bf%d" % c, dom_raw[c], share), E5M2)
+                qm_mx = quantize("qm%d" % c, interleave("qm_bf%d" % c, qm_raw[c], share), E4M3)
+                operands[c] = (dom_mx, qm_mx)
+
+        for t in range(PACK):
+            if t < PW_ROWS_ON_VECTOR:
+                nc.vector.tensor_scalar(pw_rows[:, t, :], prob[:, t, :], gate[:, t : t + 1], None, MULT)
+            else:
+                nc.scalar.activation(out=pw_rows[:, t, :], in_=prob[:, t, :], func=COPY, scale=gate[:, t : t + 1])
         for t in range(PACK):
             nc.vector.scalar_tensor_tensor(neg_slope[:, t, :], prob[:, t, :], 1.0, prob[:, t, :], SUB, MULT)
         for t in range(PACK):
             nc.vector.scalar_tensor_tensor(
                 ds_rows[:, t, :], dp_banks[t][:], neg_gate[:, t : t + 1], neg_slope[:, t, :], MULT, MULT
             )
-        for t in range(PACK):
-            nc.scalar.activation(out=pw_rows[:, t, :], in_=prob[:, t, :], func=COPY, scale=gate[:, t : t + 1])
-        pw_bf = interleave("pw_bf", nc.scalar.copy, pw_rows[:])
-        ds_bf = interleave("ds_bf", nc.vector.tensor_copy, ds_rows[:])
-        ds_codes, ds_scales = quantize("ds", ds_bf, E5M2)
+        pw_bf = interleave("pw_bf", pw_rows[:], PW_SHARE)
+        query_operands(0)
+        ds_bf = interleave("ds_bf", ds_rows[:], DS_SHARE)
         pw_codes, pw_scales = quantize("pw", pw_bf, E4M3)
+        ds_codes, ds_scales = quantize("ds", ds_bf, E5M2)
 
-        for c in range(D // D_STEP):
-            dom_codes, dom_scales = quantize("dom%d" % c, interleave("dom_bf%d" % c, nc.scalar.copy, dom_raw[c]), E5M2)
-            qm_codes, qm_scales = quantize("qm%d" % c, interleave("qm_bf%d" % c, nc.scalar.copy, qm_raw[c]), E4M3)
-            for s in range(D_STEP // P):
-                b = c * (D_STEP // P) + s
-                cols = slice(s * P, (s + 1) * P)
+        first = 0
+        for c in range(len(dom_raw)):
+            for ahead in range(AHEAD + 1):
+                query_operands(c + ahead)
+            (dom_codes, dom_scales), (qm_codes, qm_scales) = operands[c]
+            blocks = range(first, first + dom_raw[c].shape[2] // P)
+            grads = {}
+            for b in blocks:
+                cols = slice((b - first) * P, (b - first + 1) * P)
                 acc = bank(b, "grad%d" % b)
                 nc.tensor.matmul_mx(
                     out=acc[:], lhsT=dom_codes[:, cols].bitcast(E5M2), lhsT_scale=dom_scales[:, cols],
@@ -181,8 +212,10 @@ def tile_attend_gat_sig_c_kernel(tc, qT, c_words, c_scales, doT, rw, qm, dom, of
                     out=acc[:], lhsT=qm_codes[:, cols].bitcast(E4M3), lhsT_scale=qm_scales[:, cols],
                     rhs=ds_codes[:].bitcast(E5M2), rhs_scale=ds_scales[:], start=False, stop=True,
                 )
-                grad = tile("grad_sb%d" % b, [P, N], F32)
-                nc.scalar.copy(grad[:], acc[:])
-                window = windows[b % WINDOWS]
-                nc.vector.tensor_copy(window[:].indirect(offsets[:]), grad[:])
+                grads[b] = tile("grad_sb%d" % b, [P, N], F32)
+                copy = nc.vector.tensor_copy if b < COPIES_ON_VECTOR else nc.scalar.copy
+                copy(grads[b][:], acc[:])
+                window = windows[b % len(windows)]
+                nc.vector.tensor_copy(window[:].indirect(offsets[:]), grads[b][:])
                 nc.sync.dma_start(out=out[b * P : (b + 1) * P, :], in_=window[:])
+            first = blocks.stop

@@ -26,21 +26,23 @@ K_PASS = P * PACK
 PASSES = D // K_PASS
 LOAD_WIDTHS = (256, 256, 512)
 STEP_WIDTHS = ((128, 128), (256,), (256, 256))
-Q_SHARES = (104, 24)
-DO_SHARES = (64, 112)
-DS_SHARE = 112
-PW_SHARE = 48
-FIRST_SHARE = 0
+Q_SHARES = ((0, 64), (96,))
+DO_SHARES = ((64, 64), (32, 40))
+DS_SHARE = 80
+PW_SHARE = 16
 PW_ROWS_ON_VECTOR = 0
-COPIES_ON_VECTOR = 0
-AHEAD = 0
+STAGES = 8
+WINDOWS = 3
+COPIES_ON_VECTOR = 1
+FIRST_EARLY = True
+FIRST_ON_GPSIMD = False
 
 
 def tile_attend_gat_sig_c_kernel(tc, qT, c_words, c_scales, doT, rw, qm, dom, offs, out):
     nc = tc.nc
     with ExitStack() as ctx:
         sb = ctx.enter_context(tc.tile_pool(name="sb", bufs=1))
-        stage = ctx.enter_context(tc.tile_pool(name="stage", bufs=4))
+        stage = ctx.enter_context(tc.tile_pool(name="stage", bufs=STAGES))
         ps = ctx.enter_context(tc.psum_pool(name="ps", bufs=1))
 
         def tile(name, shape, dtype, tag=None):
@@ -49,34 +51,53 @@ def tile_attend_gat_sig_c_kernel(tc, qT, c_words, c_scales, doT, rw, qm, dom, of
         def bank(b, name):
             return ps.tile([P, N], F32, name=name, tag="bank%d" % b)
 
-        offsets = sb.tile([P, N // 16], U16, name="offsets")
-        nc.sync.dma_start(offsets[:], offs)
-
         def load_rows(name, rows):
             raw = stage.tile([P, PACK, rows.shape[1]], F32, name=name, tag="staged", align_bytes=64)
             nc.sync.dma_start(out=raw[:], in_=rows.rearrange("(p j) w -> p j w", j=PACK))
             return raw
 
-        pool_words = stage.tile([P, T], I32, name="pool_words", tag="staged", align_bytes=64)
+        pool_scales = tile("pool_scales", [P, T // 4 + 1], I32)
+        nc.sync.dma_start(out=pool_scales[0:32, 0 : T // 4], in_=c_scales.bitcast(I32).rearrange("o f t -> (o f) t"))
+        offsets = sb.tile([P, N // 16], U16, name="offsets")
+        nc.sync.dma_start(offsets[:], offs)
+        pool_words = tile("pool_words", [P, T], I32)
         nc.sync.dma_start(out=pool_words[:], in_=c_words[0].rearrange("p t b -> p (t b)").bitcast(I32))
 
-        pool_scales = tile("pool_scales", [P, PASSES * T // 4], I32)
-        nc.gpsimd.memset(pool_scales[:], 0)
         warm_in = tile("warm_in", [P, 1], F32)
         warm_out = tile("warm_out", [P, 1], F32)
         nc.gpsimd.memset(warm_in[:], 0.0)
-        scale_rows = c_scales.bitcast(I32)
-        for quad in range(4):
-            nc.scalar.dma_start(
-                out=pool_scales[32 * quad : 32 * quad + 4, :].rearrange("f (o t) -> f o t", o=PASSES),
-                in_=scale_rows[:, 4 * quad : 4 * quad + 4, :].rearrange("o f t -> f o t"),
-            )
-        gate = tile("gate", [P, PACK], F32)
-        nc.scalar.dma_start(out=gate[:], in_=rw[0].rearrange("(p t) o -> p (t o)", t=PACK))
+        nc.vector.memset(pool_scales[32:64, :], 0)
+        nc.vector.memset(pool_scales[64:128, :], 0)
+        c_sc = tile("c_sc", [P, PASSES * N // 4], I32)
+        nc.gpsimd.memset(c_sc[:], 0)
         nc.scalar.activation(out=warm_out[:], in_=warm_in[:], func=SIGMOID)
 
-        q_raw = [load_rows("q_raw%d" % o, qT[0, o * K_PASS : (o + 1) * K_PASS, :]) for o in range(PASSES)]
-        do_raw = [load_rows("do_raw%d" % o, doT[0, o * K_PASS : (o + 1) * K_PASS, :]) for o in range(PASSES)]
+        picked = tile("picked", [P, N], U8)
+        nc.vector.tensor_copy(picked[:], pool_scales[:, 0 : T // 4].bitcast(U8).indirect(offsets[:]))
+        for o in range(PASSES):
+            for quad in range(4):
+                row = 16 * o + 4 * quad
+                nc.scalar.dma_start(
+                    out=c_sc[32 * quad : 32 * quad + 4, o * N // 4 : (o + 1) * N // 4],
+                    in_=picked[row : row + 4, :].bitcast(I32),
+                )
+
+        def load_pieces(name, src, shares):
+            return [
+                [
+                    load_rows(
+                        "%s%d_%d" % (name, o, h),
+                        src[0, o * K_PASS : (o + 1) * K_PASS, h * R // len(parts) : (h + 1) * R // len(parts)],
+                    )
+                    for h in range(len(parts))
+                ]
+                for o, parts in enumerate(shares)
+            ]
+
+        q_raw = load_pieces("q_raw", qT, Q_SHARES)
+        gate = tile("gate", [P, PACK], F32)
+        nc.sync.dma_start(out=gate[:], in_=rw[0].rearrange("(p t) o -> p (t o)", t=PACK))
+        do_raw = load_pieces("do_raw", doT, DO_SHARES)
         qm_raw, dom_raw = [], []
         d0 = 0
         for c, width in enumerate(LOAD_WIDTHS):
@@ -89,11 +110,12 @@ def tile_attend_gat_sig_c_kernel(tc, qT, c_words, c_scales, doT, rw, qm, dom, of
                 s0 += step
             d0 += width
 
-        windows = [tile("window%d" % w, [P, T], F32) for w in range(3)]
-        nc.gpsimd.memset(windows[0][:], 0.0)
-        for window in windows[1:]:
-            nc.vector.memset(window[:, 0 : T // 2 - 1], 0.0)
-            nc.vector.memset(window[:, T // 2 - 1 : T], 0.0)
+        windows = [tile("window%d" % w, [P, T], F32) for w in range(WINDOWS)]
+        for window in windows[:-1]:
+            nc.gpsimd.memset(window[:], 0.0)
+        nc.vector.memset(windows[-1][:, 0 : T // 2 - 1], 0.0)
+        nc.vector.memset(windows[-1][:, T // 2 - 1 : T // 2], 0.0)
+        nc.gpsimd.memset(windows[-1][:, T // 2 : T], 0.0)
 
         neg_gate = tile("neg_gate", [P, PACK], F32)
         nc.gpsimd.tensor_scalar(neg_gate[:], gate[:], -1.0, 0.0, MULT, ADD)
@@ -105,13 +127,18 @@ def tile_attend_gat_sig_c_kernel(tc, qT, c_words, c_scales, doT, rw, qm, dom, of
             c_codes[:].bitcast(U16).rearrange("p (o n) -> p o n", o=PASSES),
             word_pairs[:].bitcast(U16).rearrange("p (n o) -> p o n", o=PASSES),
         )
-        c_sc = [tile("c_sc%d" % o, [P, N], U8) for o in range(PASSES)]
 
-        def quantize(name, grouped, fmt):
+        def quantize(name, grouped, fmt, pieces=1):
             words = grouped.shape[1] // PACK
             codes = tile(name + "_codes", [P, words], U32)
             scales = tile(name + "_scales", [P, words], U8)
-            nc.vector.quantize_mx(out=codes[:].bitcast(fmt), scales=scales[:], in_=grouped)
+            step = words // pieces
+            for w0 in range(0, words, step):
+                nc.vector.quantize_mx(
+                    out=codes[:, w0 : w0 + step].bitcast(fmt),
+                    scales=scales[:, w0 : w0 + step],
+                    in_=grouped[:, PACK * w0 : PACK * (w0 + step)],
+                )
             return codes, scales
 
         def shared_copy(dst, src, share):
@@ -120,22 +147,25 @@ def tile_attend_gat_sig_c_kernel(tc, qT, c_words, c_scales, doT, rw, qm, dom, of
             if share < dst.shape[1]:
                 nc.scalar.copy(dst[:, share:], src[:, share:])
 
-        def group_queries(name, raw, share):
+        def group_queries(name, halves, shares):
             grouped = tile(name, [P, PACK * R], BF16)
-            shared_copy(
-                grouped[:].rearrange("p (t m j) -> p m t j", t=PACK, j=PACK),
-                raw[:].rearrange("p j (m t) -> p m t j", t=PACK),
-                share,
-            )
+            dst = grouped[:].rearrange("p (t m j) -> p m t j", t=PACK, j=PACK)
+            for h, raw in enumerate(halves):
+                shared_copy(
+                    dst[:, h * P // len(halves) : (h + 1) * P // len(halves)],
+                    raw[:].rearrange("p j (m t) -> p m t j", t=PACK),
+                    shares[h],
+                )
             return grouped[:]
 
-        def interleave(name, rows, share):
-            grouped = tile(name, [P, PACK * rows.shape[2]], BF16)
-            shared_copy(
-                grouped[:].rearrange("p (c i t) -> p c t i", i=4, t=PACK),
-                rows.rearrange("p t (c i) -> p c t i", i=4),
-                share,
-            )
+        def interleave(name, rows, share, tag=None, copy=None):
+            grouped = tile(name, [P, PACK * rows.shape[2]], BF16, tag=tag)
+            dst = grouped[:].rearrange("p (c i t) -> p c t i", i=4, t=PACK)
+            src = rows.rearrange("p t (c i) -> p c t i", i=4)
+            if copy:
+                copy(dst, src)
+            else:
+                shared_copy(dst, src, share)
             return grouped[:]
 
         def score_pass(banks, operand, fmt, o):
@@ -147,22 +177,21 @@ def tile_attend_gat_sig_c_kernel(tc, qT, c_words, c_scales, doT, rw, qm, dom, of
                     lhsT=codes[:, cols].bitcast(fmt),
                     lhsT_scale=scales[:, cols],
                     rhs=c_codes[:, o * 2 * N : (o + 1) * 2 * N].bitcast(E2M1),
-                    rhs_scale=c_sc[o][:],
+                    rhs_scale=c_sc[:].bitcast(U8)[:, o * N : (o + 1) * N],
                     start=(o == 0),
                     stop=(o == PASSES - 1),
                 )
 
         a_banks = [bank(t, "a%d" % t) for t in range(PACK)]
         dp_banks = [bank(PACK + t, "dp%d" % t) for t in range(PACK)]
-        for o, share in enumerate(Q_SHARES):
-            nc.vector.tensor_copy(c_sc[o][:], pool_scales[:].bitcast(U8)[:, o * T : (o + 1) * T].indirect(offsets[:]))
-            q_mx = quantize("q%d" % o, group_queries("q_bf%d" % o, q_raw[o], share), E4M3)
+        for o, shares in enumerate(Q_SHARES):
+            q_mx = quantize("q%d" % o, group_queries("q_bf%d" % o, q_raw[o], shares), E4M3, 1 + 3 * o)
             score_pass(a_banks, q_mx, E4M3, o)
         prob = tile("prob", [P, PACK, N], F32)
         for t in range(PACK):
             nc.scalar.activation(out=prob[:, t, :], in_=a_banks[t][:], func=SIGMOID)
-        for o, share in enumerate(DO_SHARES):
-            do_mx = quantize("do%d" % o, group_queries("do_bf%d" % o, do_raw[o], share), E5M2)
+        for o, shares in enumerate(DO_SHARES):
+            do_mx = quantize("do%d" % o, group_queries("do_bf%d" % o, do_raw[o], shares), E5M2, 1 + 3 * o)
             score_pass(dp_banks, do_mx, E5M2, o)
 
         neg_slope = tile("neg_slope", [P, PACK, N], F32)
@@ -171,11 +200,13 @@ def tile_attend_gat_sig_c_kernel(tc, qT, c_words, c_scales, doT, rw, qm, dom, of
         operands = {}
 
         def query_operands(c):
-            if c < len(dom_raw) and c not in operands:
-                share = FIRST_SHARE if c == 0 else 0
-                dom_mx = quantize("dom%d" % c, interleave("dom_bf%d" % c, dom_raw[c], share), E5M2)
-                qm_mx = quantize("qm%d" % c, interleave("qm_bf%d" % c, qm_raw[c], share), E4M3)
-                operands[c] = (dom_mx, qm_mx)
+            if c == 0 and FIRST_ON_GPSIMD:
+                dom_bf = interleave("dom_bf0", dom_raw[0], 0, "do_bf1", nc.gpsimd.tensor_copy)
+                qm_bf = interleave("qm_bf0", qm_raw[0], 0, "do_bf0", nc.gpsimd.tensor_copy)
+            else:
+                dom_bf = interleave("dom_bf%d" % c, dom_raw[c], 0)
+                qm_bf = interleave("qm_bf%d" % c, qm_raw[c], 0)
+            operands[c] = (quantize("dom%d" % c, dom_bf, E5M2), quantize("qm%d" % c, qm_bf, E4M3))
 
         for t in range(PACK):
             if t < PW_ROWS_ON_VECTOR:
@@ -189,18 +220,18 @@ def tile_attend_gat_sig_c_kernel(tc, qT, c_words, c_scales, doT, rw, qm, dom, of
                 ds_rows[:, t, :], dp_banks[t][:], neg_gate[:, t : t + 1], neg_slope[:, t, :], MULT, MULT
             )
         pw_bf = interleave("pw_bf", pw_rows[:], PW_SHARE)
-        query_operands(0)
+        if FIRST_EARLY:
+            query_operands(0)
         ds_bf = interleave("ds_bf", ds_rows[:], DS_SHARE)
         pw_codes, pw_scales = quantize("pw", pw_bf, E4M3)
         ds_codes, ds_scales = quantize("ds", ds_bf, E5M2)
 
         first = 0
         for c in range(len(dom_raw)):
-            for ahead in range(AHEAD + 1):
-                query_operands(c + ahead)
+            if c not in operands:
+                query_operands(c)
             (dom_codes, dom_scales), (qm_codes, qm_scales) = operands[c]
             blocks = range(first, first + dom_raw[c].shape[2] // P)
-            grads = {}
             for b in blocks:
                 cols = slice((b - first) * P, (b - first + 1) * P)
                 acc = bank(b, "grad%d" % b)
@@ -212,10 +243,10 @@ def tile_attend_gat_sig_c_kernel(tc, qT, c_words, c_scales, doT, rw, qm, dom, of
                     out=acc[:], lhsT=qm_codes[:, cols].bitcast(E4M3), lhsT_scale=qm_scales[:, cols],
                     rhs=ds_codes[:].bitcast(E5M2), rhs_scale=ds_scales[:], start=False, stop=True,
                 )
-                grads[b] = tile("grad_sb%d" % b, [P, N], F32)
+                grad = tile("grad_sb%d" % b, [P, N], F32)
                 copy = nc.vector.tensor_copy if b < COPIES_ON_VECTOR else nc.scalar.copy
-                copy(grads[b][:], acc[:])
+                copy(grad[:], acc[:])
                 window = windows[b % len(windows)]
-                nc.vector.tensor_copy(window[:].indirect(offsets[:]), grads[b][:])
+                nc.vector.tensor_copy(window[:].indirect(offsets[:]), grad[:])
                 nc.sync.dma_start(out=out[b * P : (b + 1) * P, :], in_=window[:])
             first = blocks.stop

@@ -26,15 +26,20 @@ K_PASS = P * PACK
 PASSES = D // K_PASS
 LOAD_WIDTHS = (256, 256, 512)
 STEP_WIDTHS = ((128, 128), (256,), (256, 256))
-Q_SHARES = ((0, 64), (96,))
-DO_SHARES = ((64, 64), (32, 40))
-DS_SHARE = 80
-PW_SHARE = 16
-PW_ROWS_ON_VECTOR = 0
-STAGES = 8
+Q_SHARES = ((0, 64), (64, 44))
+DO_SHARES = ((64, 64), (0, 40))
+DS_SHARE = 112
+PW_SHARE = 0
+PW_ROWS_ON_VECTOR = 2
+STAGES = 6
 WINDOWS = 3
+FIRST_PARTS = 2
+PW_ON_GPSIMD = 0
+LATE_TAG = "neg_slope"
+LATE_FROM = 1
+PW_QUANT_EARLY = True
 COPIES_ON_VECTOR = 1
-FIRST_EARLY = True
+FIRST_EARLY = False
 FIRST_ON_GPSIMD = False
 
 
@@ -56,31 +61,24 @@ def tile_attend_gat_sig_c_kernel(tc, qT, c_words, c_scales, doT, rw, qm, dom, of
             nc.sync.dma_start(out=raw[:], in_=rows.rearrange("(p j) w -> p j w", j=PACK))
             return raw
 
-        pool_scales = tile("pool_scales", [P, T // 4 + 1], I32)
-        nc.sync.dma_start(out=pool_scales[0:32, 0 : T // 4], in_=c_scales.bitcast(I32).rearrange("o f t -> (o f) t"))
-        offsets = sb.tile([P, N // 16], U16, name="offsets")
-        nc.sync.dma_start(offsets[:], offs)
         pool_words = tile("pool_words", [P, T], I32)
         nc.sync.dma_start(out=pool_words[:], in_=c_words[0].rearrange("p t b -> p (t b)").bitcast(I32))
+        offsets = sb.tile([P, N // 16], U16, name="offsets")
+        nc.sync.dma_start(offsets[:], offs)
 
+        pool_scales = tile("pool_scales", [P, T // 4], I32)
+        nc.gpsimd.memset(pool_scales[:], 0)
+        scale_rows = c_scales.bitcast(I32)
+        for quad in range(4):
+            nc.sync.dma_start(
+                out=pool_scales[32 * quad : 32 * quad + 8, :], in_=scale_rows[:, 4 * quad : 4 * quad + 4, :]
+            )
+        gate = tile("gate", [P, PACK], F32)
+        nc.scalar.dma_start(out=gate[:], in_=rw[0].rearrange("(p t) o -> p (t o)", t=PACK))
         warm_in = tile("warm_in", [P, 1], F32)
         warm_out = tile("warm_out", [P, 1], F32)
         nc.gpsimd.memset(warm_in[:], 0.0)
-        nc.vector.memset(pool_scales[32:64, :], 0)
-        nc.vector.memset(pool_scales[64:128, :], 0)
-        c_sc = tile("c_sc", [P, PASSES * N // 4], I32)
-        nc.gpsimd.memset(c_sc[:], 0)
         nc.scalar.activation(out=warm_out[:], in_=warm_in[:], func=SIGMOID)
-
-        picked = tile("picked", [P, N], U8)
-        nc.vector.tensor_copy(picked[:], pool_scales[:, 0 : T // 4].bitcast(U8).indirect(offsets[:]))
-        for o in range(PASSES):
-            for quad in range(4):
-                row = 16 * o + 4 * quad
-                nc.scalar.dma_start(
-                    out=c_sc[32 * quad : 32 * quad + 4, o * N // 4 : (o + 1) * N // 4],
-                    in_=picked[row : row + 4, :].bitcast(I32),
-                )
 
         def load_pieces(name, src, shares):
             return [
@@ -95,8 +93,28 @@ def tile_attend_gat_sig_c_kernel(tc, qT, c_words, c_scales, doT, rw, qm, dom, of
             ]
 
         q_raw = load_pieces("q_raw", qT, Q_SHARES)
-        gate = tile("gate", [P, PACK], F32)
-        nc.sync.dma_start(out=gate[:], in_=rw[0].rearrange("(p t) o -> p (t o)", t=PACK))
+        windows = [tile("window%d" % w, [P, T], F32) for w in range(WINDOWS)]
+        nc.gpsimd.memset(windows[0][:], 0.0)
+        nc.vector.memset(windows[1][:, 0 : T // 2 - 1], 0.0)
+        nc.vector.memset(windows[1][:, T // 2 - 1 : T], 0.0)
+        nc.vector.memset(windows[2][:, 0 : T // 2 - 1], 0.0)
+        nc.vector.memset(windows[2][:, T // 2 - 1 : T // 2], 0.0)
+        nc.gpsimd.memset(windows[2][:, T // 2 : T], 0.0)
+
+        neg_gate = tile("neg_gate", [P, PACK], F32)
+        nc.gpsimd.tensor_scalar(neg_gate[:], gate[:], -1.0, 0.0, MULT, ADD)
+
+        word_pairs = tile("word_pairs", [P, N], U32)
+        nc.vector.tensor_copy(word_pairs[:], pool_words[:].bitcast(U32).indirect(offsets[:]))
+        c_sc = [tile("c_sc%d" % o, [P, N], U8) for o in range(PASSES)]
+        nc.vector.tensor_copy(c_sc[0][:], pool_scales[:].bitcast(U8).indirect(offsets[:]))
+        c_codes = tile("c_codes", [P, PASSES * 2 * N], U8, tag="pool_scales")
+        nc.vector.tensor_copy(
+            c_codes[:].bitcast(U16).rearrange("p (o n) -> p o n", o=PASSES),
+            word_pairs[:].bitcast(U16).rearrange("p (n o) -> p o n", o=PASSES),
+        )
+        nc.gpsimd.memset(c_sc[1][:].bitcast(I32), 0)
+        nc.sync.dma_start(out=c_sc[1][0 : P - 4, :].bitcast(I32), in_=c_sc[0][4:P, :].bitcast(I32))
         do_raw = load_pieces("do_raw", doT, DO_SHARES)
         qm_raw, dom_raw = [], []
         d0 = 0
@@ -109,24 +127,6 @@ def tile_attend_gat_sig_c_kernel(tc, qT, c_words, c_scales, doT, rw, qm, dom, of
                 qm_raw.append(qm_c[:, :, s0 : s0 + step])
                 s0 += step
             d0 += width
-
-        windows = [tile("window%d" % w, [P, T], F32) for w in range(WINDOWS)]
-        for window in windows[:-1]:
-            nc.gpsimd.memset(window[:], 0.0)
-        nc.vector.memset(windows[-1][:, 0 : T // 2 - 1], 0.0)
-        nc.vector.memset(windows[-1][:, T // 2 - 1 : T // 2], 0.0)
-        nc.gpsimd.memset(windows[-1][:, T // 2 : T], 0.0)
-
-        neg_gate = tile("neg_gate", [P, PACK], F32)
-        nc.gpsimd.tensor_scalar(neg_gate[:], gate[:], -1.0, 0.0, MULT, ADD)
-
-        word_pairs = tile("word_pairs", [P, N], U32)
-        nc.vector.tensor_copy(word_pairs[:], pool_words[:].bitcast(U32).indirect(offsets[:]))
-        c_codes = tile("c_codes", [P, PASSES * 2 * N], U8)
-        nc.vector.tensor_copy(
-            c_codes[:].bitcast(U16).rearrange("p (o n) -> p o n", o=PASSES),
-            word_pairs[:].bitcast(U16).rearrange("p (n o) -> p o n", o=PASSES),
-        )
 
         def quantize(name, grouped, fmt, pieces=1):
             words = grouped.shape[1] // PACK
@@ -158,15 +158,22 @@ def tile_attend_gat_sig_c_kernel(tc, qT, c_words, c_scales, doT, rw, qm, dom, of
                 )
             return grouped[:]
 
-        def interleave(name, rows, share, tag=None, copy=None):
-            grouped = tile(name, [P, PACK * rows.shape[2]], BF16, tag=tag)
-            dst = grouped[:].rearrange("p (c i t) -> p c t i", i=4, t=PACK)
+        def interleave(name, rows, share, tag=None, copy=None, into=None):
+            grouped = tile(name, [P, PACK * rows.shape[2]], BF16, tag=tag)[:] if into is None else into
+            dst = grouped.rearrange("p (c i t) -> p c t i", i=4, t=PACK)
             src = rows.rearrange("p t (c i) -> p c t i", i=4)
             if copy:
                 copy(dst, src)
             else:
                 shared_copy(dst, src, share)
-            return grouped[:]
+            return grouped
+
+        def interleave_on_gpsimd(name, rows, tag):
+            grouped = tile(name, [P, PACK * rows.shape[2]], BF16, tag=tag)[:]
+            nc.gpsimd.tensor_scalar(
+                grouped.rearrange("p (n t) -> p n t", t=PACK), rows.rearrange("p t n -> p n t"), 1.0, 0.0, MULT, ADD
+            )
+            return grouped
 
         def score_pass(banks, operand, fmt, o):
             codes, scales = operand
@@ -177,7 +184,7 @@ def tile_attend_gat_sig_c_kernel(tc, qT, c_words, c_scales, doT, rw, qm, dom, of
                     lhsT=codes[:, cols].bitcast(fmt),
                     lhsT_scale=scales[:, cols],
                     rhs=c_codes[:, o * 2 * N : (o + 1) * 2 * N].bitcast(E2M1),
-                    rhs_scale=c_sc[:].bitcast(U8)[:, o * N : (o + 1) * N],
+                    rhs_scale=c_sc[o][:],
                     start=(o == 0),
                     stop=(o == PASSES - 1),
                 )
@@ -198,11 +205,19 @@ def tile_attend_gat_sig_c_kernel(tc, qT, c_words, c_scales, doT, rw, qm, dom, of
         ds_rows = tile("ds_rows", [P, PACK, N], BF16)
         pw_rows = tile("pw_rows", [P, PACK, N], BF16)
         operands = {}
+        late = []
 
         def query_operands(c):
             if c == 0 and FIRST_ON_GPSIMD:
-                dom_bf = interleave("dom_bf0", dom_raw[0], 0, "do_bf1", nc.gpsimd.tensor_copy)
-                qm_bf = interleave("qm_bf0", qm_raw[0], 0, "do_bf0", nc.gpsimd.tensor_copy)
+                dom_bf = interleave_on_gpsimd("dom_bf0", dom_raw[0], "do_bf1")
+                qm_bf = interleave_on_gpsimd("qm_bf0", qm_raw[0], "do_bf0")
+            elif c >= LATE_FROM:
+                if not late:
+                    late.extend([tile("late_bf", [P, 2 * PACK * D], BF16, tag=LATE_TAG), 0])
+                width = PACK * dom_raw[c].shape[2]
+                dom_bf = interleave("", dom_raw[c], 0, into=late[0][:, late[1] : late[1] + width])
+                qm_bf = interleave("", qm_raw[c], 0, into=late[0][:, late[1] + width : late[1] + 2 * width])
+                late[1] += 2 * width
             else:
                 dom_bf = interleave("dom_bf%d" % c, dom_raw[c], 0)
                 qm_bf = interleave("qm_bf%d" % c, qm_raw[c], 0)
@@ -219,11 +234,22 @@ def tile_attend_gat_sig_c_kernel(tc, qT, c_words, c_scales, doT, rw, qm, dom, of
             nc.vector.scalar_tensor_tensor(
                 ds_rows[:, t, :], dp_banks[t][:], neg_gate[:, t : t + 1], neg_slope[:, t, :], MULT, MULT
             )
-        pw_bf = interleave("pw_bf", pw_rows[:], PW_SHARE)
+        pw_bf = tile("pw_bf", [P, PACK * N], BF16)[:]
+        cut = N - PW_ON_GPSIMD
+        if cut:
+            interleave("", pw_rows[:, :, 0:cut], PW_SHARE, into=pw_bf[:, 0 : PACK * cut])
+        if cut < N:
+            nc.gpsimd.tensor_scalar(
+                pw_bf[:, PACK * cut :].rearrange("p (n t) -> p n t", t=PACK),
+                pw_rows[:, :, cut:].rearrange("p t n -> p n t"), 1.0, 0.0, MULT, ADD,
+            )
         if FIRST_EARLY:
             query_operands(0)
+        if PW_QUANT_EARLY:
+            pw_codes, pw_scales = quantize("pw", pw_bf, E4M3)
         ds_bf = interleave("ds_bf", ds_rows[:], DS_SHARE)
-        pw_codes, pw_scales = quantize("pw", pw_bf, E4M3)
+        if not PW_QUANT_EARLY:
+            pw_codes, pw_scales = quantize("pw", pw_bf, E4M3)
         ds_codes, ds_scales = quantize("ds", ds_bf, E5M2)
 
         first = 0
@@ -245,8 +271,11 @@ def tile_attend_gat_sig_c_kernel(tc, qT, c_words, c_scales, doT, rw, qm, dom, of
                 )
                 grad = tile("grad_sb%d" % b, [P, N], F32)
                 copy = nc.vector.tensor_copy if b < COPIES_ON_VECTOR else nc.scalar.copy
-                copy(grad[:], acc[:])
                 window = windows[b % len(windows)]
-                nc.vector.tensor_copy(window[:].indirect(offsets[:]), grad[:])
+                parts = FIRST_PARTS if b == 0 else 1
+                for h in range(parts):
+                    slots = slice(h * N // parts, (h + 1) * N // parts)
+                    (copy if h == 0 else nc.scalar.copy)(grad[:, slots], acc[:, slots])
+                    nc.vector.tensor_copy(window[:].indirect(offsets[:, slots.start // 16 : slots.stop // 16]), grad[:, slots])
                 nc.sync.dma_start(out=out[b * P : (b + 1) * P, :], in_=window[:])
             first = blocks.stop

@@ -26,21 +26,26 @@ K_PASS = P * PACK
 PASSES = D // K_PASS
 LOAD_WIDTHS = (256, 256, 512)
 STEP_WIDTHS = ((128, 128), (256,), (256, 256))
-Q_SHARES = ((0, 64), (64, 44))
+Q_SHARES = ((0, 44), (32, 44))
 DO_SHARES = ((64, 64), (0, 40))
-DS_SHARE = 112
+DS_SHARE = 80
 PW_SHARE = 0
 PW_ROWS_ON_VECTOR = 2
-STAGES = 6
+STAGES = 5
 WINDOWS = 3
-FIRST_PARTS = 2
+FIRST_PARTS = 1
+PW_ROWS_ON_GPSIMD = 0
+GATE_TAG = "do1_hold"
+DS_FIRST = False
+SLOPE_TAG = "neg_slope"
+PW_TAG = "pw_rows"
 PW_ON_GPSIMD = 0
 LATE_TAG = "neg_slope"
-LATE_FROM = 1
+LATE_FROM = 2
 PW_QUANT_EARLY = True
 COPIES_ON_VECTOR = 1
 FIRST_EARLY = False
-FIRST_ON_GPSIMD = False
+FIRST_ON_GPSIMD = 1
 
 
 def tile_attend_gat_sig_c_kernel(tc, qT, c_words, c_scales, doT, rw, qm, dom, offs, out):
@@ -57,21 +62,24 @@ def tile_attend_gat_sig_c_kernel(tc, qT, c_words, c_scales, doT, rw, qm, dom, of
             return ps.tile([P, N], F32, name=name, tag="bank%d" % b)
 
         def load_rows(name, rows):
-            raw = stage.tile([P, PACK, rows.shape[1]], F32, name=name, tag="staged", align_bytes=64)
+            if name.startswith("do_raw"):
+                raw = tile(name, [P, PACK, rows.shape[1]], F32)
+            else:
+                raw = stage.tile([P, PACK, rows.shape[1]], F32, name=name, tag="staged", align_bytes=64)
             nc.sync.dma_start(out=raw[:], in_=rows.rearrange("(p j) w -> p j w", j=PACK))
             return raw
 
-        pool_words = tile("pool_words", [P, T], I32)
-        nc.sync.dma_start(out=pool_words[:], in_=c_words[0].rearrange("p t b -> p (t b)").bitcast(I32))
         offsets = sb.tile([P, N // 16], U16, name="offsets")
         nc.sync.dma_start(offsets[:], offs)
+        pool_words = tile("pool_words", [P, T], I32)
+        nc.sync.dma_start(out=pool_words[:], in_=c_words[0].rearrange("p t b -> p (t b)").bitcast(I32))
 
         pool_scales = tile("pool_scales", [P, T // 4], I32)
         nc.gpsimd.memset(pool_scales[:], 0)
         scale_rows = c_scales.bitcast(I32)
-        for quad in range(4):
+        for r in range(4):
             nc.sync.dma_start(
-                out=pool_scales[32 * quad : 32 * quad + 8, :], in_=scale_rows[:, 4 * quad : 4 * quad + 4, :]
+                out=pool_scales[r:P:16, :], in_=scale_rows[:, r:16:4, :].rearrange("o q t -> q o t")
             )
         gate = tile("gate", [P, PACK], F32)
         nc.scalar.dma_start(out=gate[:], in_=rw[0].rearrange("(p t) o -> p (t o)", t=PACK))
@@ -114,7 +122,7 @@ def tile_attend_gat_sig_c_kernel(tc, qT, c_words, c_scales, doT, rw, qm, dom, of
             word_pairs[:].bitcast(U16).rearrange("p (n o) -> p o n", o=PASSES),
         )
         nc.gpsimd.memset(c_sc[1][:].bitcast(I32), 0)
-        nc.sync.dma_start(out=c_sc[1][0 : P - 4, :].bitcast(I32), in_=c_sc[0][4:P, :].bitcast(I32))
+        nc.sync.dma_start(out=c_sc[1][0 : P - 16, :].bitcast(I32), in_=c_sc[0][16:P, :].bitcast(I32))
         do_raw = load_pieces("do_raw", doT, DO_SHARES)
         qm_raw, dom_raw = [], []
         d0 = 0
@@ -168,8 +176,7 @@ def tile_attend_gat_sig_c_kernel(tc, qT, c_words, c_scales, doT, rw, qm, dom, of
                 shared_copy(dst, src, share)
             return grouped
 
-        def interleave_on_gpsimd(name, rows, tag):
-            grouped = tile(name, [P, PACK * rows.shape[2]], BF16, tag=tag)[:]
+        def interleave_on_gpsimd(grouped, rows):
             nc.gpsimd.tensor_scalar(
                 grouped.rearrange("p (n t) -> p n t", t=PACK), rows.rearrange("p t n -> p n t"), 1.0, 0.0, MULT, ADD
             )
@@ -201,19 +208,24 @@ def tile_attend_gat_sig_c_kernel(tc, qT, c_words, c_scales, doT, rw, qm, dom, of
             do_mx = quantize("do%d" % o, group_queries("do_bf%d" % o, do_raw[o], shares), E5M2, 1 + 3 * o)
             score_pass(dp_banks, do_mx, E5M2, o)
 
-        neg_slope = tile("neg_slope", [P, PACK, N], F32)
+        neg_slope = tile("neg_slope", [P, PACK, N], F32, tag=SLOPE_TAG)
         ds_rows = tile("ds_rows", [P, PACK, N], BF16)
-        pw_rows = tile("pw_rows", [P, PACK, N], BF16)
+        pw_rows = tile("pw_rows", [P, PACK, N], BF16, tag=PW_TAG)
         operands = {}
         late = []
+        late_gate = []
+        early = []
 
         def query_operands(c):
-            if c == 0 and FIRST_ON_GPSIMD:
-                dom_bf = interleave_on_gpsimd("dom_bf0", dom_raw[0], "do_bf1")
-                qm_bf = interleave_on_gpsimd("qm_bf0", qm_raw[0], "do_bf0")
+            if c < FIRST_ON_GPSIMD:
+                if not early:
+                    early.append(tile("early_bf", [P, 4 * PACK * P], BF16, tag="do_bf1"))
+                w = PACK * P
+                dom_bf = interleave_on_gpsimd(early[0][:, 2 * c * w : (2 * c + 1) * w], dom_raw[c])
+                qm_bf = interleave_on_gpsimd(early[0][:, (2 * c + 1) * w : (2 * c + 2) * w], qm_raw[c])
             elif c >= LATE_FROM:
                 if not late:
-                    late.extend([tile("late_bf", [P, 2 * PACK * D], BF16, tag=LATE_TAG), 0])
+                    late.extend([tile("late_bf", [P, 2 * PACK * D], BF16, tag={"neg_slope": SLOPE_TAG, "pw_rows": PW_TAG}.get(LATE_TAG, LATE_TAG)), 0])
                 width = PACK * dom_raw[c].shape[2]
                 dom_bf = interleave("", dom_raw[c], 0, into=late[0][:, late[1] : late[1] + width])
                 qm_bf = interleave("", qm_raw[c], 0, into=late[0][:, late[1] + width : late[1] + 2 * width])
@@ -224,7 +236,12 @@ def tile_attend_gat_sig_c_kernel(tc, qT, c_words, c_scales, doT, rw, qm, dom, of
             operands[c] = (quantize("dom%d" % c, dom_bf, E5M2), quantize("qm%d" % c, qm_bf, E4M3))
 
         for t in range(PACK):
-            if t < PW_ROWS_ON_VECTOR:
+            if t >= PACK - PW_ROWS_ON_GPSIMD:
+                if not late_gate:
+                    late_gate.append(tile("late_gate", [P, PACK], F32, tag=("do_bf1" if FIRST_ON_GPSIMD == 0 else "late_gate")))
+                    nc.gpsimd.tensor_copy(late_gate[0][:], gate[:])
+                nc.gpsimd.tensor_scalar(pw_rows[:, t, :], prob[:, t, :], late_gate[0][:, t : t + 1], 0.0, MULT, ADD)
+            elif t < PW_ROWS_ON_VECTOR:
                 nc.vector.tensor_scalar(pw_rows[:, t, :], prob[:, t, :], gate[:, t : t + 1], None, MULT)
             else:
                 nc.scalar.activation(out=pw_rows[:, t, :], in_=prob[:, t, :], func=COPY, scale=gate[:, t : t + 1])
@@ -234,23 +251,20 @@ def tile_attend_gat_sig_c_kernel(tc, qT, c_words, c_scales, doT, rw, qm, dom, of
             nc.vector.scalar_tensor_tensor(
                 ds_rows[:, t, :], dp_banks[t][:], neg_gate[:, t : t + 1], neg_slope[:, t, :], MULT, MULT
             )
-        pw_bf = tile("pw_bf", [P, PACK * N], BF16)[:]
-        cut = N - PW_ON_GPSIMD
-        if cut:
-            interleave("", pw_rows[:, :, 0:cut], PW_SHARE, into=pw_bf[:, 0 : PACK * cut])
-        if cut < N:
-            nc.gpsimd.tensor_scalar(
-                pw_bf[:, PACK * cut :].rearrange("p (n t) -> p n t", t=PACK),
-                pw_rows[:, :, cut:].rearrange("p t n -> p n t"), 1.0, 0.0, MULT, ADD,
-            )
+        def weights():
+            return quantize("pw", interleave("pw_bf", pw_rows[:], PW_SHARE), E4M3)
+
+        def slopes():
+            return quantize("ds", interleave("ds_bf", ds_rows[:], DS_SHARE), E5M2)
+
         if FIRST_EARLY:
             query_operands(0)
-        if PW_QUANT_EARLY:
-            pw_codes, pw_scales = quantize("pw", pw_bf, E4M3)
-        ds_bf = interleave("ds_bf", ds_rows[:], DS_SHARE)
-        if not PW_QUANT_EARLY:
-            pw_codes, pw_scales = quantize("pw", pw_bf, E4M3)
-        ds_codes, ds_scales = quantize("ds", ds_bf, E5M2)
+        if DS_FIRST:
+            ds_codes, ds_scales = slopes()
+            pw_codes, pw_scales = weights()
+        else:
+            pw_codes, pw_scales = weights()
+            ds_codes, ds_scales = slopes()
 
         first = 0
         for c in range(len(dom_raw)):
@@ -261,14 +275,17 @@ def tile_attend_gat_sig_c_kernel(tc, qT, c_words, c_scales, doT, rw, qm, dom, of
             for b in blocks:
                 cols = slice((b - first) * P, (b - first + 1) * P)
                 acc = bank(b, "grad%d" % b)
-                nc.tensor.matmul_mx(
-                    out=acc[:], lhsT=dom_codes[:, cols].bitcast(E5M2), lhsT_scale=dom_scales[:, cols],
-                    rhs=pw_codes[:].bitcast(E4M3), rhs_scale=pw_scales[:], start=True, stop=False,
-                )
-                nc.tensor.matmul_mx(
-                    out=acc[:], lhsT=qm_codes[:, cols].bitcast(E4M3), lhsT_scale=qm_scales[:, cols],
-                    rhs=ds_codes[:].bitcast(E5M2), rhs_scale=ds_scales[:], start=False, stop=True,
-                )
+                products = [
+                    (dom_codes[:, cols].bitcast(E5M2), dom_scales[:, cols], pw_codes[:].bitcast(E4M3), pw_scales[:]),
+                    (qm_codes[:, cols].bitcast(E4M3), qm_scales[:, cols], ds_codes[:].bitcast(E5M2), ds_scales[:]),
+                ]
+                if DS_FIRST:
+                    products.reverse()
+                for k, (lhs, lhs_scale, rhs, rhs_scale) in enumerate(products):
+                    nc.tensor.matmul_mx(
+                        out=acc[:], lhsT=lhs, lhsT_scale=lhs_scale, rhs=rhs, rhs_scale=rhs_scale,
+                        start=(k == 0), stop=(k == 1),
+                    )
                 grad = tile("grad_sb%d" % b, [P, N], F32)
                 copy = nc.vector.tensor_copy if b < COPIES_ON_VECTOR else nc.scalar.copy
                 window = windows[b % len(windows)]

@@ -24,24 +24,24 @@ P = 128
 PACK = 4
 K_PASS = P * PACK
 PASSES = D // K_PASS
-LOAD_WIDTHS = (256, 256, 512)
-STEP_WIDTHS = ((128, 128), (256,), (256, 256))
-Q_SHARES = ((0, 44), (32, 44))
-DO_SHARES = ((64, 64), (0, 40))
-DS_SHARE = 80
-PW_SHARE = 0
-PW_ROWS_ON_VECTOR = 2
+LOAD_WIDTHS = (512, 512)
+STEP_WIDTHS = ((128, 128, 128, 128), (256, 256))
+Q_SHARES = ((0, 44), (32, 52))
+DO_SHARES = ((64, 64), (0, 56))
+DS_SHARE = 96
+PW_SHARE = 16
+PW_ROWS_ON_VECTOR = 0
 STAGES = 5
 WINDOWS = 3
-FIRST_PARTS = 1
+FIRST_PARTS = 2
 PW_ROWS_ON_GPSIMD = 0
 GATE_TAG = "do1_hold"
 DS_FIRST = False
-SLOPE_TAG = "neg_slope"
-PW_TAG = "pw_rows"
+SLOPE_TAG = "do_raw0_1"
+PW_TAG = "do_raw1_0"
 PW_ON_GPSIMD = 0
-LATE_TAG = "neg_slope"
-LATE_FROM = 2
+LATE_TAG = "ds_bf"
+LATE_FROM = 3
 PW_QUANT_EARLY = True
 COPIES_ON_VECTOR = 1
 FIRST_EARLY = False
@@ -69,6 +69,12 @@ def tile_attend_gat_sig_c_kernel(tc, qT, c_words, c_scales, doT, rw, qm, dom, of
             nc.sync.dma_start(out=raw[:], in_=rows.rearrange("(p j) w -> p j w", j=PACK))
             return raw
 
+        def load_queries(name, rows):
+            raw = stage.tile([P, PACK, rows.shape[1]], F32, name=name, tag="staged", align_bytes=64)
+            for t in range(PACK):
+                nc.sync.dma_start(out=raw[:, t, :], in_=rows.rearrange("(g t b) w -> t g b w", t=PACK, b=2)[t])
+            return raw
+
         offsets = sb.tile([P, N // 16], U16, name="offsets")
         nc.sync.dma_start(offsets[:], offs)
         pool_words = tile("pool_words", [P, T], I32)
@@ -81,8 +87,11 @@ def tile_attend_gat_sig_c_kernel(tc, qT, c_words, c_scales, doT, rw, qm, dom, of
             nc.sync.dma_start(
                 out=pool_scales[r:P:16, :], in_=scale_rows[:, r:16:4, :].rearrange("o q t -> q o t")
             )
-        gate = tile("gate", [P, PACK], F32)
-        nc.scalar.dma_start(out=gate[:], in_=rw[0].rearrange("(p t) o -> p (t o)", t=PACK))
+        gate = tile("gate", [P, 2 * PACK - 1], F32)
+        for b in range(2):
+            nc.scalar.dma_start(
+                out=gate[b:P:2, :], in_=rw[0].rearrange("(g x) o -> g (x o)", x=2 * PACK)[:, b : b + 2 * PACK - 1]
+            )
         warm_in = tile("warm_in", [P, 1], F32)
         warm_out = tile("warm_out", [P, 1], F32)
         nc.gpsimd.memset(warm_in[:], 0.0)
@@ -109,7 +118,7 @@ def tile_attend_gat_sig_c_kernel(tc, qT, c_words, c_scales, doT, rw, qm, dom, of
         nc.vector.memset(windows[2][:, T // 2 - 1 : T // 2], 0.0)
         nc.gpsimd.memset(windows[2][:, T // 2 : T], 0.0)
 
-        neg_gate = tile("neg_gate", [P, PACK], F32)
+        neg_gate = tile("neg_gate", [P, 2 * PACK - 1], F32)
         nc.gpsimd.tensor_scalar(neg_gate[:], gate[:], -1.0, 0.0, MULT, ADD)
 
         word_pairs = tile("word_pairs", [P, N], U32)
@@ -127,8 +136,8 @@ def tile_attend_gat_sig_c_kernel(tc, qT, c_words, c_scales, doT, rw, qm, dom, of
         qm_raw, dom_raw = [], []
         d0 = 0
         for c, width in enumerate(LOAD_WIDTHS):
-            dom_c = load_rows("dom_raw%d" % c, dom[0, :, d0 : d0 + width])
-            qm_c = load_rows("qm_raw%d" % c, qm[0, :, d0 : d0 + width])
+            dom_c = load_queries("dom_raw%d" % c, dom[0, :, d0 : d0 + width])
+            qm_c = load_queries("qm_raw%d" % c, qm[0, :, d0 : d0 + width])
             s0 = 0
             for step in STEP_WIDTHS[c]:
                 dom_raw.append(dom_c[:, :, s0 : s0 + step])
@@ -157,12 +166,12 @@ def tile_attend_gat_sig_c_kernel(tc, qT, c_words, c_scales, doT, rw, qm, dom, of
 
         def group_queries(name, halves, shares):
             grouped = tile(name, [P, PACK * R], BF16)
-            dst = grouped[:].rearrange("p (t m j) -> p m t j", t=PACK, j=PACK)
+            dst = grouped[:].rearrange("p (t g b j) -> p g t j b", t=PACK, b=2, j=PACK)
             for h, raw in enumerate(halves):
                 shared_copy(
-                    dst[:, h * P // len(halves) : (h + 1) * P // len(halves)],
-                    raw[:].rearrange("p j (m t) -> p m t j", t=PACK),
-                    shares[h],
+                    dst[:, h * P // 2 // len(halves) : (h + 1) * P // 2 // len(halves)],
+                    raw[:].rearrange("p j (g t b) -> p g t j b", t=PACK, b=2),
+                    shares[h] // 2,
                 )
             return grouped[:]
 
@@ -242,14 +251,14 @@ def tile_attend_gat_sig_c_kernel(tc, qT, c_words, c_scales, doT, rw, qm, dom, of
                     nc.gpsimd.tensor_copy(late_gate[0][:], gate[:])
                 nc.gpsimd.tensor_scalar(pw_rows[:, t, :], prob[:, t, :], late_gate[0][:, t : t + 1], 0.0, MULT, ADD)
             elif t < PW_ROWS_ON_VECTOR:
-                nc.vector.tensor_scalar(pw_rows[:, t, :], prob[:, t, :], gate[:, t : t + 1], None, MULT)
+                nc.vector.tensor_scalar(pw_rows[:, t, :], prob[:, t, :], gate[:, 2 * t : 2 * t + 1], None, MULT)
             else:
-                nc.scalar.activation(out=pw_rows[:, t, :], in_=prob[:, t, :], func=COPY, scale=gate[:, t : t + 1])
+                nc.scalar.activation(out=pw_rows[:, t, :], in_=prob[:, t, :], func=COPY, scale=gate[:, 2 * t : 2 * t + 1])
         for t in range(PACK):
             nc.vector.scalar_tensor_tensor(neg_slope[:, t, :], prob[:, t, :], 1.0, prob[:, t, :], SUB, MULT)
         for t in range(PACK):
             nc.vector.scalar_tensor_tensor(
-                ds_rows[:, t, :], dp_banks[t][:], neg_gate[:, t : t + 1], neg_slope[:, t, :], MULT, MULT
+                ds_rows[:, t, :], dp_banks[t][:], neg_gate[:, 2 * t : 2 * t + 1], neg_slope[:, t, :], MULT, MULT
             )
         def weights():
             return quantize("pw", interleave("pw_bf", pw_rows[:], PW_SHARE), E4M3)

@@ -25,23 +25,23 @@ PACK = 4
 K_PASS = P * PACK
 PASSES = D // K_PASS
 LOAD_WIDTHS = (512, 512)
-STEP_WIDTHS = ((128, 128, 128, 128), (256, 256))
-Q_SHARES = ((0, 44), (32, 52))
-DO_SHARES = ((64, 64), (0, 56))
-DS_SHARE = 96
-PW_SHARE = 16
-PW_ROWS_ON_VECTOR = 0
+STEP_WIDTHS = ((128, 128, 256), (256, 256))
+Q_SHARES = ((0, 44), (32, 44))
+DO_SHARES = ((64, 64), (0, 40))
+DS_SHARE = 80
+PW_SHARE = 0
+PW_ROWS_ON_VECTOR = 2
 STAGES = 5
 WINDOWS = 3
-FIRST_PARTS = 2
+FIRST_PARTS = 1
 PW_ROWS_ON_GPSIMD = 0
 GATE_TAG = "do1_hold"
 DS_FIRST = False
-SLOPE_TAG = "do_raw0_1"
-PW_TAG = "do_raw1_0"
+SLOPE_TAG = "neg_slope"
+PW_TAG = "pw_rows"
 PW_ON_GPSIMD = 0
-LATE_TAG = "ds_bf"
-LATE_FROM = 3
+LATE_TAG = "neg_slope"
+LATE_FROM = 2
 PW_QUANT_EARLY = True
 COPIES_ON_VECTOR = 1
 FIRST_EARLY = False

@@ -26,8 +26,8 @@ K_PASS = P * PACK
 PASSES = D // K_PASS
 LOAD_WIDTHS = (512, 512)
 STEP_WIDTHS = ((128, 128, 256), (256, 256))
-Q_SHARES = ((0, 44), (32, 44))
-DO_SHARES = ((64, 64), (0, 40))
+Q_SHARES = ((0, 44), (0, 44))
+DO_SHARES = ((64, 64), (0, 44))
 DS_SHARE = 80
 PW_SHARE = 0
 PW_ROWS_ON_VECTOR = 2
@@ -218,8 +218,8 @@ def tile_attend_gat_sig_c_kernel(tc, qT, c_words, c_scales, doT, rw, qm, dom, of
             score_pass(dp_banks, do_mx, E5M2, o)
 
         neg_slope = tile("neg_slope", [P, PACK, N], F32, tag=SLOPE_TAG)
-        ds_rows = tile("ds_rows", [P, PACK, N], BF16)
-        pw_rows = tile("pw_rows", [P, PACK, N], BF16, tag=PW_TAG)
+        ds_rows = tile("ds_rows", [P, PACK, N], F32)
+        pw_rows = tile("pw_rows", [P, PACK, N], F32, tag=PW_TAG)
         operands = {}
         late = []
         late_gate = []

@@ -33,7 +33,7 @@ PW_SHARE = 0
 PW_ROWS_ON_VECTOR = 2
 STAGES = 5
 WINDOWS = 3
-FIRST_PARTS = 1
+FIRST_PARTS = 2
 PW_ROWS_ON_GPSIMD = 0
 GATE_TAG = "do1_hold"
 DS_FIRST = False
@@ -44,7 +44,7 @@ LATE_TAG = "neg_slope"
 LATE_FROM = 2
 PW_QUANT_EARLY = True
 COPIES_ON_VECTOR = 1
-FIRST_EARLY = False
+FIRST_EARLY = True
 FIRST_ON_GPSIMD = 1
 
 
@@ -208,13 +208,13 @@ def tile_attend_gat_sig_c_kernel(tc, qT, c_words, c_scales, doT, rw, qm, dom, of
         a_banks = [bank(t, "a%d" % t) for t in range(PACK)]
         dp_banks = [bank(PACK + t, "dp%d" % t) for t in range(PACK)]
         for o, shares in enumerate(Q_SHARES):
-            q_mx = quantize("q%d" % o, group_queries("q_bf%d" % o, q_raw[o], shares), E4M3, 1 + 3 * o)
+            q_mx = quantize("q%d" % o, group_queries("q_bf%d" % o, q_raw[o], shares), E4M3, PACK)
             score_pass(a_banks, q_mx, E4M3, o)
         prob = tile("prob", [P, PACK, N], F32)
         for t in range(PACK):
             nc.scalar.activation(out=prob[:, t, :], in_=a_banks[t][:], func=SIGMOID)
         for o, shares in enumerate(DO_SHARES):
-            do_mx = quantize("do%d" % o, group_queries("do_bf%d" % o, do_raw[o], shares), E5M2, 1 + 3 * o)
+            do_mx = quantize("do%d" % o, group_queries("do_bf%d" % o, do_raw[o], shares), E5M2, PACK)
             score_pass(dp_banks, do_mx, E5M2, o)
 
         neg_slope = tile("neg_slope", [P, PACK, N], F32, tag=SLOPE_TAG)

@@ -111,6 +111,8 @@ def tile_attend_gat_sig_c_kernel(tc, qT, c_words, c_scales, doT, rw, qm, dom, of
 
         q_raw = load_pieces("q_raw", qT, Q_SHARES)
         windows = [tile("window%d" % w, [P, T], F32) for w in range(WINDOWS)]
+        c_sc = [tile("c_sc%d" % o, [P, N], U8) for o in range(PASSES)]
+        nc.gpsimd.memset(c_sc[1][:].bitcast(I32), 0)
         nc.gpsimd.memset(windows[0][:], 0.0)
         nc.vector.memset(windows[1][:, 0 : T // 2 - 1], 0.0)
         nc.vector.memset(windows[1][:, T // 2 - 1 : T], 0.0)
@@ -123,14 +125,12 @@ def tile_attend_gat_sig_c_kernel(tc, qT, c_words, c_scales, doT, rw, qm, dom, of
 
         word_pairs = tile("word_pairs", [P, N], U32)
         nc.vector.tensor_copy(word_pairs[:], pool_words[:].bitcast(U32).indirect(offsets[:]))
-        c_sc = [tile("c_sc%d" % o, [P, N], U8) for o in range(PASSES)]
         nc.vector.tensor_copy(c_sc[0][:], pool_scales[:].bitcast(U8).indirect(offsets[:]))
         c_codes = tile("c_codes", [P, PASSES * 2 * N], U8, tag="pool_scales")
         nc.vector.tensor_copy(
             c_codes[:].bitcast(U16).rearrange("p (o n) -> p o n", o=PASSES),
             word_pairs[:].bitcast(U16).rearrange("p (n o) -> p o n", o=PASSES),
         )
-        nc.gpsimd.memset(c_sc[1][:].bitcast(I32), 0)
         nc.sync.dma_start(out=c_sc[1][0 : P - 16, :].bitcast(I32), in_=c_sc[0][16:P, :].bitcast(I32))
         do_raw = load_pieces("do_raw", doT, DO_SHARES)
         qm_raw, dom_raw = [], []
@@ -261,7 +261,7 @@ def tile_attend_gat_sig_c_kernel(tc, qT, c_words, c_scales, doT, rw, qm, dom, of
                 ds_rows[:, t, :], dp_banks[t][:], neg_gate[:, 2 * t : 2 * t + 1], neg_slope[:, t, :], MULT, MULT
             )
         def weights():
-            return quantize("pw", interleave("pw_bf", pw_rows[:], PW_SHARE), E4M3)
+            return quantize("pw", interleave("pw_bf", pw_rows[:], PW_SHARE, "do_raw1_1"), E4M3)
 
         def slopes():
             return quantize("ds", interleave("ds_bf", ds_rows[:], DS_SHARE), E5M2)

@@ -131,8 +131,13 @@ def tile_attend_gat_sig_c_kernel(tc, qT, c_words, c_scales, doT, rw, qm, dom, of
             c_codes[:].bitcast(U16).rearrange("p (o n) -> p o n", o=PASSES),
             word_pairs[:].bitcast(U16).rearrange("p (n o) -> p o n", o=PASSES),
         )
+        halves = [slice(h * R // 2, (h + 1) * R // 2) for h in range(2)]
+        do_first = load_rows("do_raw0_0", doT[0, 0:K_PASS, halves[0]])
         nc.sync.dma_start(out=c_sc[1][0 : P - 16, :].bitcast(I32), in_=c_sc[0][16:P, :].bitcast(I32))
-        do_raw = load_pieces("do_raw", doT, DO_SHARES)
+        do_raw = [
+            [do_first, load_rows("do_raw0_1", doT[0, 0:K_PASS, halves[1]])],
+            [load_rows("do_raw1_%d" % h, doT[0, K_PASS:D, halves[h]]) for h in range(2)],
+        ]
         qm_raw, dom_raw = [], []
         d0 = 0
         for c, width in enumerate(LOAD_WIDTHS):

@@ -24,56 +24,39 @@ P = 128
 PACK = 4
 K_PASS = P * PACK
 PASSES = D // K_PASS
-LOAD_WIDTHS = (512, 512)
-STEP_WIDTHS = ((128, 128, 256), (256, 256))
-Q_SHARES = ((0, 44), (0, 44))
-DO_SHARES = ((64, 64), (0, 44))
-DS_SHARE = 80
-PW_SHARE = 0
-PW_ROWS_ON_VECTOR = 2
-STAGES = 5
+GROUPS = P // 2
+Q_PIECES = (((32, 0), (32, 32)), ((48, 16), (16, 16)))
+DO_PIECES = (((32, 32), (32, 32)), ((32, 0), (32, 22)))
+STEP_WIDTHS = ((128, 128), (256,), (512,))
 WINDOWS = 3
+EARLY = 320
+SLOPE_ROWS = 2
+PW_ROWS_ON_VECTOR = (1, 3)
+PW_FIRST = False
+PW_SHARE = 32
+PW_PARTS = 1
+DS_SHARE = 0
+ON_GPSIMD = ()
+SHARED = {'dom_bf1': ('second', 0, 1024), 'qm_bf1': ('second', 512, 1024)}
+AHEAD_OF_PW = 0
+DS_QUANT_PARTS = 1
+LOOK = 1
 FIRST_PARTS = 2
-PW_ROWS_ON_GPSIMD = 0
-GATE_TAG = "do1_hold"
-DS_FIRST = False
-SLOPE_TAG = "neg_slope"
-PW_TAG = "pw_rows"
-PW_ON_GPSIMD = 0
-LATE_TAG = "neg_slope"
-LATE_FROM = 2
-PW_QUANT_EARLY = True
-COPIES_ON_VECTOR = 1
-FIRST_EARLY = True
-FIRST_ON_GPSIMD = 1
+FIRST_ON_VECTOR = True
+TAGS = {'word_pairs': 'pool_scales', 'grad_sb1': 'qm_raw1', 'grad_sb3': 'qm_raw2', 'first': 'do_bf1', 'second': 'neg_slope'}
 
 
 def tile_attend_gat_sig_c_kernel(tc, qT, c_words, c_scales, doT, rw, qm, dom, offs, out):
     nc = tc.nc
     with ExitStack() as ctx:
         sb = ctx.enter_context(tc.tile_pool(name="sb", bufs=1))
-        stage = ctx.enter_context(tc.tile_pool(name="stage", bufs=STAGES))
         ps = ctx.enter_context(tc.psum_pool(name="ps", bufs=1))
 
-        def tile(name, shape, dtype, tag=None):
-            return sb.tile(shape, dtype, name=name, tag=tag or name, align_bytes=64)
+        def tile(name, shape, dtype):
+            return sb.tile(shape, dtype, name=name, tag=TAGS.get(name, name), align_bytes=64)
 
         def bank(b, name):
             return ps.tile([P, N], F32, name=name, tag="bank%d" % b)
-
-        def load_rows(name, rows):
-            if name.startswith("do_raw"):
-                raw = tile(name, [P, PACK, rows.shape[1]], F32)
-            else:
-                raw = stage.tile([P, PACK, rows.shape[1]], F32, name=name, tag="staged", align_bytes=64)
-            nc.sync.dma_start(out=raw[:], in_=rows.rearrange("(p j) w -> p j w", j=PACK))
-            return raw
-
-        def load_queries(name, rows):
-            raw = stage.tile([P, PACK, rows.shape[1]], F32, name=name, tag="staged", align_bytes=64)
-            for t in range(PACK):
-                nc.sync.dma_start(out=raw[:, t, :], in_=rows.rearrange("(g t b) w -> t g b w", t=PACK, b=2)[t])
-            return raw
 
         offsets = sb.tile([P, N // 16], U16, name="offsets")
         nc.sync.dma_start(offsets[:], offs)
@@ -81,74 +64,75 @@ def tile_attend_gat_sig_c_kernel(tc, qT, c_words, c_scales, doT, rw, qm, dom, of
         nc.sync.dma_start(out=pool_words[:], in_=c_words[0].rearrange("p t b -> p (t b)").bitcast(I32))
 
         pool_scales = tile("pool_scales", [P, T // 4], I32)
-        nc.gpsimd.memset(pool_scales[:], 0)
+        nc.vector.memset(pool_scales[:], 0)
         scale_rows = c_scales.bitcast(I32)
         for r in range(4):
-            nc.sync.dma_start(
-                out=pool_scales[r:P:16, :], in_=scale_rows[:, r:16:4, :].rearrange("o q t -> q o t")
-            )
-        gate = tile("gate", [P, 2 * PACK - 1], F32)
-        for b in range(2):
             nc.scalar.dma_start(
-                out=gate[b:P:2, :], in_=rw[0].rearrange("(g x) o -> g (x o)", x=2 * PACK)[:, b : b + 2 * PACK - 1]
+                out=pool_scales[r:P:16, :], in_=scale_rows[:, r:16:4, :].rearrange("o q t -> q o t")
             )
         warm_in = tile("warm_in", [P, 1], F32)
         warm_out = tile("warm_out", [P, 1], F32)
-        nc.gpsimd.memset(warm_in[:], 0.0)
+        nc.vector.memset(warm_in[:], 0.0)
         nc.scalar.activation(out=warm_out[:], in_=warm_in[:], func=SIGMOID)
 
-        def load_pieces(name, src, shares):
-            return [
-                [
-                    load_rows(
-                        "%s%d_%d" % (name, o, h),
-                        src[0, o * K_PASS : (o + 1) * K_PASS, h * R // len(parts) : (h + 1) * R // len(parts)],
-                    )
-                    for h in range(len(parts))
-                ]
-                for o, parts in enumerate(shares)
-            ]
+        def load_pieces(name, src, pieces):
+            loaded = []
+            for o in range(PASSES):
+                g0 = 0
+                loaded.append([])
+                for h, (groups, share) in enumerate(pieces[o]):
+                    raw = tile("%s%d_%d" % (name, o, h), [P, PACK, 8 * groups], F32)
+                    rows = src[0, o * K_PASS : (o + 1) * K_PASS, 8 * g0 : 8 * (g0 + groups)]
+                    nc.sync.dma_start(out=raw[:], in_=rows.rearrange("(p j) w -> p j w", j=PACK))
+                    loaded[o].append((raw, g0, groups, share))
+                    g0 += groups
+            return loaded
 
-        q_raw = load_pieces("q_raw", qT, Q_SHARES)
-        windows = [tile("window%d" % w, [P, T], F32) for w in range(WINDOWS)]
-        c_sc = [tile("c_sc%d" % o, [P, N], U8) for o in range(PASSES)]
-        nc.gpsimd.memset(c_sc[1][:].bitcast(I32), 0)
-        nc.gpsimd.memset(windows[0][:], 0.0)
-        nc.vector.memset(windows[1][:, 0 : T // 2 - 1], 0.0)
-        nc.vector.memset(windows[1][:, T // 2 - 1 : T], 0.0)
-        nc.vector.memset(windows[2][:, 0 : T // 2 - 1], 0.0)
-        nc.vector.memset(windows[2][:, T // 2 - 1 : T // 2], 0.0)
-        nc.gpsimd.memset(windows[2][:, T // 2 : T], 0.0)
+        def load_queries(name, rows):
+            raw = tile(name, [P, PACK, rows.shape[1]], F32)
+            for t in range(PACK):
+                nc.sync.dma_start(out=raw[:, t, :], in_=rows.rearrange("(g t b) w -> t g b w", t=PACK, b=2)[t])
+            return raw
 
-        neg_gate = tile("neg_gate", [P, 2 * PACK - 1], F32)
-        nc.gpsimd.tensor_scalar(neg_gate[:], gate[:], -1.0, 0.0, MULT, ADD)
-
-        word_pairs = tile("word_pairs", [P, N], U32)
-        nc.vector.tensor_copy(word_pairs[:], pool_words[:].bitcast(U32).indirect(offsets[:]))
-        nc.vector.tensor_copy(c_sc[0][:], pool_scales[:].bitcast(U8).indirect(offsets[:]))
-        c_codes = tile("c_codes", [P, PASSES * 2 * N], U8, tag="pool_scales")
-        nc.vector.tensor_copy(
-            c_codes[:].bitcast(U16).rearrange("p (o n) -> p o n", o=PASSES),
-            word_pairs[:].bitcast(U16).rearrange("p (n o) -> p o n", o=PASSES),
-        )
-        halves = [slice(h * R // 2, (h + 1) * R // 2) for h in range(2)]
-        do_first = load_rows("do_raw0_0", doT[0, 0:K_PASS, halves[0]])
-        nc.sync.dma_start(out=c_sc[1][0 : P - 16, :].bitcast(I32), in_=c_sc[0][16:P, :].bitcast(I32))
-        do_raw = [
-            [do_first, load_rows("do_raw0_1", doT[0, 0:K_PASS, halves[1]])],
-            [load_rows("do_raw1_%d" % h, doT[0, K_PASS:D, halves[h]]) for h in range(2)],
-        ]
+        q_raw = load_pieces("q_raw", qT, Q_PIECES)
+        gate = tile("gate", [P, 2 * PACK - 1], F32)
+        for b in range(2):
+            nc.gpsimd.dma_start(
+                out=gate[b:P:2, :], in_=rw[0].rearrange("(g x) o -> g (x o)", x=2 * PACK)[:, b : b + 2 * PACK - 1]
+            )
+        do_raw = load_pieces("do_raw", doT, DO_PIECES)
         qm_raw, dom_raw = [], []
         d0 = 0
-        for c, width in enumerate(LOAD_WIDTHS):
+        for c, steps in enumerate(STEP_WIDTHS):
+            width = sum(steps)
             dom_c = load_queries("dom_raw%d" % c, dom[0, :, d0 : d0 + width])
             qm_c = load_queries("qm_raw%d" % c, qm[0, :, d0 : d0 + width])
             s0 = 0
-            for step in STEP_WIDTHS[c]:
+            for step in steps:
                 dom_raw.append(dom_c[:, :, s0 : s0 + step])
                 qm_raw.append(qm_c[:, :, s0 : s0 + step])
                 s0 += step
             d0 += width
+
+        windows = [tile("window%d" % w, [P, T], F32) for w in range(WINDOWS)]
+        c_sc = [tile("c_sc%d" % o, [P, N], U8) for o in range(PASSES)]
+        nc.gpsimd.memset(c_sc[1][:].bitcast(I32), 0)
+        nc.gpsimd.memset(windows[0][:], 0.0)
+        for w in range(1, WINDOWS):
+            nc.vector.memset(windows[w][:, 0 : T // 2 - 1], 0.0)
+            nc.vector.memset(windows[w][:, T // 2 - 1 : T], 0.0)
+
+        nc.vector.tensor_copy(c_sc[0][:], pool_scales[:].bitcast(U8).indirect(offsets[:]))
+        nc.scalar.dma_start(out=c_sc[1][0 : P - 16, :].bitcast(I32), in_=c_sc[0][16:P, :].bitcast(I32))
+        word_pairs = tile("word_pairs", [P, N], U32)
+        nc.vector.tensor_copy(word_pairs[:], pool_words[:].bitcast(U32).indirect(offsets[:]))
+        c_codes = tile("c_codes", [P, PASSES * 2 * N], U8)
+        nc.vector.tensor_copy(
+            c_codes[:].bitcast(U16).rearrange("p (o n) -> p o n", o=PASSES),
+            word_pairs[:].bitcast(U16).rearrange("p (n o) -> p o n", o=PASSES),
+        )
+        neg_gate = tile("neg_gate", [P, 2 * PACK - 1], F32)
+        nc.gpsimd.tensor_scalar(neg_gate[:], gate[:], -1.0, 0.0, MULT, ADD)
 
         def quantize(name, grouped, fmt, pieces=1):
             words = grouped.shape[1] // PACK
@@ -163,38 +147,22 @@ def tile_attend_gat_sig_c_kernel(tc, qT, c_words, c_scales, doT, rw, qm, dom, of
                 )
             return codes, scales
 
-        def shared_copy(dst, src, share):
-            if share > 0:
-                nc.vector.tensor_copy(dst[:, 0:share], src[:, 0:share])
-            if share < dst.shape[1]:
-                nc.scalar.copy(dst[:, share:], src[:, share:])
-
-        def group_queries(name, halves, shares):
+        def group_queries(name, pieces):
             grouped = tile(name, [P, PACK * R], BF16)
             dst = grouped[:].rearrange("p (t g b j) -> p g t j b", t=PACK, b=2, j=PACK)
-            for h, raw in enumerate(halves):
-                shared_copy(
-                    dst[:, h * P // 2 // len(halves) : (h + 1) * P // 2 // len(halves)],
-                    raw[:].rearrange("p j (g t b) -> p g t j b", t=PACK, b=2),
-                    shares[h] // 2,
-                )
+            for raw, g0, groups, share in pieces:
+                src = raw[:].rearrange("p j (g t b) -> p g t j b", t=PACK, b=2)
+                if share > 0:
+                    nc.vector.tensor_copy(dst[:, g0 : g0 + share], src[:, 0:share])
+                if share < groups:
+                    nc.scalar.copy(dst[:, g0 + share : g0 + groups], src[:, share:groups])
             return grouped[:]
 
-        def interleave(name, rows, share, tag=None, copy=None, into=None):
-            grouped = tile(name, [P, PACK * rows.shape[2]], BF16, tag=tag)[:] if into is None else into
-            dst = grouped.rearrange("p (c i t) -> p c t i", i=4, t=PACK)
-            src = rows.rearrange("p t (c i) -> p c t i", i=4)
-            if copy:
-                copy(dst, src)
-            else:
-                shared_copy(dst, src, share)
-            return grouped
+        def words_view(grouped):
+            return grouped.rearrange("p (c i t) -> p c t i", i=4, t=PACK)
 
-        def interleave_on_gpsimd(grouped, rows):
-            nc.gpsimd.tensor_scalar(
-                grouped.rearrange("p (n t) -> p n t", t=PACK), rows.rearrange("p t n -> p n t"), 1.0, 0.0, MULT, ADD
-            )
-            return grouped
+        def rows_view(rows):
+            return rows.rearrange("p t (c i) -> p c t i", i=4)
 
         def score_pass(banks, operand, fmt, o):
             codes, scales = operand
@@ -212,78 +180,94 @@ def tile_attend_gat_sig_c_kernel(tc, qT, c_words, c_scales, doT, rw, qm, dom, of
 
         a_banks = [bank(t, "a%d" % t) for t in range(PACK)]
         dp_banks = [bank(PACK + t, "dp%d" % t) for t in range(PACK)]
-        for o, shares in enumerate(Q_SHARES):
-            q_mx = quantize("q%d" % o, group_queries("q_bf%d" % o, q_raw[o], shares), E4M3, PACK)
+        for o in range(PASSES):
+            q_mx = quantize("q%d" % o, group_queries("q_bf%d" % o, q_raw[o]), E4M3, PACK)
             score_pass(a_banks, q_mx, E4M3, o)
         prob = tile("prob", [P, PACK, N], F32)
         for t in range(PACK):
             nc.scalar.activation(out=prob[:, t, :], in_=a_banks[t][:], func=SIGMOID)
-        for o, shares in enumerate(DO_SHARES):
-            do_mx = quantize("do%d" % o, group_queries("do_bf%d" % o, do_raw[o], shares), E5M2, PACK)
+        for o in range(PASSES):
+            do_mx = quantize("do%d" % o, group_queries("do_bf%d" % o, do_raw[o]), E5M2, PACK)
             score_pass(dp_banks, do_mx, E5M2, o)
 
-        neg_slope = tile("neg_slope", [P, PACK, N], F32, tag=SLOPE_TAG)
-        ds_rows = tile("ds_rows", [P, PACK, N], F32)
-        pw_rows = tile("pw_rows", [P, PACK, N], F32, tag=PW_TAG)
-        operands = {}
-        late = []
-        late_gate = []
-        early = []
+        def minus_gate(t):
+            return neg_gate[:, 2 * t : 2 * t + 1]
 
-        def query_operands(c):
-            if c < FIRST_ON_GPSIMD:
-                if not early:
-                    early.append(tile("early_bf", [P, 4 * PACK * P], BF16, tag="do_bf1"))
-                w = PACK * P
-                dom_bf = interleave_on_gpsimd(early[0][:, 2 * c * w : (2 * c + 1) * w], dom_raw[c])
-                qm_bf = interleave_on_gpsimd(early[0][:, (2 * c + 1) * w : (2 * c + 2) * w], qm_raw[c])
-            elif c >= LATE_FROM:
-                if not late:
-                    late.extend([tile("late_bf", [P, 2 * PACK * D], BF16, tag={"neg_slope": SLOPE_TAG, "pw_rows": PW_TAG}.get(LATE_TAG, LATE_TAG)), 0])
-                width = PACK * dom_raw[c].shape[2]
-                dom_bf = interleave("", dom_raw[c], 0, into=late[0][:, late[1] : late[1] + width])
-                qm_bf = interleave("", qm_raw[c], 0, into=late[0][:, late[1] + width : late[1] + 2 * width])
-                late[1] += 2 * width
-            else:
-                dom_bf = interleave("dom_bf%d" % c, dom_raw[c], 0)
-                qm_bf = interleave("qm_bf%d" % c, qm_raw[c], 0)
-            operands[c] = (quantize("dom%d" % c, dom_bf, E5M2), quantize("qm%d" % c, qm_bf, E4M3))
-
-        for t in range(PACK):
-            if t >= PACK - PW_ROWS_ON_GPSIMD:
-                if not late_gate:
-                    late_gate.append(tile("late_gate", [P, PACK], F32, tag=("do_bf1" if FIRST_ON_GPSIMD == 0 else "late_gate")))
-                    nc.gpsimd.tensor_copy(late_gate[0][:], gate[:])
-                nc.gpsimd.tensor_scalar(pw_rows[:, t, :], prob[:, t, :], late_gate[0][:, t : t + 1], 0.0, MULT, ADD)
-            elif t < PW_ROWS_ON_VECTOR:
-                nc.vector.tensor_scalar(pw_rows[:, t, :], prob[:, t, :], gate[:, 2 * t : 2 * t + 1], None, MULT)
-            else:
-                nc.scalar.activation(out=pw_rows[:, t, :], in_=prob[:, t, :], func=COPY, scale=gate[:, 2 * t : 2 * t + 1])
-        for t in range(PACK):
-            nc.vector.scalar_tensor_tensor(neg_slope[:, t, :], prob[:, t, :], 1.0, prob[:, t, :], SUB, MULT)
-        for t in range(PACK):
-            nc.vector.scalar_tensor_tensor(
-                ds_rows[:, t, :], dp_banks[t][:], neg_gate[:, 2 * t : 2 * t + 1], neg_slope[:, t, :], MULT, MULT
-            )
-        def weights():
-            return quantize("pw", interleave("pw_bf", pw_rows[:], PW_SHARE, "do_raw1_1"), E4M3)
+        early, late = slice(0, EARLY), slice(EARLY, N)
+        neg_slope = tile("neg_slope", [P, PACK, max(EARLY, 16)], F32)
 
         def slopes():
-            return quantize("ds", interleave("ds_bf", ds_rows[:], DS_SHARE), E5M2)
+            for t0 in range(0, PACK if EARLY else 0, SLOPE_ROWS):
+                rows = prob[:, t0 : t0 + SLOPE_ROWS, early]
+                nc.vector.scalar_tensor_tensor(neg_slope[:, t0 : t0 + SLOPE_ROWS, :], rows, 1.0, rows, SUB, MULT)
 
-        if FIRST_EARLY:
-            query_operands(0)
-        if DS_FIRST:
-            ds_codes, ds_scales = slopes()
-            pw_codes, pw_scales = weights()
-        else:
-            pw_codes, pw_scales = weights()
-            ds_codes, ds_scales = slopes()
+        if not PW_FIRST:
+            slopes()
+        neg_pw = tile("neg_pw", [P, PACK, N], F32)
+        for t in range(PACK):
+            if t in PW_ROWS_ON_VECTOR:
+                nc.vector.tensor_scalar(neg_pw[:, t, :], prob[:, t, :], minus_gate(t), None, MULT)
+            else:
+                nc.scalar.activation(out=neg_pw[:, t, :], in_=prob[:, t, :], func=COPY, scale=minus_gate(t))
+        if PW_FIRST:
+            slopes()
+        pw_bf = tile("pw_bf", [P, PACK * N], BF16)
+        if PW_SHARE:
+            nc.vector.tensor_scalar(words_view(pw_bf[:])[:, 0:PW_SHARE], rows_view(neg_pw[:])[:, 0:PW_SHARE], -1.0, None, MULT)
+        for k in range(PW_PARTS):
+            cs = slice(PW_SHARE + k * (N // 4 - PW_SHARE) // PW_PARTS, PW_SHARE + (k + 1) * (N // 4 - PW_SHARE) // PW_PARTS)
+            nc.scalar.activation(out=words_view(pw_bf[:])[:, cs], in_=rows_view(neg_pw[:])[:, cs], func=COPY, scale=-1.0)
+
+        part = tile("part", [P, PACK, N], F32)
+        for t in range(PACK):
+            if EARLY:
+                nc.vector.scalar_tensor_tensor(
+                    part[:, t, early], dp_banks[t][:, early], minus_gate(t), neg_slope[:, t, :], MULT, MULT
+                )
+            if EARLY < N:
+                nc.vector.scalar_tensor_tensor(part[:, t, late], prob[:, t, late], 1.0, dp_banks[t][:, late], SUB, MULT)
+        ds_bf = tile("ds_bf", [P, PACK * N], BF16)
+        e4 = EARLY // 4
+        if EARLY:
+            if DS_SHARE:
+                nc.vector.tensor_copy(words_view(ds_bf[:])[:, 0:DS_SHARE], rows_view(part[:])[:, 0:DS_SHARE])
+            nc.scalar.copy(words_view(ds_bf[:])[:, DS_SHARE:e4], rows_view(part[:])[:, DS_SHARE:e4])
+        if EARLY < N:
+            nc.vector.tensor_tensor(
+                words_view(ds_bf[:])[:, e4:], rows_view(part[:])[:, e4:], rows_view(neg_pw[:])[:, e4:], MULT
+            )
+
+        def query_operands(c):
+            made = []
+            for name, raw, fmt in (("dom", dom_raw[c], E5M2), ("qm", qm_raw[c], E4M3)):
+                key = "%s_bf%d" % (name, c)
+                width = PACK * raw.shape[2]
+                if key in SHARED:
+                    home, at, size = SHARED[key]
+                    if home not in homes:
+                        homes[home] = tile(home, [P, size], BF16)
+                    grouped = homes[home][:, at : at + width]
+                else:
+                    grouped = tile(key, [P, width], BF16)[:]
+                if key in ON_GPSIMD:
+                    nc.gpsimd.tensor_scalar(words_view(grouped), rows_view(raw), 1.0, 0.0, MULT, ADD)
+                else:
+                    nc.scalar.copy(words_view(grouped), rows_view(raw))
+                made.append((name, grouped, fmt))
+            return [quantize("%s%d" % (name, c), grouped, fmt) for name, grouped, fmt in made]
+
+        homes = {}
+        operands = {}
+        for c in range(AHEAD_OF_PW):
+            operands[c] = query_operands(c)
+        pw_codes, pw_scales = quantize("pw", pw_bf[:], E4M3)
+        ds_codes, ds_scales = quantize("ds", ds_bf[:], E5M2, DS_QUANT_PARTS)
 
         first = 0
         for c in range(len(dom_raw)):
-            if c not in operands:
-                query_operands(c)
+            for ahead in range(c, min(c + LOOK + 1, len(dom_raw))):
+                if ahead not in operands:
+                    operands[ahead] = query_operands(ahead)
             (dom_codes, dom_scales), (qm_codes, qm_scales) = operands[c]
             blocks = range(first, first + dom_raw[c].shape[2] // P)
             for b in blocks:
@@ -293,20 +277,18 @@ def tile_attend_gat_sig_c_kernel(tc, qT, c_words, c_scales, doT, rw, qm, dom, of
                     (dom_codes[:, cols].bitcast(E5M2), dom_scales[:, cols], pw_codes[:].bitcast(E4M3), pw_scales[:]),
                     (qm_codes[:, cols].bitcast(E4M3), qm_scales[:, cols], ds_codes[:].bitcast(E5M2), ds_scales[:]),
                 ]
-                if DS_FIRST:
-                    products.reverse()
                 for k, (lhs, lhs_scale, rhs, rhs_scale) in enumerate(products):
                     nc.tensor.matmul_mx(
                         out=acc[:], lhsT=lhs, lhsT_scale=lhs_scale, rhs=rhs, rhs_scale=rhs_scale,
                         start=(k == 0), stop=(k == 1),
                     )
                 grad = tile("grad_sb%d" % b, [P, N], F32)
-                copy = nc.vector.tensor_copy if b < COPIES_ON_VECTOR else nc.scalar.copy
                 window = windows[b % len(windows)]
                 parts = FIRST_PARTS if b == 0 else 1
                 for h in range(parts):
                     slots = slice(h * N // parts, (h + 1) * N // parts)
-                    (copy if h == 0 else nc.scalar.copy)(grad[:, slots], acc[:, slots])
+                    copy = nc.vector.tensor_copy if (b == 0 and h == 0 and FIRST_ON_VECTOR) else nc.scalar.copy
+                    copy(grad[:, slots], acc[:, slots])
                     nc.vector.tensor_copy(window[:].indirect(offsets[:, slots.start // 16 : slots.stop // 16]), grad[:, slots])
                 nc.sync.dma_start(out=out[b * P : (b + 1) * P, :], in_=window[:])
             first = blocks.stop

@@ -25,25 +25,27 @@ PACK = 4
 K_PASS = P * PACK
 PASSES = D // K_PASS
 GROUPS = P // 2
-Q_PIECES = (((32, 0), (32, 32)), ((48, 16), (16, 16)))
-DO_PIECES = (((32, 32), (32, 32)), ((32, 0), (32, 22)))
-STEP_WIDTHS = ((128, 128), (256,), (512,))
+Q_PIECES = (((64, 40),), ((32, 0), (32, 22)))
+DO_PIECES = (((32, 32), (32, 32)), ((32, 32), (32, 32)))
+STEP_WIDTHS = ((128, 128, 256), (256, 256))
 WINDOWS = 3
+HEAD = 'back'
+SHIFT_BEFORE = 'do_raw0_1'
 EARLY = 320
-SLOPE_ROWS = 2
-PW_ROWS_ON_VECTOR = (1, 3)
-PW_FIRST = False
-PW_SHARE = 32
+SLOPE_ROWS = 1
+PW_ROWS_ON_VECTOR = ()
+PW_FIRST = True
+PW_SHARE = 0
 PW_PARTS = 1
 DS_SHARE = 0
 ON_GPSIMD = ()
-SHARED = {'dom_bf1': ('second', 0, 1024), 'qm_bf1': ('second', 512, 1024)}
-AHEAD_OF_PW = 0
+SHARED = {'dom_bf2': ('late', 0, 2048), 'qm_bf2': ('late', 1024, 2048), 'dom_bf1': ('second', 0, 1024), 'qm_bf1': ('second', 512, 1024)}
+AHEAD_OF_PW = 1
 DS_QUANT_PARTS = 1
 LOOK = 1
 FIRST_PARTS = 2
 FIRST_ON_VECTOR = True
-TAGS = {'word_pairs': 'pool_scales', 'grad_sb1': 'qm_raw1', 'grad_sb3': 'qm_raw2', 'first': 'do_bf1', 'second': 'neg_slope'}
+TAGS = {'first': 'do_bf1', 'c_codes': 'pool_scales', 'grad_sb1': 'qm_raw0', 'late': 'prob', 'second': 'neg_slope'}
 
 
 def tile_attend_gat_sig_c_kernel(tc, qT, c_words, c_scales, doT, rw, qm, dom, offs, out):
@@ -60,20 +62,52 @@ def tile_attend_gat_sig_c_kernel(tc, qT, c_words, c_scales, doT, rw, qm, dom, of
 
         offsets = sb.tile([P, N // 16], U16, name="offsets")
         nc.sync.dma_start(offsets[:], offs)
+        gate = tile("gate", [P, 2 * PACK - 1], F32)
+        for b in range(2):
+            (nc.sync if HEAD == "front" else nc.scalar).dma_start(
+                out=gate[b:P:2, :], in_=rw[0].rearrange("(g x) o -> g (x o)", x=2 * PACK)[:, b : b + 2 * PACK - 1]
+            )
         pool_words = tile("pool_words", [P, T], I32)
-        nc.sync.dma_start(out=pool_words[:], in_=c_words[0].rearrange("p t b -> p (t b)").bitcast(I32))
+        if HEAD != "front":
+            nc.sync.dma_start(out=pool_words[:], in_=c_words[0].rearrange("p t b -> p (t b)").bitcast(I32))
 
         pool_scales = tile("pool_scales", [P, T // 4], I32)
-        nc.vector.memset(pool_scales[:], 0)
+        (nc.vector if HEAD == "front" else nc.gpsimd).memset(pool_scales[:], 0)
         scale_rows = c_scales.bitcast(I32)
         for r in range(4):
-            nc.scalar.dma_start(
+            nc.sync.dma_start(
                 out=pool_scales[r:P:16, :], in_=scale_rows[:, r:16:4, :].rearrange("o q t -> q o t")
             )
+        if HEAD == "front":
+            nc.sync.dma_start(out=pool_words[:], in_=c_words[0].rearrange("p t b -> p (t b)").bitcast(I32))
         warm_in = tile("warm_in", [P, 1], F32)
         warm_out = tile("warm_out", [P, 1], F32)
-        nc.vector.memset(warm_in[:], 0.0)
+        nc.gpsimd.memset(warm_in[:], 0.0)
         nc.scalar.activation(out=warm_out[:], in_=warm_in[:], func=SIGMOID)
+
+        c_sc = [tile("c_sc%d" % o, [P, N], U8) for o in range(PASSES)]
+        nc.gpsimd.memset(c_sc[1][:].bitcast(I32), 0)
+        windows = [tile("window%d" % w, [P, T], F32) for w in range(WINDOWS)]
+        nc.gpsimd.memset(windows[0][:], 0.0)
+        nc.vector.memset(windows[1][:, 0 : T // 2 - 1], 0.0)
+        nc.vector.memset(windows[1][:, T // 2 - 1 : T], 0.0)
+        nc.vector.memset(windows[2][:, 0 : T // 2 - 1], 0.0)
+        nc.vector.memset(windows[2][:, T // 2 - 1 : T // 2], 0.0)
+        nc.gpsimd.memset(windows[2][:, T // 2 : T], 0.0)
+        neg_gate = tile("neg_gate", [P, 2 * PACK - 1], F32)
+        nc.gpsimd.tensor_scalar(neg_gate[:], gate[:], -1.0, 0.0, MULT, ADD)
+
+        word_pairs = tile("word_pairs", [P, N], U32)
+        if HEAD == "front":
+            nc.vector.tensor_copy(c_sc[0][:], pool_scales[:].bitcast(U8).indirect(offsets[:]))
+        nc.vector.tensor_copy(word_pairs[:], pool_words[:].bitcast(U32).indirect(offsets[:]))
+        if HEAD != "front":
+            nc.vector.tensor_copy(c_sc[0][:], pool_scales[:].bitcast(U8).indirect(offsets[:]))
+        c_codes = tile("c_codes", [P, PASSES * 2 * N], U8)
+        nc.vector.tensor_copy(
+            c_codes[:].bitcast(U16).rearrange("p (o n) -> p o n", o=PASSES),
+            word_pairs[:].bitcast(U16).rearrange("p (n o) -> p o n", o=PASSES),
+        )
 
         def load_pieces(name, src, pieces):
             loaded = []
@@ -81,7 +115,10 @@ def tile_attend_gat_sig_c_kernel(tc, qT, c_words, c_scales, doT, rw, qm, dom, of
                 g0 = 0
                 loaded.append([])
                 for h, (groups, share) in enumerate(pieces[o]):
-                    raw = tile("%s%d_%d" % (name, o, h), [P, PACK, 8 * groups], F32)
+                    key = "%s%d_%d" % (name, o, h)
+                    if key == SHIFT_BEFORE:
+                        nc.sync.dma_start(out=c_sc[1][0 : P - 16, :].bitcast(I32), in_=c_sc[0][16:P, :].bitcast(I32))
+                    raw = tile(key, [P, PACK, 8 * groups], F32)
                     rows = src[0, o * K_PASS : (o + 1) * K_PASS, 8 * g0 : 8 * (g0 + groups)]
                     nc.sync.dma_start(out=raw[:], in_=rows.rearrange("(p j) w -> p j w", j=PACK))
                     loaded[o].append((raw, g0, groups, share))
@@ -95,11 +132,6 @@ def tile_attend_gat_sig_c_kernel(tc, qT, c_words, c_scales, doT, rw, qm, dom, of
             return raw
 
         q_raw = load_pieces("q_raw", qT, Q_PIECES)
-        gate = tile("gate", [P, 2 * PACK - 1], F32)
-        for b in range(2):
-            nc.gpsimd.dma_start(
-                out=gate[b:P:2, :], in_=rw[0].rearrange("(g x) o -> g (x o)", x=2 * PACK)[:, b : b + 2 * PACK - 1]
-            )
         do_raw = load_pieces("do_raw", doT, DO_PIECES)
         qm_raw, dom_raw = [], []
         d0 = 0
@@ -113,26 +145,6 @@ def tile_attend_gat_sig_c_kernel(tc, qT, c_words, c_scales, doT, rw, qm, dom, of
                 qm_raw.append(qm_c[:, :, s0 : s0 + step])
                 s0 += step
             d0 += width
-
-        windows = [tile("window%d" % w, [P, T], F32) for w in range(WINDOWS)]
-        c_sc = [tile("c_sc%d" % o, [P, N], U8) for o in range(PASSES)]
-        nc.gpsimd.memset(c_sc[1][:].bitcast(I32), 0)
-        nc.gpsimd.memset(windows[0][:], 0.0)
-        for w in range(1, WINDOWS):
-            nc.vector.memset(windows[w][:, 0 : T // 2 - 1], 0.0)
-            nc.vector.memset(windows[w][:, T // 2 - 1 : T], 0.0)
-
-        nc.vector.tensor_copy(c_sc[0][:], pool_scales[:].bitcast(U8).indirect(offsets[:]))
-        nc.scalar.dma_start(out=c_sc[1][0 : P - 16, :].bitcast(I32), in_=c_sc[0][16:P, :].bitcast(I32))
-        word_pairs = tile("word_pairs", [P, N], U32)
-        nc.vector.tensor_copy(word_pairs[:], pool_words[:].bitcast(U32).indirect(offsets[:]))
-        c_codes = tile("c_codes", [P, PASSES * 2 * N], U8)
-        nc.vector.tensor_copy(
-            c_codes[:].bitcast(U16).rearrange("p (o n) -> p o n", o=PASSES),
-            word_pairs[:].bitcast(U16).rearrange("p (n o) -> p o n", o=PASSES),
-        )
-        neg_gate = tile("neg_gate", [P, 2 * PACK - 1], F32)
-        nc.gpsimd.tensor_scalar(neg_gate[:], gate[:], -1.0, 0.0, MULT, ADD)
 
         def quantize(name, grouped, fmt, pieces=1):
             words = grouped.shape[1] // PACK

@@ -25,27 +25,28 @@ PACK = 4
 K_PASS = P * PACK
 PASSES = D // K_PASS
 GROUPS = P // 2
-Q_PIECES = (((64, 40),), ((32, 0), (32, 22)))
-DO_PIECES = (((32, 32), (32, 32)), ((32, 32), (32, 32)))
-STEP_WIDTHS = ((128, 128, 256), (256, 256))
+Q_PIECES = (((64, 44),), ((64, 64),))
+DO_PIECES = (((64, 44),), ((32, 32), (32, 22)))
+STEP_WIDTHS = ((128, 128, 256), (512,))
 WINDOWS = 3
+PW_ON_GPSIMD = 0
 HEAD = 'back'
-SHIFT_BEFORE = 'do_raw0_1'
-EARLY = 320
+SHIFT_BEFORE = 'do_raw1_0'
+EARLY = 288
 SLOPE_ROWS = 1
-PW_ROWS_ON_VECTOR = ()
+PW_ROWS_ON_VECTOR = (2, 3)
 PW_FIRST = True
 PW_SHARE = 0
-PW_PARTS = 1
+PW_PARTS = 2
 DS_SHARE = 0
 ON_GPSIMD = ()
 SHARED = {'dom_bf2': ('late', 0, 2048), 'qm_bf2': ('late', 1024, 2048), 'dom_bf1': ('second', 0, 1024), 'qm_bf1': ('second', 512, 1024)}
 AHEAD_OF_PW = 1
-DS_QUANT_PARTS = 1
+DS_QUANT_PARTS = 2
 LOOK = 1
 FIRST_PARTS = 2
 FIRST_ON_VECTOR = True
-TAGS = {'first': 'do_bf1', 'c_codes': 'pool_scales', 'grad_sb1': 'qm_raw0', 'late': 'prob', 'second': 'neg_slope'}
+TAGS = {'first': 'do_bf1', 'c_codes': 'pool_scales', 'grad_sb3': 'qm_raw1', 'late': 'pw_bf', 'second': 'do_raw1_0'}
 
 
 def tile_attend_gat_sig_c_kernel(tc, qT, c_words, c_scales, doT, rw, qm, dom, offs, out):
@@ -205,6 +206,7 @@ def tile_attend_gat_sig_c_kernel(tc, qT, c_words, c_scales, doT, rw, qm, dom, of
         def minus_gate(t):
             return neg_gate[:, 2 * t : 2 * t + 1]
 
+        homes = {}
         early, late = slice(0, EARLY), slice(EARLY, N)
         neg_slope = tile("neg_slope", [P, PACK, max(EARLY, 16)], F32)
 
@@ -223,11 +225,20 @@ def tile_attend_gat_sig_c_kernel(tc, qT, c_words, c_scales, doT, rw, qm, dom, of
                 nc.scalar.activation(out=neg_pw[:, t, :], in_=prob[:, t, :], func=COPY, scale=minus_gate(t))
         if PW_FIRST:
             slopes()
-        pw_bf = tile("pw_bf", [P, PACK * N], BF16)
+        own = N // 4 - PW_ON_GPSIMD
+        pw_bf = tile("pw_bf", [P, 16 * own], BF16)
+        if PW_ON_GPSIMD:
+            homes["first"] = tile("first", [P, 2048], BF16)
+            pw_late = homes["first"][:, 1024:2048]
+            nc.gpsimd.tensor_scalar(
+                pw_late.rearrange("p (n t) -> p n t", t=PACK),
+                neg_pw[:, :, 4 * own : N].rearrange("p t n -> p n t"),
+                -1.0, 0.0, MULT, ADD,
+            )
         if PW_SHARE:
             nc.vector.tensor_scalar(words_view(pw_bf[:])[:, 0:PW_SHARE], rows_view(neg_pw[:])[:, 0:PW_SHARE], -1.0, None, MULT)
         for k in range(PW_PARTS):
-            cs = slice(PW_SHARE + k * (N // 4 - PW_SHARE) // PW_PARTS, PW_SHARE + (k + 1) * (N // 4 - PW_SHARE) // PW_PARTS)
+            cs = slice(PW_SHARE + k * (own - PW_SHARE) // PW_PARTS, PW_SHARE + (k + 1) * (own - PW_SHARE) // PW_PARTS)
             nc.scalar.activation(out=words_view(pw_bf[:])[:, cs], in_=rows_view(neg_pw[:])[:, cs], func=COPY, scale=-1.0)
 
         part = tile("part", [P, PACK, N], F32)
@@ -262,17 +273,26 @@ def tile_attend_gat_sig_c_kernel(tc, qT, c_words, c_scales, doT, rw, qm, dom, of
                 else:
                     grouped = tile(key, [P, width], BF16)[:]
                 if key in ON_GPSIMD:
-                    nc.gpsimd.tensor_scalar(words_view(grouped), rows_view(raw), 1.0, 0.0, MULT, ADD)
+                    nc.gpsimd.tensor_scalar(
+                        grouped.rearrange("p (n t) -> p n t", t=PACK), raw.rearrange("p t n -> p n t"), 1.0, 0.0, MULT, ADD
+                    )
                 else:
                     nc.scalar.copy(words_view(grouped), rows_view(raw))
                 made.append((name, grouped, fmt))
             return [quantize("%s%d" % (name, c), grouped, fmt) for name, grouped, fmt in made]
 
-        homes = {}
         operands = {}
         for c in range(AHEAD_OF_PW):
             operands[c] = query_operands(c)
-        pw_codes, pw_scales = quantize("pw", pw_bf[:], E4M3)
+        if PW_ON_GPSIMD:
+            pw_codes = tile("pw_codes", [P, N], U32)
+            pw_scales = tile("pw_scales", [P, N], U8)
+            for w0, src in ((0, pw_bf[:]), (N // 2, pw_late)):
+                nc.vector.quantize_mx(
+                    out=pw_codes[:, w0 : w0 + N // 2].bitcast(E4M3), scales=pw_scales[:, w0 : w0 + N // 2], in_=src
+                )
+        else:
+            pw_codes, pw_scales = quantize("pw", pw_bf[:], E4M3)
         ds_codes, ds_scales = quantize("ds", ds_bf[:], E5M2, DS_QUANT_PARTS)
 
         first = 0

@@ -25,28 +25,28 @@ PACK = 4
 K_PASS = P * PACK
 PASSES = D // K_PASS
 GROUPS = P // 2
-Q_PIECES = (((64, 44),), ((64, 64),))
-DO_PIECES = (((64, 44),), ((32, 32), (32, 22)))
-STEP_WIDTHS = ((128, 128, 256), (512,))
+HALF = N // 2
+Q_PIECES = (((64, 40),), ((64, (40, 40)),))
+DO_PIECES = (((64, (64, 40)),), ((64, (64, 24)),))
+STEPS = (128, 128, 256, 512)
+ROW_LOADS = (('dom', 128), ('qm', 128), ('dom', 128), ('qm', 128), ('dom', 256), ('qm', 256), ('dom', 512), ('qm', 512))
+BY_PARITY = 256
+SHIFT_ON_SCALAR = False
+SPLIT_TWICE = True
+RANGES = (((256, 'S'),), ((128, 'S'), (128, 'F')))
+SIG_SPLIT = False
+TEXT = 'r0 s0 w0 r1 s1 o0 P0 p0 d0 D0 e0 w1 p1 d1 P1 D1 x0'
 WINDOWS = 3
-PW_ON_GPSIMD = 0
 HEAD = 'back'
 SHIFT_BEFORE = 'do_raw1_0'
-EARLY = 288
 SLOPE_ROWS = 1
-PW_ROWS_ON_VECTOR = (2, 3)
-PW_FIRST = True
-PW_SHARE = 0
-PW_PARTS = 2
-DS_SHARE = 0
+PW_ROWS_ON_VECTOR = ((0,), (0,))
+PW_SHARE = (32, 32)
 ON_GPSIMD = ()
-SHARED = {'dom_bf2': ('late', 0, 2048), 'qm_bf2': ('late', 1024, 2048), 'dom_bf1': ('second', 0, 1024), 'qm_bf1': ('second', 512, 1024)}
-AHEAD_OF_PW = 1
-DS_QUANT_PARTS = 2
+SHARED = {}
 LOOK = 1
-FIRST_PARTS = 2
-FIRST_ON_VECTOR = True
-TAGS = {'first': 'do_bf1', 'c_codes': 'pool_scales', 'grad_sb3': 'qm_raw1', 'late': 'pw_bf', 'second': 'do_raw1_0'}
+FIRST_ON_VECTOR = False
+TAGS = {'first': 'do_bf1', 'c_codes': 'pool_scales', 'pw_bf0': 'do_raw1_0', 'pw_bf1': 'neg_slope0', 'dom_bf1': 'part0', 'qm_bf1': 'dom_bf0', 'dom_bf2': 'ds_bf0', 'part1': 'do_raw1_0', 'ds_bf1': 'ds_bf0', 'grad_sb1': 'qm_raw2', 'grad_sb2': 'dom_raw2', 'grad_sb3': 'qm_raw3'}
 
 
 def tile_attend_gat_sig_c_kernel(tc, qT, c_words, c_scales, doT, rw, qm, dom, offs, out):
@@ -65,11 +65,11 @@ def tile_attend_gat_sig_c_kernel(tc, qT, c_words, c_scales, doT, rw, qm, dom, of
         nc.sync.dma_start(offsets[:], offs)
         gate = tile("gate", [P, 2 * PACK - 1], F32)
         for b in range(2):
-            (nc.sync if HEAD == "front" else nc.scalar).dma_start(
+            (nc.sync if HEAD == "front" or (HEAD == "front2" and b == 0) else nc.scalar).dma_start(
                 out=gate[b:P:2, :], in_=rw[0].rearrange("(g x) o -> g (x o)", x=2 * PACK)[:, b : b + 2 * PACK - 1]
             )
         pool_words = tile("pool_words", [P, T], I32)
-        if HEAD != "front":
+        if HEAD == "back":
             nc.sync.dma_start(out=pool_words[:], in_=c_words[0].rearrange("p t b -> p (t b)").bitcast(I32))
 
         pool_scales = tile("pool_scales", [P, T // 4], I32)
@@ -79,7 +79,7 @@ def tile_attend_gat_sig_c_kernel(tc, qT, c_words, c_scales, doT, rw, qm, dom, of
             nc.sync.dma_start(
                 out=pool_scales[r:P:16, :], in_=scale_rows[:, r:16:4, :].rearrange("o q t -> q o t")
             )
-        if HEAD == "front":
+        if HEAD != "back":
             nc.sync.dma_start(out=pool_words[:], in_=c_words[0].rearrange("p t b -> p (t b)").bitcast(I32))
         warm_in = tile("warm_in", [P, 1], F32)
         warm_out = tile("warm_out", [P, 1], F32)
@@ -88,6 +88,11 @@ def tile_attend_gat_sig_c_kernel(tc, qT, c_words, c_scales, doT, rw, qm, dom, of
 
         c_sc = [tile("c_sc%d" % o, [P, N], U8) for o in range(PASSES)]
         nc.gpsimd.memset(c_sc[1][:].bitcast(I32), 0)
+        moving = {}
+        for name in ("pw", "ds"):
+            moving[name] = (tile(name + "_codes", [P, HALF + N], U32), tile(name + "_scales", [P, HALF + N], U8))
+            for x in moving[name]:
+                nc.gpsimd.memset(x[:, 0:HALF].bitcast(I32), 0)
         windows = [tile("window%d" % w, [P, T], F32) for w in range(WINDOWS)]
         nc.gpsimd.memset(windows[0][:], 0.0)
         nc.vector.memset(windows[1][:, 0 : T // 2 - 1], 0.0)
@@ -99,16 +104,17 @@ def tile_attend_gat_sig_c_kernel(tc, qT, c_words, c_scales, doT, rw, qm, dom, of
         nc.gpsimd.tensor_scalar(neg_gate[:], gate[:], -1.0, 0.0, MULT, ADD)
 
         word_pairs = tile("word_pairs", [P, N], U32)
-        if HEAD == "front":
+        if HEAD != "back":
             nc.vector.tensor_copy(c_sc[0][:], pool_scales[:].bitcast(U8).indirect(offsets[:]))
         nc.vector.tensor_copy(word_pairs[:], pool_words[:].bitcast(U32).indirect(offsets[:]))
-        if HEAD != "front":
+        if HEAD == "back":
             nc.vector.tensor_copy(c_sc[0][:], pool_scales[:].bitcast(U8).indirect(offsets[:]))
         c_codes = tile("c_codes", [P, PASSES * 2 * N], U8)
-        nc.vector.tensor_copy(
-            c_codes[:].bitcast(U16).rearrange("p (o n) -> p o n", o=PASSES),
-            word_pairs[:].bitcast(U16).rearrange("p (n o) -> p o n", o=PASSES),
-        )
+        for part_o in ([slice(0, 1), slice(1, 2)] if SPLIT_TWICE else [slice(0, 2)]):
+            nc.vector.tensor_copy(
+                c_codes[:].bitcast(U16).rearrange("p (o n) -> p o n", o=PASSES)[:, part_o],
+                word_pairs[:].bitcast(U16).rearrange("p (n o) -> p o n", o=PASSES)[:, part_o],
+            )
 
         def load_pieces(name, src, pieces):
             loaded = []
@@ -118,7 +124,7 @@ def tile_attend_gat_sig_c_kernel(tc, qT, c_words, c_scales, doT, rw, qm, dom, of
                 for h, (groups, share) in enumerate(pieces[o]):
                     key = "%s%d_%d" % (name, o, h)
                     if key == SHIFT_BEFORE:
-                        nc.sync.dma_start(out=c_sc[1][0 : P - 16, :].bitcast(I32), in_=c_sc[0][16:P, :].bitcast(I32))
+                        (nc.scalar if SHIFT_ON_SCALAR else nc.sync).dma_start(out=c_sc[1][0 : P - 16, :].bitcast(I32), in_=c_sc[0][16:P, :].bitcast(I32))
                     raw = tile(key, [P, PACK, 8 * groups], F32)
                     rows = src[0, o * K_PASS : (o + 1) * K_PASS, 8 * g0 : 8 * (g0 + groups)]
                     nc.sync.dma_start(out=raw[:], in_=rows.rearrange("(p j) w -> p j w", j=PACK))
@@ -128,24 +134,31 @@ def tile_attend_gat_sig_c_kernel(tc, qT, c_words, c_scales, doT, rw, qm, dom, of
 
         def load_queries(name, rows):
             raw = tile(name, [P, PACK, rows.shape[1]], F32)
-            for t in range(PACK):
-                nc.sync.dma_start(out=raw[:, t, :], in_=rows.rearrange("(g t b) w -> t g b w", t=PACK, b=2)[t])
+            if rows.shape[1] <= BY_PARITY:
+                for b in range(2):
+                    nc.sync.dma_start(out=raw[b:P:2], in_=rows.rearrange("(g t b) w -> b g t w", t=PACK, b=2)[b])
+            else:
+                for t in range(PACK):
+                    nc.sync.dma_start(out=raw[:, t, :], in_=rows.rearrange("(g t b) w -> t g b w", t=PACK, b=2)[t])
             return raw
 
         q_raw = load_pieces("q_raw", qT, Q_PIECES)
         do_raw = load_pieces("do_raw", doT, DO_PIECES)
-        qm_raw, dom_raw = [], []
-        d0 = 0
-        for c, steps in enumerate(STEP_WIDTHS):
-            width = sum(steps)
-            dom_c = load_queries("dom_raw%d" % c, dom[0, :, d0 : d0 + width])
-            qm_c = load_queries("qm_raw%d" % c, qm[0, :, d0 : d0 + width])
-            s0 = 0
-            for step in steps:
-                dom_raw.append(dom_c[:, :, s0 : s0 + step])
-                qm_raw.append(qm_c[:, :, s0 : s0 + step])
-                s0 += step
-            d0 += width
+        loaded = {"dom": [], "qm": []}
+        for name, width in ROW_LOADS:
+            d0 = sum(w for a, w, x in loaded[name])
+            src = {"dom": dom, "qm": qm}[name]
+            loaded[name].append((d0, width, load_queries("%s_raw%d" % (name, len(loaded[name])), src[0, :, d0 : d0 + width])))
+
+        def steps_of(name):
+            cut, d0 = [], 0
+            for step in STEPS:
+                at, width, raw = [x for x in loaded[name] if x[0] <= d0 and d0 + step <= x[0] + x[1]][0]
+                cut.append(raw[:, :, d0 - at : d0 - at + step])
+                d0 += step
+            return cut
+
+        dom_raw, qm_raw = steps_of("dom"), steps_of("qm")
 
         def quantize(name, grouped, fmt, pieces=1):
             words = grouped.shape[1] // PACK
@@ -165,10 +178,11 @@ def tile_attend_gat_sig_c_kernel(tc, qT, c_words, c_scales, doT, rw, qm, dom, of
             dst = grouped[:].rearrange("p (t g b j) -> p g t j b", t=PACK, b=2, j=PACK)
             for raw, g0, groups, share in pieces:
                 src = raw[:].rearrange("p j (g t b) -> p g t j b", t=PACK, b=2)
-                if share > 0:
-                    nc.vector.tensor_copy(dst[:, g0 : g0 + share], src[:, 0:share])
-                if share < groups:
-                    nc.scalar.copy(dst[:, g0 + share : g0 + groups], src[:, share:groups])
+                for ts, part_share in ([(slice(0, PACK), share)] if isinstance(share, int) else [(slice(0, 2), share[0]), (slice(2, 4), share[1])]):
+                    if part_share > 0:
+                        nc.vector.tensor_copy(dst[:, g0 : g0 + part_share, ts], src[:, 0:part_share, ts])
+                    if part_share < groups:
+                        nc.scalar.copy(dst[:, g0 + part_share : g0 + groups, ts], src[:, part_share:groups, ts])
             return grouped[:]
 
         def words_view(grouped):
@@ -196,9 +210,16 @@ def tile_attend_gat_sig_c_kernel(tc, qT, c_words, c_scales, doT, rw, qm, dom, of
         for o in range(PASSES):
             q_mx = quantize("q%d" % o, group_queries("q_bf%d" % o, q_raw[o]), E4M3, PACK)
             score_pass(a_banks, q_mx, E4M3, o)
-        prob = tile("prob", [P, PACK, N], F32)
-        for t in range(PACK):
-            nc.scalar.activation(out=prob[:, t, :], in_=a_banks[t][:], func=SIGMOID)
+        prob = [tile("prob%d" % h, [P, PACK, HALF], F32) for h in range(2)] if SIG_SPLIT else None
+        if SIG_SPLIT:
+            for h in range(2):
+                for t in range(PACK):
+                    nc.scalar.activation(out=prob[h][:, t, :], in_=a_banks[t][:, h * HALF : (h + 1) * HALF], func=SIGMOID)
+        else:
+            whole = tile("prob0", [P, PACK, N], F32)
+            prob = [whole[:, :, h * HALF : (h + 1) * HALF] for h in range(2)]
+            for t in range(PACK):
+                nc.scalar.activation(out=whole[:, t, :], in_=a_banks[t][:], func=SIGMOID)
         for o in range(PASSES):
             do_mx = quantize("do%d" % o, group_queries("do_bf%d" % o, do_raw[o]), E5M2, PACK)
             score_pass(dp_banks, do_mx, E5M2, o)
@@ -207,58 +228,71 @@ def tile_attend_gat_sig_c_kernel(tc, qT, c_words, c_scales, doT, rw, qm, dom, of
             return neg_gate[:, 2 * t : 2 * t + 1]
 
         homes = {}
-        early, late = slice(0, EARLY), slice(EARLY, N)
-        neg_slope = tile("neg_slope", [P, PACK, max(EARLY, 16)], F32)
+        neg_pw, neg_slope, pw_bf, part, ds_bf, cuts = {}, {}, {}, {}, {}, {}
+        for h in range(2):
+            cuts[h], at = [], 0
+            for width, kind in RANGES[h]:
+                cuts[h].append((slice(at, at + width), kind))
+                at += width
 
-        def slopes():
-            for t0 in range(0, PACK if EARLY else 0, SLOPE_ROWS):
-                rows = prob[:, t0 : t0 + SLOPE_ROWS, early]
-                nc.vector.scalar_tensor_tensor(neg_slope[:, t0 : t0 + SLOPE_ROWS, :], rows, 1.0, rows, SUB, MULT)
+        def pw_rows(h):
+            neg_pw[h] = tile("neg_pw%d" % h, [P, PACK, HALF], F32)
+            for t in range(PACK):
+                if t in PW_ROWS_ON_VECTOR[h]:
+                    nc.vector.tensor_scalar(neg_pw[h][:, t, :], prob[h][:, t, :], minus_gate(t), None, MULT)
+                else:
+                    nc.scalar.activation(out=neg_pw[h][:, t, :], in_=prob[h][:, t, :], func=COPY, scale=minus_gate(t))
 
-        if not PW_FIRST:
-            slopes()
-        neg_pw = tile("neg_pw", [P, PACK, N], F32)
-        for t in range(PACK):
-            if t in PW_ROWS_ON_VECTOR:
-                nc.vector.tensor_scalar(neg_pw[:, t, :], prob[:, t, :], minus_gate(t), None, MULT)
-            else:
-                nc.scalar.activation(out=neg_pw[:, t, :], in_=prob[:, t, :], func=COPY, scale=minus_gate(t))
-        if PW_FIRST:
-            slopes()
-        own = N // 4 - PW_ON_GPSIMD
-        pw_bf = tile("pw_bf", [P, 16 * own], BF16)
-        if PW_ON_GPSIMD:
-            homes["first"] = tile("first", [P, 2048], BF16)
-            pw_late = homes["first"][:, 1024:2048]
-            nc.gpsimd.tensor_scalar(
-                pw_late.rearrange("p (n t) -> p n t", t=PACK),
-                neg_pw[:, :, 4 * own : N].rearrange("p t n -> p n t"),
-                -1.0, 0.0, MULT, ADD,
-            )
-        if PW_SHARE:
-            nc.vector.tensor_scalar(words_view(pw_bf[:])[:, 0:PW_SHARE], rows_view(neg_pw[:])[:, 0:PW_SHARE], -1.0, None, MULT)
-        for k in range(PW_PARTS):
-            cs = slice(PW_SHARE + k * (own - PW_SHARE) // PW_PARTS, PW_SHARE + (k + 1) * (own - PW_SHARE) // PW_PARTS)
-            nc.scalar.activation(out=words_view(pw_bf[:])[:, cs], in_=rows_view(neg_pw[:])[:, cs], func=COPY, scale=-1.0)
+        def slopes(h):
+            width = sum(w for w, kind in RANGES[h] if kind != "F")
+            if width:
+                neg_slope[h] = tile("neg_slope%d" % h, [P, PACK, width], F32)
+                for t0 in range(0, PACK, SLOPE_ROWS):
+                    rows = prob[h][:, t0 : t0 + SLOPE_ROWS, 0:width]
+                    nc.vector.scalar_tensor_tensor(neg_slope[h][:, t0 : t0 + SLOPE_ROWS, :], rows, 1.0, rows, SUB, MULT)
 
-        part = tile("part", [P, PACK, N], F32)
-        for t in range(PACK):
-            if EARLY:
-                nc.vector.scalar_tensor_tensor(
-                    part[:, t, early], dp_banks[t][:, early], minus_gate(t), neg_slope[:, t, :], MULT, MULT
+        def pw_weave(h):
+            share = PW_SHARE[h]
+            if share == "G":
+                homes["first"] = tile("first", [P, 2048], BF16)
+                pw_bf[h] = homes["first"][:, 1024:2048]
+                nc.gpsimd.tensor_scalar(
+                    pw_bf[h].rearrange("p (n t) -> p n t", t=PACK), neg_pw[h][:].rearrange("p t n -> p n t"), -1.0, 0.0, MULT, ADD
                 )
-            if EARLY < N:
-                nc.vector.scalar_tensor_tensor(part[:, t, late], prob[:, t, late], 1.0, dp_banks[t][:, late], SUB, MULT)
-        ds_bf = tile("ds_bf", [P, PACK * N], BF16)
-        e4 = EARLY // 4
-        if EARLY:
-            if DS_SHARE:
-                nc.vector.tensor_copy(words_view(ds_bf[:])[:, 0:DS_SHARE], rows_view(part[:])[:, 0:DS_SHARE])
-            nc.scalar.copy(words_view(ds_bf[:])[:, DS_SHARE:e4], rows_view(part[:])[:, DS_SHARE:e4])
-        if EARLY < N:
-            nc.vector.tensor_tensor(
-                words_view(ds_bf[:])[:, e4:], rows_view(part[:])[:, e4:], rows_view(neg_pw[:])[:, e4:], MULT
-            )
+                return
+            pw_bf[h] = tile("pw_bf%d" % h, [P, PACK * HALF], BF16)[:]
+            dst, src = words_view(pw_bf[h]), rows_view(neg_pw[h][:])
+            if share:
+                nc.vector.tensor_scalar(dst[:, 0:share], src[:, 0:share], -1.0, None, MULT)
+            if share < HALF // 4:
+                nc.scalar.activation(out=dst[:, share:], in_=src[:, share:], func=COPY, scale=-1.0)
+
+        def products(h):
+            part[h] = tile("part%d" % h, [P, PACK, HALF], F32)
+            for cols, kind in cuts[h]:
+                for t in range(PACK):
+                    dp = dp_banks[t][:, h * HALF + cols.start : h * HALF + cols.stop]
+                    if kind == "F":
+                        nc.vector.scalar_tensor_tensor(part[h][:, t, cols], prob[h][:, t, cols], 1.0, dp, SUB, MULT)
+                    else:
+                        nc.vector.scalar_tensor_tensor(part[h][:, t, cols], dp, minus_gate(t), neg_slope[h][:, t, cols], MULT, MULT)
+
+        def ds_weave(h):
+            ds_bf[h] = tile("ds_bf%d" % h, [P, PACK * HALF], BF16)[:]
+            for cols, kind in cuts[h]:
+                cs = slice(cols.start // 4, cols.stop // 4)
+                dst, src = words_view(ds_bf[h])[:, cs], rows_view(part[h][:])[:, cs]
+                if kind == "F":
+                    nc.vector.tensor_tensor(dst, src, rows_view(neg_pw[h][:])[:, cs], MULT)
+                elif kind == "V":
+                    nc.vector.tensor_copy(dst, src)
+                else:
+                    nc.scalar.copy(dst, src)
+
+        def quantize_half(name, grouped, fmt, h):
+            codes, scales = moving[name]
+            cols = slice((h + 1) * HALF, (h + 2) * HALF)
+            nc.vector.quantize_mx(out=codes[:, cols].bitcast(fmt), scales=scales[:, cols], in_=grouped)
 
         def query_operands(c):
             made = []
@@ -281,46 +315,56 @@ def tile_attend_gat_sig_c_kernel(tc, qT, c_words, c_scales, doT, rw, qm, dom, of
                 made.append((name, grouped, fmt))
             return [quantize("%s%d" % (name, c), grouped, fmt) for name, grouped, fmt in made]
 
-        operands = {}
-        for c in range(AHEAD_OF_PW):
-            operands[c] = query_operands(c)
-        if PW_ON_GPSIMD:
-            pw_codes = tile("pw_codes", [P, N], U32)
-            pw_scales = tile("pw_scales", [P, N], U8)
-            for w0, src in ((0, pw_bf[:]), (N // 2, pw_late)):
-                nc.vector.quantize_mx(
-                    out=pw_codes[:, w0 : w0 + N // 2].bitcast(E4M3), scales=pw_scales[:, w0 : w0 + N // 2], in_=src
-                )
-        else:
-            pw_codes, pw_scales = quantize("pw", pw_bf[:], E4M3)
-        ds_codes, ds_scales = quantize("ds", ds_bf[:], E5M2, DS_QUANT_PARTS)
+        operands, stationary = {}, {}
 
-        first = 0
-        for c in range(len(dom_raw)):
-            for ahead in range(c, min(c + LOOK + 1, len(dom_raw))):
-                if ahead not in operands:
-                    operands[ahead] = query_operands(ahead)
-            (dom_codes, dom_scales), (qm_codes, qm_scales) = operands[c]
-            blocks = range(first, first + dom_raw[c].shape[2] // P)
-            for b in blocks:
-                cols = slice((b - first) * P, (b - first + 1) * P)
-                acc = bank(b, "grad%d" % b)
-                products = [
-                    (dom_codes[:, cols].bitcast(E5M2), dom_scales[:, cols], pw_codes[:].bitcast(E4M3), pw_scales[:]),
-                    (qm_codes[:, cols].bitcast(E4M3), qm_scales[:, cols], ds_codes[:].bitcast(E5M2), ds_scales[:]),
-                ]
-                for k, (lhs, lhs_scale, rhs, rhs_scale) in enumerate(products):
-                    nc.tensor.matmul_mx(
-                        out=acc[:], lhsT=lhs, lhsT_scale=lhs_scale, rhs=rhs, rhs_scale=rhs_scale,
-                        start=(k == 0), stop=(k == 1),
-                    )
-                grad = tile("grad_sb%d" % b, [P, N], F32)
-                window = windows[b % len(windows)]
-                parts = FIRST_PARTS if b == 0 else 1
-                for h in range(parts):
-                    slots = slice(h * N // parts, (h + 1) * N // parts)
-                    copy = nc.vector.tensor_copy if (b == 0 and h == 0 and FIRST_ON_VECTOR) else nc.scalar.copy
-                    copy(grad[:, slots], acc[:, slots])
-                    nc.vector.tensor_copy(window[:].indirect(offsets[:, slots.start // 16 : slots.stop // 16]), grad[:, slots])
-                nc.sync.dma_start(out=out[b * P : (b + 1) * P, :], in_=window[:])
-            first = blocks.stop
+        def prepare(c):
+            if c not in operands and c < len(STEPS):
+                operands[c] = query_operands(c)
+                first = sum(STEPS[:c]) // P
+                for k in range(STEPS[c] // P):
+                    stationary[first + k] = [(codes[:, k * P : (k + 1) * P], scales[:, k * P : (k + 1) * P]) for codes, scales in operands[c]]
+
+        def gradient(b, acc, at):
+            cols = slice(at, at + N)
+            (dom_codes, dom_scales), (qm_codes, qm_scales) = stationary[b]
+            passes = [
+                (dom_codes.bitcast(E5M2), dom_scales, moving["pw"][0][:, cols].bitcast(E4M3), moving["pw"][1][:, cols]),
+                (qm_codes.bitcast(E4M3), qm_scales, moving["ds"][0][:, cols].bitcast(E5M2), moving["ds"][1][:, cols]),
+            ]
+            for k, (lhs, lhs_scale, rhs, rhs_scale) in enumerate(passes):
+                nc.tensor.matmul_mx(
+                    out=acc[:], lhsT=lhs, lhsT_scale=lhs_scale, rhs=rhs, rhs_scale=rhs_scale, start=(k == 0), stop=(k == 1)
+                )
+
+        def scatter(b, values, slots):
+            nc.vector.tensor_copy(windows[b % WINDOWS][:].indirect(offsets[:, slots.start // 16 : slots.stop // 16]), values)
+
+        ahead = {}
+
+        def early_product(b):
+            prepare([c for c in range(len(STEPS)) if sum(STEPS[: c + 1]) > b * P][0])
+            acc = bank(PACK - 1 - b, "early%d" % b)
+            gradient(b, acc, 0)
+            ahead[b] = tile("early_sb%d" % b, [P, HALF], F32)
+            (nc.vector.tensor_copy if FIRST_ON_VECTOR and b == 0 else nc.scalar.copy)(ahead[b][:], acc[:, HALF:N])
+
+        steps = {
+            "r": pw_rows, "s": slopes, "w": pw_weave, "p": products, "d": ds_weave, "o": prepare, "e": early_product,
+            "P": lambda h: quantize_half("pw", pw_bf[h], E4M3, h),
+            "D": lambda h: quantize_half("ds", ds_bf[h], E5M2, h),
+            "x": lambda b: scatter(b, ahead[b][:], slice(0, HALF)),
+        }
+        for step in TEXT.split():
+            steps[step[0]](int(step[1]))
+
+        for b in range(D // P):
+            c = [c for c in range(len(STEPS)) if sum(STEPS[: c + 1]) > b * P][0]
+            for k in range(c, c + LOOK + 1):
+                prepare(k)
+            acc = bank(b, "grad%d" % b)
+            gradient(b, acc, HALF)
+            slots = slice(HALF, N) if b in ahead else slice(0, N)
+            grad = tile("grad_sb%d" % b, [P, slots.stop - slots.start], F32)
+            nc.scalar.copy(grad[:], acc[:, slots])
+            scatter(b, grad[:], slots)
+            nc.sync.dma_start(out=out[b * P : (b + 1) * P, :], in_=windows[b % WINDOWS][:])

@@ -26,27 +26,27 @@ K_PASS = P * PACK
 PASSES = D // K_PASS
 GROUPS = P // 2
 HALF = N // 2
-Q_PIECES = (((64, 40),), ((64, (40, 40)),))
-DO_PIECES = (((64, (64, 40)),), ((64, (64, 24)),))
-STEPS = (128, 128, 256, 512)
-ROW_LOADS = (('dom', 128), ('qm', 128), ('dom', 128), ('qm', 128), ('dom', 256), ('qm', 256), ('dom', 512), ('qm', 512))
-BY_PARITY = 256
+Q_PIECES = (((64, 44),), ((64, (64, 24)),))
+DO_PIECES = (((64, (64, 40)),), ((64, (64, 64)),))
+STEPS = (256, 256, 512)
+ROW_LOADS = (('dom', 512), ('qm', 256), ('qm', 768), ('dom', 512))
+BY_PARITY = 0
 SHIFT_ON_SCALAR = False
-SPLIT_TWICE = True
-RANGES = (((256, 'S'),), ((128, 'S'), (128, 'F')))
+SPLIT_TWICE = False
+RANGES = (((256, 'F'),), ((256, 'F'),))
 SIG_SPLIT = False
-TEXT = 'r0 s0 w0 r1 s1 o0 P0 p0 d0 D0 e0 w1 p1 d1 P1 D1 x0'
+TEXT = 'r0 r1 s0 s1 w0 w1 o0 P0 P1 p0 d0 D0 e0 p1 d1 D1 x0'
 WINDOWS = 3
 HEAD = 'back'
 SHIFT_BEFORE = 'do_raw1_0'
-SLOPE_ROWS = 1
-PW_ROWS_ON_VECTOR = ((0,), (0,))
-PW_SHARE = (32, 32)
+SLOPE_ROWS = 4
+PW_ROWS_ON_VECTOR = ((0, 1), ())
+PW_SHARE = (16, 0)
 ON_GPSIMD = ()
 SHARED = {}
 LOOK = 1
 FIRST_ON_VECTOR = False
-TAGS = {'first': 'do_bf1', 'c_codes': 'pool_scales', 'pw_bf0': 'do_raw1_0', 'pw_bf1': 'neg_slope0', 'dom_bf1': 'part0', 'qm_bf1': 'dom_bf0', 'dom_bf2': 'ds_bf0', 'part1': 'do_raw1_0', 'ds_bf1': 'ds_bf0', 'grad_sb1': 'qm_raw2', 'grad_sb2': 'dom_raw2', 'grad_sb3': 'qm_raw3'}
+TAGS = {'first': 'do_bf1', 'c_codes': 'pool_scales', 'neg_pw1': 'do_bf1', 'dom_bf1': 'prob0', 'dom_bf3': 'qm_raw1', 'grad_sb1': 'qm_raw2', 'grad_sb3': 'qm_bf3'}
 
 
 def tile_attend_gat_sig_c_kernel(tc, qT, c_words, c_scales, doT, rw, qm, dom, offs, out):
@@ -90,9 +90,7 @@ def tile_attend_gat_sig_c_kernel(tc, qT, c_words, c_scales, doT, rw, qm, dom, of
         nc.gpsimd.memset(c_sc[1][:].bitcast(I32), 0)
         moving = {}
         for name in ("pw", "ds"):
-            moving[name] = (tile(name + "_codes", [P, HALF + N], U32), tile(name + "_scales", [P, HALF + N], U8))
-            for x in moving[name]:
-                nc.gpsimd.memset(x[:, 0:HALF].bitcast(I32), 0)
+            moving[name] = (tile(name + "_codes", [P, 2 * N], U32), tile(name + "_scales", [P, 2 * N], U8))
         windows = [tile("window%d" % w, [P, T], F32) for w in range(WINDOWS)]
         nc.gpsimd.memset(windows[0][:], 0.0)
         nc.vector.memset(windows[1][:, 0 : T // 2 - 1], 0.0)
@@ -162,8 +160,11 @@ def tile_attend_gat_sig_c_kernel(tc, qT, c_words, c_scales, doT, rw, qm, dom, of
 
         def quantize(name, grouped, fmt, pieces=1):
             words = grouped.shape[1] // PACK
-            codes = tile(name + "_codes", [P, words], U32)
-            scales = tile(name + "_scales", [P, words], U8)
+            if name in ("q1", "do1"):
+                codes, scales = [x[:, 0:N] for x in moving[{"q1": "pw", "do1": "ds"}[name]]]
+            else:
+                codes = tile(name + "_codes", [P, words], U32)
+                scales = tile(name + "_scales", [P, words], U8)
             step = words // pieces
             for w0 in range(0, words, step):
                 nc.vector.quantize_mx(
@@ -291,7 +292,7 @@ def tile_attend_gat_sig_c_kernel(tc, qT, c_words, c_scales, doT, rw, qm, dom, of
 
         def quantize_half(name, grouped, fmt, h):
             codes, scales = moving[name]
-            cols = slice((h + 1) * HALF, (h + 2) * HALF)
+            cols = slice(N + h * HALF, N + (h + 1) * HALF)
             nc.vector.quantize_mx(out=codes[:, cols].bitcast(fmt), scales=scales[:, cols], in_=grouped)
 
         def query_operands(c):
@@ -344,7 +345,7 @@ def tile_attend_gat_sig_c_kernel(tc, qT, c_words, c_scales, doT, rw, qm, dom, of
         def early_product(b):
             prepare([c for c in range(len(STEPS)) if sum(STEPS[: c + 1]) > b * P][0])
             acc = bank(PACK - 1 - b, "early%d" % b)
-            gradient(b, acc, 0)
+            gradient(b, acc, HALF)
             ahead[b] = tile("early_sb%d" % b, [P, HALF], F32)
             (nc.vector.tensor_copy if FIRST_ON_VECTOR and b == 0 else nc.scalar.copy)(ahead[b][:], acc[:, HALF:N])
 
@@ -362,7 +363,7 @@ def tile_attend_gat_sig_c_kernel(tc, qT, c_words, c_scales, doT, rw, qm, dom, of
             for k in range(c, c + LOOK + 1):
                 prepare(k)
             acc = bank(b, "grad%d" % b)
-            gradient(b, acc, HALF)
+            gradient(b, acc, N)
             slots = slice(HALF, N) if b in ahead else slice(0, N)
             grad = tile("grad_sb%d" % b, [P, slots.stop - slots.start], F32)
             nc.scalar.copy(grad[:], acc[:, slots])

@@ -24,29 +24,17 @@ P = 128
 PACK = 4
 K_PASS = P * PACK
 PASSES = D // K_PASS
-GROUPS = P // 2
+GROUPS = R // 8
 HALF = N // 2
-Q_PIECES = (((64, 44),), ((64, (64, 24)),))
-DO_PIECES = (((64, (64, 40)),), ((64, (64, 64)),))
-STEPS = (256, 256, 512)
-ROW_LOADS = (('dom', 512), ('qm', 256), ('qm', 768), ('dom', 512))
-BY_PARITY = 0
-SHIFT_ON_SCALAR = False
-SPLIT_TWICE = False
-RANGES = (((256, 'F'),), ((256, 'F'),))
-SIG_SPLIT = False
-TEXT = 'r0 r1 s0 s1 w0 w1 o0 P0 P1 p0 d0 D0 e0 p1 d1 D1 x0'
+LIST_BAND = 16
+PLANE_SHIFT = 16
+RUN = 4
 WINDOWS = 3
-HEAD = 'back'
-SHIFT_BEFORE = 'do_raw1_0'
-SLOPE_ROWS = 4
-PW_ROWS_ON_VECTOR = ((0, 1), ())
-PW_SHARE = (16, 0)
-ON_GPSIMD = ()
-SHARED = {}
-LOOK = 1
-FIRST_ON_VECTOR = False
-TAGS = {'first': 'do_bf1', 'c_codes': 'pool_scales', 'neg_pw1': 'do_bf1', 'dom_bf1': 'prob0', 'dom_bf3': 'qm_raw1', 'grad_sb1': 'qm_raw2', 'grad_sb3': 'qm_bf3'}
+
+Q_GROUPS_ON_VECTOR = 44
+PW_ROW_ON_VECTOR_FROM = 2
+FIRST_LOAD = 384
+STEP_WIDTHS = (P, P, P, P, 2 * P, 2 * P)
 
 
 def tile_attend_gat_sig_c_kernel(tc, qT, c_words, c_scales, doT, rw, qm, dom, offs, out):
@@ -55,32 +43,30 @@ def tile_attend_gat_sig_c_kernel(tc, qT, c_words, c_scales, doT, rw, qm, dom, of
         sb = ctx.enter_context(tc.tile_pool(name="sb", bufs=1))
         ps = ctx.enter_context(tc.psum_pool(name="ps", bufs=1))
 
-        def tile(name, shape, dtype):
-            return sb.tile(shape, dtype, name=name, tag=TAGS.get(name, name), align_bytes=64)
+        def tile(name, shape, dtype, place_of=None):
+            return sb.tile(shape, dtype, name=name, tag=place_of or name, align_bytes=64)
 
-        def bank(b, name):
-            return ps.tile([P, N], F32, name=name, tag="bank%d" % b)
+        def bank(index, name):
+            return ps.tile([P, N], F32, name=name, tag="bank%d" % index)
 
-        offsets = sb.tile([P, N // 16], U16, name="offsets")
+        offsets = sb.tile([P, N // LIST_BAND], U16, name="offsets")
         nc.sync.dma_start(offsets[:], offs)
         gate = tile("gate", [P, 2 * PACK - 1], F32)
         for b in range(2):
-            (nc.sync if HEAD == "front" or (HEAD == "front2" and b == 0) else nc.scalar).dma_start(
+            nc.scalar.dma_start(
                 out=gate[b:P:2, :], in_=rw[0].rearrange("(g x) o -> g (x o)", x=2 * PACK)[:, b : b + 2 * PACK - 1]
             )
         pool_words = tile("pool_words", [P, T], I32)
-        if HEAD == "back":
-            nc.sync.dma_start(out=pool_words[:], in_=c_words[0].rearrange("p t b -> p (t b)").bitcast(I32))
+        nc.sync.dma_start(out=pool_words[:], in_=c_words[0].rearrange("p t b -> p (t b)").bitcast(I32))
 
         pool_scales = tile("pool_scales", [P, T // 4], I32)
-        (nc.vector if HEAD == "front" else nc.gpsimd).memset(pool_scales[:], 0)
+        nc.gpsimd.memset(pool_scales[:], 0)
         scale_rows = c_scales.bitcast(I32)
-        for r in range(4):
+        for i in range(4):
             nc.sync.dma_start(
-                out=pool_scales[r:P:16, :], in_=scale_rows[:, r:16:4, :].rearrange("o q t -> q o t")
+                out=pool_scales[i:P:PLANE_SHIFT, :], in_=scale_rows[:, i:16:4, :].rearrange("o q t -> q o t")
             )
-        if HEAD != "back":
-            nc.sync.dma_start(out=pool_words[:], in_=c_words[0].rearrange("p t b -> p (t b)").bitcast(I32))
+
         warm_in = tile("warm_in", [P, 1], F32)
         warm_out = tile("warm_out", [P, 1], F32)
         nc.gpsimd.memset(warm_in[:], 0.0)
@@ -88,118 +74,84 @@ def tile_attend_gat_sig_c_kernel(tc, qT, c_words, c_scales, doT, rw, qm, dom, of
 
         c_sc = [tile("c_sc%d" % o, [P, N], U8) for o in range(PASSES)]
         nc.gpsimd.memset(c_sc[1][:].bitcast(I32), 0)
-        moving = {}
-        for name in ("pw", "ds"):
-            moving[name] = (tile(name + "_codes", [P, 2 * N], U32), tile(name + "_scales", [P, 2 * N], U8))
+
+        pw_mx = (tile("pw_codes", [P, 2 * N], U32), tile("pw_scales", [P, 2 * N], U8))
+        ds_mx = (tile("ds_codes", [P, 2 * N], U32), tile("ds_scales", [P, 2 * N], U8))
+
         windows = [tile("window%d" % w, [P, T], F32) for w in range(WINDOWS)]
+        middle = T // 2
         nc.gpsimd.memset(windows[0][:], 0.0)
-        nc.vector.memset(windows[1][:, 0 : T // 2 - 1], 0.0)
-        nc.vector.memset(windows[1][:, T // 2 - 1 : T], 0.0)
-        nc.vector.memset(windows[2][:, 0 : T // 2 - 1], 0.0)
-        nc.vector.memset(windows[2][:, T // 2 - 1 : T // 2], 0.0)
-        nc.gpsimd.memset(windows[2][:, T // 2 : T], 0.0)
+        nc.vector.memset(windows[1][:, 0 : middle - 1], 0.0)
+        nc.vector.memset(windows[1][:, middle - 1 : T], 0.0)
+        nc.vector.memset(windows[2][:, 0 : middle - 1], 0.0)
+        nc.vector.memset(windows[2][:, middle - 1 : middle], 0.0)
+        nc.gpsimd.memset(windows[2][:, middle:T], 0.0)
         neg_gate = tile("neg_gate", [P, 2 * PACK - 1], F32)
         nc.gpsimd.tensor_scalar(neg_gate[:], gate[:], -1.0, 0.0, MULT, ADD)
 
         word_pairs = tile("word_pairs", [P, N], U32)
-        if HEAD != "back":
-            nc.vector.tensor_copy(c_sc[0][:], pool_scales[:].bitcast(U8).indirect(offsets[:]))
         nc.vector.tensor_copy(word_pairs[:], pool_words[:].bitcast(U32).indirect(offsets[:]))
-        if HEAD == "back":
-            nc.vector.tensor_copy(c_sc[0][:], pool_scales[:].bitcast(U8).indirect(offsets[:]))
-        c_codes = tile("c_codes", [P, PASSES * 2 * N], U8)
-        for part_o in ([slice(0, 1), slice(1, 2)] if SPLIT_TWICE else [slice(0, 2)]):
-            nc.vector.tensor_copy(
-                c_codes[:].bitcast(U16).rearrange("p (o n) -> p o n", o=PASSES)[:, part_o],
-                word_pairs[:].bitcast(U16).rearrange("p (n o) -> p o n", o=PASSES)[:, part_o],
-            )
+        nc.vector.tensor_copy(c_sc[0][:], pool_scales[:].bitcast(U8).indirect(offsets[:]))
+        c_codes = tile("c_codes", [P, PASSES * 2 * N], U8, place_of="pool_scales")
+        nc.vector.tensor_copy(
+            c_codes[:].bitcast(U16).rearrange("p (o n) -> p o n", o=PASSES),
+            word_pairs[:].bitcast(U16).rearrange("p (n o) -> p o n", o=PASSES),
+        )
 
-        def load_pieces(name, src, pieces):
-            loaded = []
+        def load_passes(name, src):
+            raws = []
             for o in range(PASSES):
-                g0 = 0
-                loaded.append([])
-                for h, (groups, share) in enumerate(pieces[o]):
-                    key = "%s%d_%d" % (name, o, h)
-                    if key == SHIFT_BEFORE:
-                        (nc.scalar if SHIFT_ON_SCALAR else nc.sync).dma_start(out=c_sc[1][0 : P - 16, :].bitcast(I32), in_=c_sc[0][16:P, :].bitcast(I32))
-                    raw = tile(key, [P, PACK, 8 * groups], F32)
-                    rows = src[0, o * K_PASS : (o + 1) * K_PASS, 8 * g0 : 8 * (g0 + groups)]
-                    nc.sync.dma_start(out=raw[:], in_=rows.rearrange("(p j) w -> p j w", j=PACK))
-                    loaded[o].append((raw, g0, groups, share))
-                    g0 += groups
-            return loaded
+                raw = tile("%s%d" % (name, o), [P, PACK, R], F32)
+                rows = src[0, o * K_PASS : (o + 1) * K_PASS, :]
+                nc.sync.dma_start(out=raw[:], in_=rows.rearrange("(p j) w -> p j w", j=PACK))
+                raws.append(raw)
+            return raws
 
-        def load_queries(name, rows):
-            raw = tile(name, [P, PACK, rows.shape[1]], F32)
-            if rows.shape[1] <= BY_PARITY:
-                for b in range(2):
-                    nc.sync.dma_start(out=raw[b:P:2], in_=rows.rearrange("(g t b) w -> b g t w", t=PACK, b=2)[b])
-            else:
-                for t in range(PACK):
-                    nc.sync.dma_start(out=raw[:, t, :], in_=rows.rearrange("(g t b) w -> t g b w", t=PACK, b=2)[t])
+        def load_queries(name, src, features):
+            raw = tile(name, [P, PACK, features.stop - features.start], F32)
+            for t in range(PACK):
+                nc.sync.dma_start(
+                    out=raw[:, t, :], in_=src[0, :, features].rearrange("(g t b) w -> t g b w", t=PACK, b=2)[t]
+                )
             return raw
 
-        q_raw = load_pieces("q_raw", qT, Q_PIECES)
-        do_raw = load_pieces("do_raw", doT, DO_PIECES)
-        loaded = {"dom": [], "qm": []}
-        for name, width in ROW_LOADS:
-            d0 = sum(w for a, w, x in loaded[name])
-            src = {"dom": dom, "qm": qm}[name]
-            loaded[name].append((d0, width, load_queries("%s_raw%d" % (name, len(loaded[name])), src[0, :, d0 : d0 + width])))
+        q_raw = load_passes("q_raw", qT)
+        nc.sync.dma_start(out=c_sc[1][0 : P - PLANE_SHIFT, :].bitcast(I32), in_=c_sc[0][PLANE_SHIFT:P, :].bitcast(I32))
+        do_raw = load_passes("do_raw", doT)
+        dom_raw, qm_raw = [], []
+        for k, features in enumerate((slice(0, FIRST_LOAD), slice(FIRST_LOAD, D))):
+            dom_raw.append(load_queries("dom_raw%d" % k, dom, features))
+            qm_raw.append(load_queries("qm_raw%d" % k, qm, features))
 
-        def steps_of(name):
-            cut, d0 = [], 0
-            for step in STEPS:
-                at, width, raw = [x for x in loaded[name] if x[0] <= d0 and d0 + step <= x[0] + x[1]][0]
-                cut.append(raw[:, :, d0 - at : d0 - at + step])
-                d0 += step
-            return cut
+        def loaded(raws, first, width):
+            if first < FIRST_LOAD:
+                return raws[0][:, :, first : first + width]
+            return raws[1][:, :, first - FIRST_LOAD : first - FIRST_LOAD + width]
 
-        dom_raw, qm_raw = steps_of("dom"), steps_of("qm")
+        def mx_tiles(name, words):
+            return tile(name + "_codes", [P, words], U32), tile(name + "_scales", [P, words], U8)
 
-        def quantize(name, grouped, fmt, pieces=1):
-            words = grouped.shape[1] // PACK
-            if name in ("q1", "do1"):
-                codes, scales = [x[:, 0:N] for x in moving[{"q1": "pw", "do1": "ds"}[name]]]
-            else:
-                codes = tile(name + "_codes", [P, words], U32)
-                scales = tile(name + "_scales", [P, words], U8)
-            step = words // pieces
-            for w0 in range(0, words, step):
-                nc.vector.quantize_mx(
-                    out=codes[:, w0 : w0 + step].bitcast(fmt),
-                    scales=scales[:, w0 : w0 + step],
-                    in_=grouped[:, PACK * w0 : PACK * (w0 + step)],
-                )
-            return codes, scales
-
-        def group_queries(name, pieces):
-            grouped = tile(name, [P, PACK * R], BF16)
-            dst = grouped[:].rearrange("p (t g b j) -> p g t j b", t=PACK, b=2, j=PACK)
-            for raw, g0, groups, share in pieces:
-                src = raw[:].rearrange("p j (g t b) -> p g t j b", t=PACK, b=2)
-                for ts, part_share in ([(slice(0, PACK), share)] if isinstance(share, int) else [(slice(0, 2), share[0]), (slice(2, 4), share[1])]):
-                    if part_share > 0:
-                        nc.vector.tensor_copy(dst[:, g0 : g0 + part_share, ts], src[:, 0:part_share, ts])
-                    if part_share < groups:
-                        nc.scalar.copy(dst[:, g0 + part_share : g0 + groups, ts], src[:, part_share:groups, ts])
-            return grouped[:]
-
-        def words_view(grouped):
-            return grouped.rearrange("p (c i t) -> p c t i", i=4, t=PACK)
-
-        def rows_view(rows):
-            return rows.rearrange("p t (c i) -> p c t i", i=4)
-
-        def score_pass(banks, operand, fmt, o):
+        def quantize(operand, fmt, first_word, values):
             codes, scales = operand
+            words = slice(first_word, first_word + values.shape[1] // PACK)
+            nc.vector.quantize_mx(out=codes[:, words].bitcast(fmt), scales=scales[:, words], in_=values)
+
+        def score_pass(name, raw, o, groups_on_vector, operand, fmt, banks):
+            values = tile(name, [P, PACK * R], BF16)
+            dst = values[:].rearrange("p (t g b j) -> p g t j b", t=PACK, b=2, j=PACK)
+            src = raw[:].rearrange("p j (g t b) -> p g t j b", t=PACK, b=2)
+            for pair in (slice(0, 2), slice(2, PACK)):
+                nc.vector.tensor_copy(dst[:, 0:groups_on_vector, pair], src[:, 0:groups_on_vector, pair])
+                if groups_on_vector < GROUPS:
+                    nc.scalar.copy(dst[:, groups_on_vector:GROUPS, pair], src[:, groups_on_vector:GROUPS, pair])
+            codes, scales = operand or mx_tiles(name, R)
             for t in range(PACK):
-                cols = slice(t * P, (t + 1) * P)
+                quantize((codes, scales), fmt, t * P, values[:, t * K_PASS : (t + 1) * K_PASS])
+            for t in range(PACK):
                 nc.tensor.matmul_mx(
                     out=banks[t][:],
-                    lhsT=codes[:, cols].bitcast(fmt),
-                    lhsT_scale=scales[:, cols],
+                    lhsT=codes[:, t * P : (t + 1) * P].bitcast(fmt),
+                    lhsT_scale=scales[:, t * P : (t + 1) * P],
                     rhs=c_codes[:, o * 2 * N : (o + 1) * 2 * N].bitcast(E2M1),
                     rhs_scale=c_sc[o][:],
                     start=(o == 0),
@@ -208,164 +160,100 @@ def tile_attend_gat_sig_c_kernel(tc, qT, c_words, c_scales, doT, rw, qm, dom, of
 
         a_banks = [bank(t, "a%d" % t) for t in range(PACK)]
         dp_banks = [bank(PACK + t, "dp%d" % t) for t in range(PACK)]
-        for o in range(PASSES):
-            q_mx = quantize("q%d" % o, group_queries("q_bf%d" % o, q_raw[o]), E4M3, PACK)
-            score_pass(a_banks, q_mx, E4M3, o)
-        prob = [tile("prob%d" % h, [P, PACK, HALF], F32) for h in range(2)] if SIG_SPLIT else None
-        if SIG_SPLIT:
-            for h in range(2):
-                for t in range(PACK):
-                    nc.scalar.activation(out=prob[h][:, t, :], in_=a_banks[t][:, h * HALF : (h + 1) * HALF], func=SIGMOID)
-        else:
-            whole = tile("prob0", [P, PACK, N], F32)
-            prob = [whole[:, :, h * HALF : (h + 1) * HALF] for h in range(2)]
+        for o, operand in enumerate((None, pw_mx)):
+            score_pass("q_bf%d" % o, q_raw[o], o, Q_GROUPS_ON_VECTOR, operand, E4M3, a_banks)
+        prob = tile("prob", [P, PACK, N], F32)
+        for t in range(PACK):
+            nc.scalar.activation(out=prob[:, t, :], in_=a_banks[t][:], func=SIGMOID)
+        for o, operand in enumerate((None, ds_mx)):
+            score_pass("do_bf%d" % o, do_raw[o], o, GROUPS, operand, E5M2, dp_banks)
+
+        def words_view(values):
+            return values.rearrange("p (c i t) -> p c t i", i=RUN, t=PACK)
+
+        def rows_view(rows):
+            return rows.rearrange("p t (c i) -> p c t i", i=RUN)
+
+        halves = (slice(0, HALF), slice(HALF, N))
+        neg_pw, pw_bf = [], []
+        for h, slots in enumerate(halves):
+            rows = tile("neg_pw%d" % h, [P, PACK, HALF], F32, place_of=(None, "do_raw1")[h])
             for t in range(PACK):
-                nc.scalar.activation(out=whole[:, t, :], in_=a_banks[t][:], func=SIGMOID)
-        for o in range(PASSES):
-            do_mx = quantize("do%d" % o, group_queries("do_bf%d" % o, do_raw[o]), E5M2, PACK)
-            score_pass(dp_banks, do_mx, E5M2, o)
+                minus_gate = neg_gate[:, 2 * t : 2 * t + 1]
+                if h == 0 and t >= PW_ROW_ON_VECTOR_FROM:
+                    nc.vector.tensor_scalar(rows[:, t, :], prob[:, t, slots], minus_gate, None, MULT)
+                else:
+                    nc.scalar.activation(out=rows[:, t, :], in_=prob[:, t, slots], func=COPY, scale=minus_gate)
+            values = tile("pw_bf%d" % h, [P, PACK * HALF], BF16)
+            nc.scalar.activation(out=words_view(values[:]), in_=rows_view(rows[:]), func=COPY, scale=-1.0)
+            neg_pw.append(rows)
+            pw_bf.append(values)
 
-        def minus_gate(t):
-            return neg_gate[:, 2 * t : 2 * t + 1]
-
-        homes = {}
-        neg_pw, neg_slope, pw_bf, part, ds_bf, cuts = {}, {}, {}, {}, {}, {}
-        for h in range(2):
-            cuts[h], at = [], 0
-            for width, kind in RANGES[h]:
-                cuts[h].append((slice(at, at + width), kind))
-                at += width
-
-        def pw_rows(h):
-            neg_pw[h] = tile("neg_pw%d" % h, [P, PACK, HALF], F32)
+        def ds_half(h):
+            rows = tile("part%d" % h, [P, PACK, HALF], F32)
             for t in range(PACK):
-                if t in PW_ROWS_ON_VECTOR[h]:
-                    nc.vector.tensor_scalar(neg_pw[h][:, t, :], prob[h][:, t, :], minus_gate(t), None, MULT)
-                else:
-                    nc.scalar.activation(out=neg_pw[h][:, t, :], in_=prob[h][:, t, :], func=COPY, scale=minus_gate(t))
-
-        def slopes(h):
-            width = sum(w for w, kind in RANGES[h] if kind != "F")
-            if width:
-                neg_slope[h] = tile("neg_slope%d" % h, [P, PACK, width], F32)
-                for t0 in range(0, PACK, SLOPE_ROWS):
-                    rows = prob[h][:, t0 : t0 + SLOPE_ROWS, 0:width]
-                    nc.vector.scalar_tensor_tensor(neg_slope[h][:, t0 : t0 + SLOPE_ROWS, :], rows, 1.0, rows, SUB, MULT)
-
-        def pw_weave(h):
-            share = PW_SHARE[h]
-            if share == "G":
-                homes["first"] = tile("first", [P, 2048], BF16)
-                pw_bf[h] = homes["first"][:, 1024:2048]
-                nc.gpsimd.tensor_scalar(
-                    pw_bf[h].rearrange("p (n t) -> p n t", t=PACK), neg_pw[h][:].rearrange("p t n -> p n t"), -1.0, 0.0, MULT, ADD
+                nc.vector.scalar_tensor_tensor(
+                    rows[:, t, :], prob[:, t, halves[h]], 1.0, dp_banks[t][:, halves[h]], SUB, MULT
                 )
-                return
-            pw_bf[h] = tile("pw_bf%d" % h, [P, PACK * HALF], BF16)[:]
-            dst, src = words_view(pw_bf[h]), rows_view(neg_pw[h][:])
-            if share:
-                nc.vector.tensor_scalar(dst[:, 0:share], src[:, 0:share], -1.0, None, MULT)
-            if share < HALF // 4:
-                nc.scalar.activation(out=dst[:, share:], in_=src[:, share:], func=COPY, scale=-1.0)
+            values = tile("ds_bf%d" % h, [P, PACK * HALF], BF16)
+            nc.vector.tensor_tensor(words_view(values[:]), rows_view(rows[:]), rows_view(neg_pw[h][:]), MULT)
+            return values
 
-        def products(h):
-            part[h] = tile("part%d" % h, [P, PACK, HALF], F32)
-            for cols, kind in cuts[h]:
-                for t in range(PACK):
-                    dp = dp_banks[t][:, h * HALF + cols.start : h * HALF + cols.stop]
-                    if kind == "F":
-                        nc.vector.scalar_tensor_tensor(part[h][:, t, cols], prob[h][:, t, cols], 1.0, dp, SUB, MULT)
-                    else:
-                        nc.vector.scalar_tensor_tensor(part[h][:, t, cols], dp, minus_gate(t), neg_slope[h][:, t, cols], MULT, MULT)
+        dom_places = {1: "prob", 2: "early_grad", 3: "qm_bf2"}
+        stationary = []
+        step_of_block = [s for s, width in enumerate(STEP_WIDTHS) for block in range(width // P)]
 
-        def ds_weave(h):
-            ds_bf[h] = tile("ds_bf%d" % h, [P, PACK * HALF], BF16)[:]
-            for cols, kind in cuts[h]:
-                cs = slice(cols.start // 4, cols.stop // 4)
-                dst, src = words_view(ds_bf[h])[:, cs], rows_view(part[h][:])[:, cs]
-                if kind == "F":
-                    nc.vector.tensor_tensor(dst, src, rows_view(neg_pw[h][:])[:, cs], MULT)
-                elif kind == "V":
-                    nc.vector.tensor_copy(dst, src)
-                else:
-                    nc.scalar.copy(dst, src)
+        def prepare_step(s):
+            first, width = sum(STEP_WIDTHS[:s]), STEP_WIDTHS[s]
+            dom_bf = tile("dom_bf%d" % s, [P, PACK * width], BF16, place_of=dom_places.get(s))
+            nc.scalar.copy(words_view(dom_bf[:]), rows_view(loaded(dom_raw, first, width)))
+            qm_bf = tile("qm_bf%d" % s, [P, PACK * width], BF16)
+            nc.scalar.copy(words_view(qm_bf[:]), rows_view(loaded(qm_raw, first, width)))
+            dom_mx = mx_tiles("dom%d" % s, width)
+            quantize(dom_mx, E5M2, 0, dom_bf[:])
+            qm_mx = mx_tiles("qm%d" % s, width)
+            quantize(qm_mx, E4M3, 0, qm_bf[:])
+            for w0 in range(0, width, P):
+                stationary.append([[x[:, w0 : w0 + P] for x in operand] for operand in (dom_mx, qm_mx)])
 
-        def quantize_half(name, grouped, fmt, h):
-            codes, scales = moving[name]
-            cols = slice(N + h * HALF, N + (h + 1) * HALF)
-            nc.vector.quantize_mx(out=codes[:, cols].bitcast(fmt), scales=scales[:, cols], in_=grouped)
+        def gradient(block, acc, first_word):
+            words = slice(first_word, first_word + N)
+            (dom_codes, dom_scales), (qm_codes, qm_scales) = stationary[block]
+            nc.tensor.matmul_mx(
+                out=acc[:], lhsT=dom_codes.bitcast(E5M2), lhsT_scale=dom_scales,
+                rhs=pw_mx[0][:, words].bitcast(E4M3), rhs_scale=pw_mx[1][:, words], start=True, stop=False,
+            )
+            nc.tensor.matmul_mx(
+                out=acc[:], lhsT=qm_codes.bitcast(E4M3), lhsT_scale=qm_scales,
+                rhs=ds_mx[0][:, words].bitcast(E5M2), rhs_scale=ds_mx[1][:, words], start=False, stop=True,
+            )
 
-        def query_operands(c):
-            made = []
-            for name, raw, fmt in (("dom", dom_raw[c], E5M2), ("qm", qm_raw[c], E4M3)):
-                key = "%s_bf%d" % (name, c)
-                width = PACK * raw.shape[2]
-                if key in SHARED:
-                    home, at, size = SHARED[key]
-                    if home not in homes:
-                        homes[home] = tile(home, [P, size], BF16)
-                    grouped = homes[home][:, at : at + width]
-                else:
-                    grouped = tile(key, [P, width], BF16)[:]
-                if key in ON_GPSIMD:
-                    nc.gpsimd.tensor_scalar(
-                        grouped.rearrange("p (n t) -> p n t", t=PACK), raw.rearrange("p t n -> p n t"), 1.0, 0.0, MULT, ADD
-                    )
-                else:
-                    nc.scalar.copy(words_view(grouped), rows_view(raw))
-                made.append((name, grouped, fmt))
-            return [quantize("%s%d" % (name, c), grouped, fmt) for name, grouped, fmt in made]
+        def scatter(block, values, slots):
+            columns = offsets[:, slots.start // LIST_BAND : slots.stop // LIST_BAND]
+            nc.vector.tensor_copy(windows[block % WINDOWS][:].indirect(columns), values)
 
-        operands, stationary = {}, {}
+        prepare_step(0)
+        quantize(pw_mx, E4M3, N, pw_bf[0][:])
+        quantize(ds_mx, E5M2, N, ds_half(0)[:])
+        early_acc = bank(PACK - 1, "early")
+        gradient(0, early_acc, HALF)
+        early_grad = tile("early_grad", [P, HALF], F32)
+        nc.scalar.copy(early_grad[:], early_acc[:, HALF:N])
+        prepare_step(1)
+        ds_second = ds_half(1)
+        quantize(pw_mx, E4M3, N + HALF, pw_bf[1][:])
+        quantize(ds_mx, E5M2, N + HALF, ds_second[:])
+        scatter(0, early_grad[:], halves[0])
 
-        def prepare(c):
-            if c not in operands and c < len(STEPS):
-                operands[c] = query_operands(c)
-                first = sum(STEPS[:c]) // P
-                for k in range(STEPS[c] // P):
-                    stationary[first + k] = [(codes[:, k * P : (k + 1) * P], scales[:, k * P : (k + 1) * P]) for codes, scales in operands[c]]
-
-        def gradient(b, acc, at):
-            cols = slice(at, at + N)
-            (dom_codes, dom_scales), (qm_codes, qm_scales) = stationary[b]
-            passes = [
-                (dom_codes.bitcast(E5M2), dom_scales, moving["pw"][0][:, cols].bitcast(E4M3), moving["pw"][1][:, cols]),
-                (qm_codes.bitcast(E4M3), qm_scales, moving["ds"][0][:, cols].bitcast(E5M2), moving["ds"][1][:, cols]),
-            ]
-            for k, (lhs, lhs_scale, rhs, rhs_scale) in enumerate(passes):
-                nc.tensor.matmul_mx(
-                    out=acc[:], lhsT=lhs, lhsT_scale=lhs_scale, rhs=rhs, rhs_scale=rhs_scale, start=(k == 0), stop=(k == 1)
-                )
-
-        def scatter(b, values, slots):
-            nc.vector.tensor_copy(windows[b % WINDOWS][:].indirect(offsets[:, slots.start // 16 : slots.stop // 16]), values)
-
-        ahead = {}
-
-        def early_product(b):
-            prepare([c for c in range(len(STEPS)) if sum(STEPS[: c + 1]) > b * P][0])
-            acc = bank(PACK - 1 - b, "early%d" % b)
-            gradient(b, acc, HALF)
-            ahead[b] = tile("early_sb%d" % b, [P, HALF], F32)
-            (nc.vector.tensor_copy if FIRST_ON_VECTOR and b == 0 else nc.scalar.copy)(ahead[b][:], acc[:, HALF:N])
-
-        steps = {
-            "r": pw_rows, "s": slopes, "w": pw_weave, "p": products, "d": ds_weave, "o": prepare, "e": early_product,
-            "P": lambda h: quantize_half("pw", pw_bf[h], E4M3, h),
-            "D": lambda h: quantize_half("ds", ds_bf[h], E5M2, h),
-            "x": lambda b: scatter(b, ahead[b][:], slice(0, HALF)),
-        }
-        for step in TEXT.split():
-            steps[step[0]](int(step[1]))
-
-        for b in range(D // P):
-            c = [c for c in range(len(STEPS)) if sum(STEPS[: c + 1]) > b * P][0]
-            for k in range(c, c + LOOK + 1):
-                prepare(k)
-            acc = bank(b, "grad%d" % b)
-            gradient(b, acc, N)
-            slots = slice(HALF, N) if b in ahead else slice(0, N)
-            grad = tile("grad_sb%d" % b, [P, slots.stop - slots.start], F32)
+        prepared = 2
+        for block in range(D // P):
+            if prepared == step_of_block[block] + 1 and prepared < len(STEP_WIDTHS):
+                prepare_step(prepared)
+                prepared += 1
+            acc = bank(block, "grad%d" % block)
+            gradient(block, acc, N)
+            slots = halves[1] if block == 0 else slice(0, N)
+            grad = tile("grad_sb%d" % block, [P, slots.stop - slots.start], F32)
             nc.scalar.copy(grad[:], acc[:, slots])
-            scatter(b, grad[:], slots)
-            nc.sync.dma_start(out=out[b * P : (b + 1) * P, :], in_=windows[b % WINDOWS][:])
+            scatter(block, grad[:], slots)
+            nc.sync.dma_start(out=out[block * P : (block + 1) * P, :], in_=windows[block % WINDOWS][:])

@@ -79,13 +79,8 @@ def tile_attend_gat_sig_c_kernel(tc, qT, c_words, c_scales, doT, rw, qm, dom, of
         ds_mx = (tile("ds_codes", [P, 2 * N], U32), tile("ds_scales", [P, 2 * N], U8))
 
         windows = [tile("window%d" % w, [P, T], F32) for w in range(WINDOWS)]
-        middle = T // 2
-        nc.gpsimd.memset(windows[0][:], 0.0)
-        nc.vector.memset(windows[1][:, 0 : middle - 1], 0.0)
-        nc.vector.memset(windows[1][:, middle - 1 : T], 0.0)
-        nc.vector.memset(windows[2][:, 0 : middle - 1], 0.0)
-        nc.vector.memset(windows[2][:, middle - 1 : middle], 0.0)
-        nc.gpsimd.memset(windows[2][:, middle:T], 0.0)
+        for window in windows:
+            nc.vector.memset(window[:], 0.0)
         neg_gate = tile("neg_gate", [P, 2 * PACK - 1], F32)
         nc.gpsimd.tensor_scalar(neg_gate[:], gate[:], -1.0, 0.0, MULT, ADD)
 

@@ -32,8 +32,9 @@ RUN = 4
 WINDOWS = 3
 
 Q_GROUPS_ON_VECTOR = 44
-PW_ROW_ON_VECTOR_FROM = 2
-FIRST_LOAD = 384
+FIRST_GROUPS_ON_VECTOR = 32
+PW_ROW_ON_VECTOR_FROM = 4
+LOAD_WIDTH = 512
 STEP_WIDTHS = (P, P, P, P, 2 * P, 2 * P)
 
 
@@ -41,10 +42,14 @@ def tile_attend_gat_sig_c_kernel(tc, qT, c_words, c_scales, doT, rw, qm, dom, of
     nc = tc.nc
     with ExitStack() as ctx:
         sb = ctx.enter_context(tc.tile_pool(name="sb", bufs=1))
+        shared = ctx.enter_context(tc.tile_pool(name="shared", bufs=1))
         ps = ctx.enter_context(tc.psum_pool(name="ps", bufs=1))
 
         def tile(name, shape, dtype, place_of=None):
             return sb.tile(shape, dtype, name=name, tag=place_of or name, align_bytes=64)
+
+        def placed(name, shape, dtype, offset):
+            return shared.tile(shape, dtype, name=name, offset=offset, align_bytes=64)
 
         def bank(index, name):
             return ps.tile([P, N], F32, name=name, tag="bank%d" % index)
@@ -93,14 +98,11 @@ def tile_attend_gat_sig_c_kernel(tc, qT, c_words, c_scales, doT, rw, qm, dom, of
             word_pairs[:].bitcast(U16).rearrange("p (n o) -> p o n", o=PASSES),
         )
 
-        def load_passes(name, src):
-            raws = []
-            for o in range(PASSES):
-                raw = tile("%s%d" % (name, o), [P, PACK, R], F32)
-                rows = src[0, o * K_PASS : (o + 1) * K_PASS, :]
-                nc.sync.dma_start(out=raw[:], in_=rows.rearrange("(p j) w -> p j w", j=PACK))
-                raws.append(raw)
-            return raws
+        def load_pass(name, src, o):
+            raw = tile("%s%d" % (name, o), [P, PACK, R], F32)
+            rows = src[0, o * K_PASS : (o + 1) * K_PASS, :]
+            nc.sync.dma_start(out=raw[:], in_=rows.rearrange("(p j) w -> p j w", j=PACK))
+            return raw
 
         def load_queries(name, src, features):
             raw = tile(name, [P, PACK, features.stop - features.start], F32)
@@ -110,18 +112,18 @@ def tile_attend_gat_sig_c_kernel(tc, qT, c_words, c_scales, doT, rw, qm, dom, of
                 )
             return raw
 
-        q_raw = load_passes("q_raw", qT)
+        q_raw = [load_pass("q_raw", qT, o) for o in range(PASSES)]
+        do_raw = [load_pass("do_raw", doT, 0)]
         nc.sync.dma_start(out=c_sc[1][0 : P - PLANE_SHIFT, :].bitcast(I32), in_=c_sc[0][PLANE_SHIFT:P, :].bitcast(I32))
-        do_raw = load_passes("do_raw", doT)
+        do_raw.append(load_pass("do_raw", doT, 1))
         dom_raw, qm_raw = [], []
-        for k, features in enumerate((slice(0, FIRST_LOAD), slice(FIRST_LOAD, D))):
+        for k in range(D // LOAD_WIDTH):
+            features = slice(k * LOAD_WIDTH, (k + 1) * LOAD_WIDTH)
             dom_raw.append(load_queries("dom_raw%d" % k, dom, features))
             qm_raw.append(load_queries("qm_raw%d" % k, qm, features))
 
         def loaded(raws, first, width):
-            if first < FIRST_LOAD:
-                return raws[0][:, :, first : first + width]
-            return raws[1][:, :, first - FIRST_LOAD : first - FIRST_LOAD + width]
+            return raws[first // LOAD_WIDTH][:, :, first % LOAD_WIDTH : first % LOAD_WIDTH + width]
 
         def mx_tiles(name, words):
             return tile(name + "_codes", [P, words], U32), tile(name + "_scales", [P, words], U8)
@@ -156,12 +158,12 @@ def tile_attend_gat_sig_c_kernel(tc, qT, c_words, c_scales, doT, rw, qm, dom, of
         a_banks = [bank(t, "a%d" % t) for t in range(PACK)]
         dp_banks = [bank(PACK + t, "dp%d" % t) for t in range(PACK)]
         for o, operand in enumerate((None, pw_mx)):
-            score_pass("q_bf%d" % o, q_raw[o], o, Q_GROUPS_ON_VECTOR, operand, E4M3, a_banks)
+            score_pass("q_bf%d" % o, q_raw[o], o, (FIRST_GROUPS_ON_VECTOR, Q_GROUPS_ON_VECTOR)[o], operand, E4M3, a_banks)
+        for o, operand in enumerate((None, ds_mx)):
+            score_pass("do_bf%d" % o, do_raw[o], o, (Q_GROUPS_ON_VECTOR, GROUPS)[o], operand, E5M2, dp_banks)
         prob = tile("prob", [P, PACK, N], F32)
         for t in range(PACK):
             nc.scalar.activation(out=prob[:, t, :], in_=a_banks[t][:], func=SIGMOID)
-        for o, operand in enumerate((None, ds_mx)):
-            score_pass("do_bf%d" % o, do_raw[o], o, GROUPS, operand, E5M2, dp_banks)
 
         def words_view(values):
             return values.rearrange("p (c i t) -> p c t i", i=RUN, t=PACK)
@@ -171,6 +173,12 @@ def tile_attend_gat_sig_c_kernel(tc, qT, c_words, c_scales, doT, rw, qm, dom, of
 
         halves = (slice(0, HALF), slice(HALF, N))
         neg_pw, pw_bf = [], []
+
+        def pw_words(h, place_of):
+            values = tile("pw_bf%d" % h, [P, PACK * HALF], BF16, place_of=place_of)
+            nc.scalar.activation(out=words_view(values[:]), in_=rows_view(neg_pw[h][:]), func=COPY, scale=-1.0)
+            return values
+
         for h, slots in enumerate(halves):
             rows = tile("neg_pw%d" % h, [P, PACK, HALF], F32, place_of=(None, "do_raw1")[h])
             for t in range(PACK):
@@ -179,35 +187,40 @@ def tile_attend_gat_sig_c_kernel(tc, qT, c_words, c_scales, doT, rw, qm, dom, of
                     nc.vector.tensor_scalar(rows[:, t, :], prob[:, t, slots], minus_gate, None, MULT)
                 else:
                     nc.scalar.activation(out=rows[:, t, :], in_=prob[:, t, slots], func=COPY, scale=minus_gate)
-            values = tile("pw_bf%d" % h, [P, PACK * HALF], BF16)
-            nc.scalar.activation(out=words_view(values[:]), in_=rows_view(rows[:]), func=COPY, scale=-1.0)
             neg_pw.append(rows)
-            pw_bf.append(values)
+            if h == 0:
+                pw_bf.append(pw_words(0, None))
 
-        def ds_half(h):
-            rows = tile("part%d" % h, [P, PACK, HALF], F32)
+        def ds_part(h):
+            rows = placed("part%d" % h, [P, PACK, HALF], F32, h * 4 * PACK * HALF)
             for t in range(PACK):
                 nc.vector.scalar_tensor_tensor(
                     rows[:, t, :], prob[:, t, halves[h]], 1.0, dp_banks[t][:, halves[h]], SUB, MULT
                 )
-            values = tile("ds_bf%d" % h, [P, PACK * HALF], BF16)
-            nc.vector.tensor_tensor(words_view(values[:]), rows_view(rows[:]), rows_view(neg_pw[h][:]), MULT)
-            return values
+            return rows
 
-        dom_places = {1: "prob", 2: "early_grad", 3: "qm_bf2"}
+        def ds_words(engine, values, h, first, count):
+            slots = slice(first, first + count)
+            engine.tensor_tensor(
+                words_view(values), rows_view(parts[h][:, :, slots]), rows_view(neg_pw[h][:, :, slots]), MULT
+            )
+
+        step_places = {2: "qm0_codes", 3: "qm1_codes", 4: "qm2_codes", 5: "qm3_codes"}
+        grad_places = {2: "qm_raw0", 4: "qm_raw1"}
         stationary = []
         step_of_block = [s for s, width in enumerate(STEP_WIDTHS) for block in range(width // P)]
 
-        def prepare_step(s):
+        def prepare_step(s, values=None):
             first, width = sum(STEP_WIDTHS[:s]), STEP_WIDTHS[s]
-            dom_bf = tile("dom_bf%d" % s, [P, PACK * width], BF16, place_of=dom_places.get(s))
-            nc.scalar.copy(words_view(dom_bf[:]), rows_view(loaded(dom_raw, first, width)))
-            qm_bf = tile("qm_bf%d" % s, [P, PACK * width], BF16)
-            nc.scalar.copy(words_view(qm_bf[:]), rows_view(loaded(qm_raw, first, width)))
+            if values is None:
+                values = tile("step_bf%d" % s, [P, 2 * PACK * width], BF16, place_of=step_places.get(s))
+            dom_bf, qm_bf = values[:, 0 : PACK * width], values[:, PACK * width : 2 * PACK * width]
+            nc.scalar.copy(words_view(dom_bf), rows_view(loaded(dom_raw, first, width)))
+            nc.scalar.copy(words_view(qm_bf), rows_view(loaded(qm_raw, first, width)))
             dom_mx = mx_tiles("dom%d" % s, width)
-            quantize(dom_mx, E5M2, 0, dom_bf[:])
+            quantize(dom_mx, E5M2, 0, dom_bf)
             qm_mx = mx_tiles("qm%d" % s, width)
-            quantize(qm_mx, E4M3, 0, qm_bf[:])
+            quantize(qm_mx, E4M3, 0, qm_bf)
             for w0 in range(0, width, P):
                 stationary.append([[x[:, w0 : w0 + P] for x in operand] for operand in (dom_mx, qm_mx)])
 
@@ -227,18 +240,26 @@ def tile_attend_gat_sig_c_kernel(tc, qT, c_words, c_scales, doT, rw, qm, dom, of
             columns = offsets[:, slots.start // LIST_BAND : slots.stop // LIST_BAND]
             nc.vector.tensor_copy(windows[block % WINDOWS][:].indirect(columns), values)
 
-        prepare_step(0)
+        def early_product(block, grad):
+            acc = bank(PACK - 1 - block, "early%d" % block)
+            gradient(block, acc, HALF)
+            nc.scalar.copy(grad[:], acc[:, HALF:N])
+            return grad
+
+        parts = [ds_part(0), ds_part(1)]
+        ds_first = tile("ds_bf0", [P, PACK * HALF], BF16)
+        ds_words(nc.vector, ds_first[:], 0, 0, HALF)
         quantize(pw_mx, E4M3, N, pw_bf[0][:])
-        quantize(ds_mx, E5M2, N, ds_half(0)[:])
-        early_acc = bank(PACK - 1, "early")
-        gradient(0, early_acc, HALF)
-        early_grad = tile("early_grad", [P, HALF], F32)
-        nc.scalar.copy(early_grad[:], early_acc[:, HALF:N])
-        prepare_step(1)
-        ds_second = ds_half(1)
+        prepare_step(0)
+        quantize(ds_mx, E5M2, N, ds_first[:])
+        pw_bf.append(pw_words(1, "ds_bf0"))
+        ds_second = tile("ds_bf1", [P, PACK * HALF], BF16, place_of="step_bf0")
+        ds_words(nc.vector, ds_second[:], 1, 0, HALF)
+        early_grads = [early_product(0, placed("early_grad0", [P, HALF], F32, 4096))]
         quantize(pw_mx, E4M3, N + HALF, pw_bf[1][:])
         quantize(ds_mx, E5M2, N + HALF, ds_second[:])
-        scatter(0, early_grad[:], halves[0])
+        scatter(0, early_grads[0][:], halves[0])
+        prepare_step(1, placed("step_bf1", [P, 2 * PACK * P], BF16, 4096 + 1024))
 
         prepared = 2
         for block in range(D // P):
@@ -247,8 +268,8 @@ def tile_attend_gat_sig_c_kernel(tc, qT, c_words, c_scales, doT, rw, qm, dom, of
                 prepared += 1
             acc = bank(block, "grad%d" % block)
             gradient(block, acc, N)
-            slots = halves[1] if block == 0 else slice(0, N)
-            grad = tile("grad_sb%d" % block, [P, slots.stop - slots.start], F32)
+            slots = halves[1] if block < len(early_grads) else slice(0, N)
+            grad = tile("grad_sb%d" % block, [P, slots.stop - slots.start], F32, place_of=grad_places.get(block))
             nc.scalar.copy(grad[:], acc[:, slots])
             scatter(block, grad[:], slots)
             nc.sync.dma_start(out=out[block * P : (block + 1) * P, :], in_=windows[block % WINDOWS][:])

@@ -34,8 +34,9 @@ WINDOWS = 3
 Q_GROUPS_ON_VECTOR = 44
 FIRST_GROUPS_ON_VECTOR = 32
 PW_ROW_ON_VECTOR_FROM = 4
-LOAD_WIDTH = 512
-STEP_WIDTHS = (P, P, P, P, 2 * P, 2 * P)
+DOM_CUT, QM_CUT = 512, 640
+STRIPES = D // P
+AHEAD = 3
 
 
 def tile_attend_gat_sig_c_kernel(tc, qT, c_words, c_scales, doT, rw, qm, dom, offs, out):
@@ -80,8 +81,8 @@ def tile_attend_gat_sig_c_kernel(tc, qT, c_words, c_scales, doT, rw, qm, dom, of
         c_sc = [tile("c_sc%d" % o, [P, N], U8) for o in range(PASSES)]
         nc.gpsimd.memset(c_sc[1][:].bitcast(I32), 0)
 
-        pw_mx = (tile("pw_codes", [P, 2 * N], U32), tile("pw_scales", [P, 2 * N], U8))
-        ds_mx = (tile("ds_codes", [P, 2 * N], U32), tile("ds_scales", [P, 2 * N], U8))
+        pw_mx = (tile("pw_codes", [P, N], U32), tile("pw_scales", [P, N], U8))
+        ds_mx = (tile("ds_codes", [P, N], U32), tile("ds_scales", [P, N], U8))
 
         windows = [tile("window%d" % w, [P, T], F32) for w in range(WINDOWS)]
         for window in windows:
@@ -117,13 +118,14 @@ def tile_attend_gat_sig_c_kernel(tc, qT, c_words, c_scales, doT, rw, qm, dom, of
         nc.sync.dma_start(out=c_sc[1][0 : P - PLANE_SHIFT, :].bitcast(I32), in_=c_sc[0][PLANE_SHIFT:P, :].bitcast(I32))
         do_raw.append(load_pass("do_raw", doT, 1))
         dom_raw, qm_raw = [], []
-        for k in range(D // LOAD_WIDTH):
-            features = slice(k * LOAD_WIDTH, (k + 1) * LOAD_WIDTH)
-            dom_raw.append(load_queries("dom_raw%d" % k, dom, features))
-            qm_raw.append(load_queries("qm_raw%d" % k, qm, features))
+        for k in range(2):
+            for name, src, raws, cut in (("dom", dom, dom_raw, DOM_CUT), ("qm", qm, qm_raw, QM_CUT)):
+                features = (slice(0, cut), slice(cut, D))[k]
+                raws.append((features, load_queries("%s_raw%d" % (name, k), src, features)))
 
         def loaded(raws, first, width):
-            return raws[first // LOAD_WIDTH][:, :, first % LOAD_WIDTH : first % LOAD_WIDTH + width]
+            features, raw = raws[int(first >= raws[0][0].stop)]
+            return raw[:, :, first - features.start : first - features.start + width]
 
         def mx_tiles(name, words):
             return tile(name + "_codes", [P, words], U32), tile(name + "_scales", [P, words], U8)
@@ -157,9 +159,9 @@ def tile_attend_gat_sig_c_kernel(tc, qT, c_words, c_scales, doT, rw, qm, dom, of
 
         a_banks = [bank(t, "a%d" % t) for t in range(PACK)]
         dp_banks = [bank(PACK + t, "dp%d" % t) for t in range(PACK)]
-        for o, operand in enumerate((None, pw_mx)):
+        for o, operand in enumerate((None, None)):
             score_pass("q_bf%d" % o, q_raw[o], o, (FIRST_GROUPS_ON_VECTOR, Q_GROUPS_ON_VECTOR)[o], operand, E4M3, a_banks)
-        for o, operand in enumerate((None, ds_mx)):
+        for o, operand in enumerate((None, None)):
             score_pass("do_bf%d" % o, do_raw[o], o, (Q_GROUPS_ON_VECTOR, GROUPS)[o], operand, E5M2, dp_banks)
         prob = tile("prob", [P, PACK, N], F32)
         for t in range(PACK):
@@ -205,71 +207,83 @@ def tile_attend_gat_sig_c_kernel(tc, qT, c_words, c_scales, doT, rw, qm, dom, of
                 words_view(values), rows_view(parts[h][:, :, slots]), rows_view(neg_pw[h][:, :, slots]), MULT
             )
 
-        step_places = {2: "qm0_codes", 3: "qm1_codes", 4: "qm2_codes", 5: "qm3_codes"}
-        grad_places = {2: "qm_raw0", 4: "qm_raw1"}
-        stationary = []
-        step_of_block = [s for s, width in enumerate(STEP_WIDTHS) for block in range(width // P)]
+        def stripe_casts(engine, stripe, values):
+            dom_bf, qm_bf = values[:, 0 : PACK * P], values[:, PACK * P : 2 * PACK * P]
+            copy = nc.vector.tensor_copy if engine is nc.vector else nc.scalar.copy
+            copy(words_view(dom_bf), rows_view(loaded(dom_raw, stripe * P, P)))
+            copy(words_view(qm_bf), rows_view(loaded(qm_raw, stripe * P, P)))
+            return dom_bf, qm_bf
 
-        def prepare_step(s, values=None):
-            first, width = sum(STEP_WIDTHS[:s]), STEP_WIDTHS[s]
-            if values is None:
-                values = tile("step_bf%d" % s, [P, 2 * PACK * width], BF16, place_of=step_places.get(s))
-            dom_bf, qm_bf = values[:, 0 : PACK * width], values[:, PACK * width : 2 * PACK * width]
-            nc.scalar.copy(words_view(dom_bf), rows_view(loaded(dom_raw, first, width)))
-            nc.scalar.copy(words_view(qm_bf), rows_view(loaded(qm_raw, first, width)))
-            dom_mx = mx_tiles("dom%d" % s, width)
-            quantize(dom_mx, E5M2, 0, dom_bf)
-            qm_mx = mx_tiles("qm%d" % s, width)
-            quantize(qm_mx, E4M3, 0, qm_bf)
-            for w0 in range(0, width, P):
-                stationary.append([[x[:, w0 : w0 + P] for x in operand] for operand in (dom_mx, qm_mx)])
+        def stripe_codes(stripe, casts):
+            dom_mx = mx_tiles("dom%d" % stripe, P)
+            quantize(dom_mx, E5M2, 0, casts[0])
+            qm_mx = mx_tiles("qm%d" % stripe, P)
+            quantize(qm_mx, E4M3, 0, casts[1])
+            return dom_mx, qm_mx
 
-        def gradient(block, acc, first_word):
-            words = slice(first_word, first_word + N)
-            (dom_codes, dom_scales), (qm_codes, qm_scales) = stationary[block]
+        def gradient(operands, acc, slots):
+            (dom_codes, dom_scales), (qm_codes, qm_scales) = operands
             nc.tensor.matmul_mx(
-                out=acc[:], lhsT=dom_codes.bitcast(E5M2), lhsT_scale=dom_scales,
-                rhs=pw_mx[0][:, words].bitcast(E4M3), rhs_scale=pw_mx[1][:, words], start=True, stop=False,
+                out=acc, lhsT=dom_codes[:].bitcast(E5M2), lhsT_scale=dom_scales[:],
+                rhs=pw_mx[0][:, slots].bitcast(E4M3), rhs_scale=pw_mx[1][:, slots], start=True, stop=False,
             )
             nc.tensor.matmul_mx(
-                out=acc[:], lhsT=qm_codes.bitcast(E4M3), lhsT_scale=qm_scales,
-                rhs=ds_mx[0][:, words].bitcast(E5M2), rhs_scale=ds_mx[1][:, words], start=False, stop=True,
+                out=acc, lhsT=qm_codes[:].bitcast(E4M3), lhsT_scale=qm_scales[:],
+                rhs=ds_mx[0][:, slots].bitcast(E5M2), rhs_scale=ds_mx[1][:, slots], start=False, stop=True,
             )
 
-        def scatter(block, values, slots):
+        def window_at(stripe, slots):
             columns = offsets[:, slots.start // LIST_BAND : slots.stop // LIST_BAND]
-            nc.vector.tensor_copy(windows[block % WINDOWS][:].indirect(columns), values)
+            return windows[stripe % len(windows)][:].indirect(columns)
 
-        def early_product(block, grad):
-            acc = bank(PACK - 1 - block, "early%d" % block)
-            gradient(block, acc, HALF)
-            nc.scalar.copy(grad[:], acc[:, HALF:N])
-            return grad
+        def step_tile(stripe, place_of):
+            return tile("step_bf%d" % stripe, [P, 2 * PACK * P], BF16, place_of=place_of)
+
+        last_window = tile("window3", [P, T], F32, place_of="do_bf1")
+        nc.gpsimd.memset(last_window[:], 0.0)
+        windows.append(last_window)
 
         parts = [ds_part(0), ds_part(1)]
         ds_first = tile("ds_bf0", [P, PACK * HALF], BF16)
         ds_words(nc.vector, ds_first[:], 0, 0, HALF)
-        quantize(pw_mx, E4M3, N, pw_bf[0][:])
-        prepare_step(0)
-        quantize(ds_mx, E5M2, N, ds_first[:])
+        quantize(pw_mx, E4M3, 0, pw_bf[0][:])
+        operands = [stripe_codes(0, stripe_casts(nc.scalar, 0, step_tile(0, None)[:]))]
+        quantize(ds_mx, E5M2, 0, ds_first[:])
         pw_bf.append(pw_words(1, "ds_bf0"))
         ds_second = tile("ds_bf1", [P, PACK * HALF], BF16, place_of="step_bf0")
         ds_words(nc.vector, ds_second[:], 1, 0, HALF)
-        early_grads = [early_product(0, placed("early_grad0", [P, HALF], F32, 4096))]
-        quantize(pw_mx, E4M3, N + HALF, pw_bf[1][:])
-        quantize(ds_mx, E5M2, N + HALF, ds_second[:])
-        scatter(0, early_grads[0][:], halves[0])
-        prepare_step(1, placed("step_bf1", [P, 2 * PACK * P], BF16, 4096 + 1024))
 
-        prepared = 2
-        for block in range(D // P):
-            if prepared == step_of_block[block] + 1 and prepared < len(STEP_WIDTHS):
-                prepare_step(prepared)
-                prepared += 1
-            acc = bank(block, "grad%d" % block)
-            gradient(block, acc, N)
-            slots = halves[1] if block < len(early_grads) else slice(0, N)
-            grad = tile("grad_sb%d" % block, [P, slots.stop - slots.start], F32, place_of=grad_places.get(block))
-            nc.scalar.copy(grad[:], acc[:, slots])
-            scatter(block, grad[:], slots)
-            nc.sync.dma_start(out=out[block * P : (block + 1) * P, :], in_=windows[block % WINDOWS][:])
+        acc = bank(0, "grad0a")
+        gradient(operands[0], acc[:, 0:HALF], halves[0])
+        first = tile("first0", [P, HALF], F32)
+        nc.scalar.copy(first[:], acc[:, 0:HALF])
+        nc.scalar.activation(window_at(0, halves[0]), first[:], COPY)
+
+        quantize(pw_mx, E4M3, HALF, pw_bf[1][:])
+        quantize(ds_mx, E5M2, HALF, ds_second[:])
+        acc = bank(1, "grad0b")
+        gradient(operands[0], acc[:, 0:HALF], halves[1])
+        step_bytes = 2 * 2 * PACK * P
+        values = placed("step_bf1", [P, 2 * PACK * P], BF16, 4 * PACK * HALF)
+        operands.append(stripe_codes(1, stripe_casts(nc.vector, 1, values[:])))
+        values = placed("step_bf2", [P, 2 * PACK * P], BF16, 4 * PACK * HALF + step_bytes)
+        casts = stripe_casts(nc.scalar, 2, values[:])
+        second = tile("second0", [P, HALF], F32)
+        nc.vector.tensor_copy(second[:], acc[:, 0:HALF])
+
+        for stripe in range(STRIPES):
+            if stripe > 0:
+                acc = bank((stripe + 1) % 8, "grad%d" % stripe)
+                gradient(operands[stripe], acc[:], slice(0, N))
+                first = tile("first%d" % stripe, [P, HALF], F32, place_of="first0")
+                second = tile("second%d" % stripe, [P, HALF], F32)
+                nc.scalar.copy(first[:], acc[:, halves[0]])
+                nc.scalar.copy(second[:], acc[:, halves[1]])
+                nc.scalar.activation(window_at(stripe, halves[0]), first[:], COPY)
+            nc.vector.tensor_copy(window_at(stripe, halves[1]), second[:])
+            nc.sync.dma_start(out=out[stripe * P : (stripe + 1) * P, :], in_=windows[stripe % len(windows)][:])
+            if stripe == 0:
+                operands.append(stripe_codes(2, casts))
+            if stripe + AHEAD < STRIPES:
+                values = placed("step_bf%d" % (stripe + AHEAD), [P, 2 * PACK * P], BF16, 4 * PACK * HALF + stripe % 2 * step_bytes)
+                operands.append(stripe_codes(stripe + AHEAD, stripe_casts(nc.vector, stripe + AHEAD, values[:])))

@@ -29,7 +29,7 @@ HALF = N // 2
 LIST_BAND = 16
 PLANE_SHIFT = 16
 RUN = 4
-WINDOWS = 3
+WINDOWS = 2
 
 Q_GROUPS_ON_VECTOR = 44
 FIRST_GROUPS_ON_VECTOR = 32
@@ -57,13 +57,13 @@ def tile_attend_gat_sig_c_kernel(tc, qT, c_words, c_scales, doT, rw, qm, dom, of
 
         offsets = sb.tile([P, N // LIST_BAND], U16, name="offsets")
         nc.sync.dma_start(offsets[:], offs)
-        gate = tile("gate", [P, 2 * PACK - 1], F32)
-        for b in range(2):
-            nc.scalar.dma_start(
-                out=gate[b:P:2, :], in_=rw[0].rearrange("(g x) o -> g (x o)", x=2 * PACK)[:, b : b + 2 * PACK - 1]
-            )
         pool_words = tile("pool_words", [P, T], I32)
         nc.sync.dma_start(out=pool_words[:], in_=c_words[0].rearrange("p t b -> p (t b)").bitcast(I32))
+        gate = tile("gate", [P, 2 * PACK - 1], F32)
+        for b in range(2):
+            nc.sync.dma_start(
+                out=gate[b:P:2, :], in_=rw[0].rearrange("(g x) o -> g (x o)", x=2 * PACK)[:, b : b + 2 * PACK - 1]
+            )
 
         pool_scales = tile("pool_scales", [P, T // 4], I32)
         nc.gpsimd.memset(pool_scales[:], 0)
@@ -89,6 +89,8 @@ def tile_attend_gat_sig_c_kernel(tc, qT, c_words, c_scales, doT, rw, qm, dom, of
             nc.vector.memset(window[:], 0.0)
         neg_gate = tile("neg_gate", [P, 2 * PACK - 1], F32)
         nc.gpsimd.tensor_scalar(neg_gate[:], gate[:], -1.0, 0.0, MULT, ADD)
+        windows.append(tile("window2", [P, T], F32, place_of="gate"))
+        nc.gpsimd.memset(windows[2][:], 0.0)
 
         word_pairs = tile("word_pairs", [P, N], U32)
         nc.vector.tensor_copy(word_pairs[:], pool_words[:].bitcast(U32).indirect(offsets[:]))

@@ -31,12 +31,18 @@ PLANE_SHIFT = 16
 RUN = 4
 WINDOWS = 2
 
-Q_GROUPS_ON_VECTOR = 44
+Q_GROUPS_ON_VECTOR = 36
 FIRST_GROUPS_ON_VECTOR = 32
 PW_ROW_ON_VECTOR_FROM = 4
-DOM_CUT, QM_CUT = 512, 640
+CUT = 512
 STRIPES = D // P
-AHEAD = 3
+EARLY = 3
+KIB = 1024
+EVEN_CASTS = 16 * KIB
+SECOND0 = EVEN_CASTS + 6 * KIB
+ODD_CASTS = SECOND0 - 3 * KIB // 2
+PW_ROWS = 0
+FIRSTS = 26 * KIB
 
 
 def tile_attend_gat_sig_c_kernel(tc, qT, c_words, c_scales, doT, rw, qm, dom, offs, out):
@@ -81,25 +87,31 @@ def tile_attend_gat_sig_c_kernel(tc, qT, c_words, c_scales, doT, rw, qm, dom, of
         c_sc = [tile("c_sc%d" % o, [P, N], U8) for o in range(PASSES)]
         nc.gpsimd.memset(c_sc[1][:].bitcast(I32), 0)
 
-        pw_mx = (tile("pw_codes", [P, N], U32), tile("pw_scales", [P, N], U8))
+        pw_mx = (tile("pw_codes", [P, N], U32), placed("pw_scales", [P, N], U8, PW_ROWS + 2 * KIB))
         ds_mx = (tile("ds_codes", [P, N], U32), tile("ds_scales", [P, N], U8))
 
         windows = [tile("window%d" % w, [P, T], F32) for w in range(WINDOWS)]
-        for window in windows:
-            nc.vector.memset(window[:], 0.0)
+        nc.vector.memset(windows[0][:], 0.0)
+        nc.vector.memset(windows[1][:], 0.0)
         neg_gate = tile("neg_gate", [P, 2 * PACK - 1], F32)
         nc.gpsimd.tensor_scalar(neg_gate[:], gate[:], -1.0, 0.0, MULT, ADD)
         windows.append(tile("window2", [P, T], F32, place_of="gate"))
         nc.gpsimd.memset(windows[2][:], 0.0)
+        windows.append(tile("window3", [P, T], F32))
+        nc.vector.memset(windows[3][:], 0.0)
 
         word_pairs = tile("word_pairs", [P, N], U32)
         nc.vector.tensor_copy(word_pairs[:], pool_words[:].bitcast(U32).indirect(offsets[:]))
         nc.vector.tensor_copy(c_sc[0][:], pool_scales[:].bitcast(U8).indirect(offsets[:]))
-        c_codes = tile("c_codes", [P, PASSES * 2 * N], U8, place_of="pool_scales")
-        nc.vector.tensor_copy(
-            c_codes[:].bitcast(U16).rearrange("p (o n) -> p o n", o=PASSES),
-            word_pairs[:].bitcast(U16).rearrange("p (n o) -> p o n", o=PASSES),
-        )
+        c_codes = [tile("c_codes%d" % o, [P, 2 * N], U8, place_of=("pool_scales", "q_bf0")[o]) for o in range(PASSES)]
+
+        def part_words(o):
+            nc.vector.tensor_copy(
+                c_codes[o][:].bitcast(U16),
+                word_pairs[:].bitcast(U16).rearrange("p (n o) -> p o n", o=PASSES)[:, o],
+            )
+
+        part_words(0)
 
         def load_pass(name, src, o):
             raw = tile("%s%d" % (name, o), [P, PACK, R], F32)
@@ -107,27 +119,30 @@ def tile_attend_gat_sig_c_kernel(tc, qT, c_words, c_scales, doT, rw, qm, dom, of
             nc.sync.dma_start(out=raw[:], in_=rows.rearrange("(p j) w -> p j w", j=PACK))
             return raw
 
-        def load_queries(name, src, features):
-            raw = tile(name, [P, PACK, features.stop - features.start], F32)
+        def load_queries(raw, src, features):
             for t in range(PACK):
                 nc.sync.dma_start(
                     out=raw[:, t, :], in_=src[0, :, features].rearrange("(g t b) w -> t g b w", t=PACK, b=2)[t]
                 )
-            return raw
 
         q_raw = [load_pass("q_raw", qT, o) for o in range(PASSES)]
-        do_raw = [load_pass("do_raw", doT, 0)]
-        nc.sync.dma_start(out=c_sc[1][0 : P - PLANE_SHIFT, :].bitcast(I32), in_=c_sc[0][PLANE_SHIFT:P, :].bitcast(I32))
-        do_raw.append(load_pass("do_raw", doT, 1))
-        dom_raw, qm_raw = [], []
-        for k in range(2):
-            for name, src, raws, cut in (("dom", dom, dom_raw, DOM_CUT), ("qm", qm, qm_raw, QM_CUT)):
-                features = (slice(0, cut), slice(cut, D))[k]
-                raws.append((features, load_queries("%s_raw%d" % (name, k), src, features)))
-
-        def loaded(raws, first, width):
-            features, raw = raws[int(first >= raws[0][0].stop)]
-            return raw[:, :, first - features.start : first - features.start + width]
+        first_pass = tile("do_raw0", [P, PACK, R], F32)
+        first_rows = doT[0, 0:K_PASS, :].rearrange("(p j) w -> p j w", j=PACK)
+        nc.sync.dma_start(out=first_pass[:, 0:2, :], in_=first_rows[:, 0:2, :])
+        for first, count in ((0, 64), (64, 4), (96, 4)):
+            nc.sync.dma_start(
+                out=c_sc[1][first : first + count, :].bitcast(I32),
+                in_=c_sc[0][first + PLANE_SHIFT : first + PLANE_SHIFT + count, :].bitcast(I32),
+            )
+        nc.sync.dma_start(out=first_pass[:, 2:PACK, :], in_=first_rows[:, 2:PACK, :])
+        do_raw = [first_pass, load_pass("do_raw", doT, 1)]
+        dom_raw = tile("dom_raw", [P, PACK, CUT], F32)
+        load_queries(dom_raw, dom, slice(0, CUT))
+        qm_raw = tile("qm_raw", [P, PACK, CUT], F32)
+        load_queries(qm_raw, qm, slice(0, CUT))
+        late_raw = tile("late_raw", [P, 2, PACK, D - CUT], F32)
+        load_queries(late_raw[:, 0], dom, slice(CUT, D))
+        load_queries(late_raw[:, 1], qm, slice(CUT, D))
 
         def mx_tiles(name, words):
             return tile(name + "_codes", [P, words], U32), tile(name + "_scales", [P, words], U8)
@@ -138,34 +153,40 @@ def tile_attend_gat_sig_c_kernel(tc, qT, c_words, c_scales, doT, rw, qm, dom, of
             nc.vector.quantize_mx(out=codes[:, words].bitcast(fmt), scales=scales[:, words], in_=values)
 
         def score_pass(name, raw, o, groups_on_vector, operand, fmt, banks):
-            values = tile(name, [P, PACK * R], BF16)
+            if name == "do_bf1":
+                values = placed(name, [P, PACK * R], BF16, EVEN_CASTS - 4 * KIB)
+            else:
+                values = tile(name, [P, PACK * R], BF16)
             dst = values[:].rearrange("p (t g b j) -> p g t j b", t=PACK, b=2, j=PACK)
             src = raw[:].rearrange("p j (g t b) -> p g t j b", t=PACK, b=2)
-            for pair in (slice(0, 2), slice(2, PACK)):
-                nc.vector.tensor_copy(dst[:, 0:groups_on_vector, pair], src[:, 0:groups_on_vector, pair])
-                if groups_on_vector < GROUPS:
-                    nc.scalar.copy(dst[:, groups_on_vector:GROUPS, pair], src[:, groups_on_vector:GROUPS, pair])
             codes, scales = operand or mx_tiles(name, R)
+            for pair, groups in zip((slice(0, 2), slice(2, PACK)), groups_on_vector):
+                nc.vector.tensor_copy(dst[:, 0:groups, pair], src[:, 0:groups, pair])
+                if groups < GROUPS:
+                    nc.scalar.copy(dst[:, groups:GROUPS, pair], src[:, groups:GROUPS, pair])
             for t in range(PACK):
                 quantize((codes, scales), fmt, t * P, values[:, t * K_PASS : (t + 1) * K_PASS])
+            if name == "q_bf0":
+                part_words(1)
             for t in range(PACK):
                 nc.tensor.matmul_mx(
                     out=banks[t][:],
                     lhsT=codes[:, t * P : (t + 1) * P].bitcast(fmt),
                     lhsT_scale=scales[:, t * P : (t + 1) * P],
-                    rhs=c_codes[:, o * 2 * N : (o + 1) * 2 * N].bitcast(E2M1),
+                    rhs=c_codes[o][:].bitcast(E2M1),
                     rhs_scale=c_sc[o][:],
                     start=(o == 0),
                     stop=(o == PASSES - 1),
                 )
+            return codes, scales
 
         a_banks = [bank(t, "a%d" % t) for t in range(PACK)]
         dp_banks = [bank(PACK + t, "dp%d" % t) for t in range(PACK)]
         for o, operand in enumerate((None, None)):
-            score_pass("q_bf%d" % o, q_raw[o], o, (FIRST_GROUPS_ON_VECTOR, Q_GROUPS_ON_VECTOR)[o], operand, E4M3, a_banks)
+            score_pass("q_bf%d" % o, q_raw[o], o, ((28, 28), (Q_GROUPS_ON_VECTOR,) * 2)[o], operand, E4M3, a_banks)
         for o, operand in enumerate((None, None)):
-            score_pass("do_bf%d" % o, do_raw[o], o, (Q_GROUPS_ON_VECTOR, GROUPS)[o], operand, E5M2, dp_banks)
-        prob = tile("prob", [P, PACK, N], F32)
+            last_codes = score_pass("do_bf%d" % o, do_raw[o], o, ((52, 52), (GROUPS, GROUPS))[o], operand, E5M2, dp_banks)
+        prob = placed("prob", [P, PACK, N], F32, PW_ROWS)
         for t in range(PACK):
             nc.scalar.activation(out=prob[:, t, :], in_=a_banks[t][:], func=SIGMOID)
 
@@ -176,32 +197,22 @@ def tile_attend_gat_sig_c_kernel(tc, qT, c_words, c_scales, doT, rw, qm, dom, of
             return rows.rearrange("p t (c i) -> p c t i", i=RUN)
 
         halves = (slice(0, HALF), slice(HALF, N))
-        neg_pw, pw_bf = [], []
+        minus_pw = tile("minus_pw", [P, PACK, N], F32)
+        for t in range(PACK):
+            nc.scalar.activation(out=minus_pw[:, t, :], in_=prob[:, t, :], func=COPY, scale=neg_gate[:, 2 * t : 2 * t + 1])
+        neg_pw = [minus_pw[:, :, slots] for slots in halves]
 
-        def pw_words(h, place_of):
-            values = tile("pw_bf%d" % h, [P, PACK * HALF], BF16, place_of=place_of)
-            nc.scalar.activation(out=words_view(values[:]), in_=rows_view(neg_pw[h][:]), func=COPY, scale=-1.0)
+        def pw_words(h, values):
+            nc.scalar.activation(out=words_view(values[:]), in_=rows_view(neg_pw[h]), func=COPY, scale=-1.0)
             return values
 
-        for h, slots in enumerate(halves):
-            rows = tile("neg_pw%d" % h, [P, PACK, HALF], F32, place_of=(None, "do_raw1")[h])
-            for t in range(PACK):
-                minus_gate = neg_gate[:, 2 * t : 2 * t + 1]
-                if h == 0 and t >= PW_ROW_ON_VECTOR_FROM:
-                    nc.vector.tensor_scalar(rows[:, t, :], prob[:, t, slots], minus_gate, None, MULT)
-                else:
-                    nc.scalar.activation(out=rows[:, t, :], in_=prob[:, t, slots], func=COPY, scale=minus_gate)
-            neg_pw.append(rows)
-            if h == 0:
-                pw_bf.append(pw_words(0, None))
+        pw_bf = [pw_words(0, placed("pw_bf0", [P, PACK * HALF], BF16, EVEN_CASTS + 7 * KIB // 2))]
 
-        def ds_part(h):
-            rows = placed("part%d" % h, [P, PACK, HALF], F32, h * 4 * PACK * HALF)
+        def ds_part():
+            rows = tile("part", [P, PACK, N], F32)
             for t in range(PACK):
-                nc.vector.scalar_tensor_tensor(
-                    rows[:, t, :], prob[:, t, halves[h]], 1.0, dp_banks[t][:, halves[h]], SUB, MULT
-                )
-            return rows
+                nc.vector.scalar_tensor_tensor(rows[:, t, :], prob[:, t, :], 1.0, dp_banks[t][:], SUB, MULT)
+            return [rows[:, :, slots] for slots in halves]
 
         def ds_words(engine, values, h, first, count):
             slots = slice(first, first + count)
@@ -209,19 +220,22 @@ def tile_attend_gat_sig_c_kernel(tc, qT, c_words, c_scales, doT, rw, qm, dom, of
                 words_view(values), rows_view(parts[h][:, :, slots]), rows_view(neg_pw[h][:, :, slots]), MULT
             )
 
-        def stripe_casts(engine, stripe, values):
-            dom_bf, qm_bf = values[:, 0 : PACK * P], values[:, PACK * P : 2 * PACK * P]
-            copy = nc.vector.tensor_copy if engine is nc.vector else nc.scalar.copy
-            copy(words_view(dom_bf), rows_view(loaded(dom_raw, stripe * P, P)))
-            copy(words_view(qm_bf), rows_view(loaded(qm_raw, stripe * P, P)))
-            return dom_bf, qm_bf
+        def cast(copy, values, raw, stripe):
+            copy(words_view(values), rows_view(raw[:, :, stripe * P : (stripe + 1) * P]))
 
-        def stripe_codes(stripe, casts):
-            dom_mx = mx_tiles("dom%d" % stripe, P)
-            quantize(dom_mx, E5M2, 0, casts[0])
-            qm_mx = mx_tiles("qm%d" % stripe, P)
-            quantize(qm_mx, E4M3, 0, casts[1])
-            return dom_mx, qm_mx
+        def stripe_codes(stripe, dom_bf, qm_bf, place=None):
+            both = []
+            for k, (name, fmt, values) in enumerate((("dom", E5M2, dom_bf), ("qm", E4M3, qm_bf))):
+                if place is None or (stripe, name) in ((0, "dom"), (3, "dom")):
+                    operand = mx_tiles("%s%d" % (name, stripe), P)
+                else:
+                    operand = (
+                        tile("%s%d_codes" % (name, stripe), [P, P], U32),
+                        placed("%s%d_scales" % (name, stripe), [P, P], U8, place + KIB // 2 + k * P),
+                    )
+                quantize(operand, fmt, 0, values)
+                both.append(operand)
+            return both
 
         def gradient(operands, acc, slots):
             (dom_codes, dom_scales), (qm_codes, qm_scales) = operands
@@ -238,54 +252,116 @@ def tile_attend_gat_sig_c_kernel(tc, qT, c_words, c_scales, doT, rw, qm, dom, of
             columns = offsets[:, slots.start // LIST_BAND : slots.stop // LIST_BAND]
             return windows[stripe % len(windows)][:].indirect(columns)
 
-        def step_tile(stripe, place_of):
-            return tile("step_bf%d" % stripe, [P, 2 * PACK * P], BF16, place_of=place_of)
+        def store(stripe):
+            nc.sync.dma_start(out=out[stripe * P : (stripe + 1) * P, :], in_=windows[stripe % len(windows)][:])
 
-        last_window = tile("window3", [P, T], F32, place_of="do_bf1")
-        nc.gpsimd.memset(last_window[:], 0.0)
-        windows.append(last_window)
+        def product(stripe, slots, index):
+            acc = bank(index, "grad%d_%d" % (stripe, slots.start))[:, 0 : slots.stop - slots.start]
+            gradient(operands[stripe], acc, slots)
+            return acc
 
-        parts = [ds_part(0), ds_part(1)]
+        words = PACK * P
+        dom_early = placed("dom_early", [P, 2 * words], BF16, EVEN_CASTS - EARLY * KIB)
+        nc.gpsimd.tensor_scalar(
+            dom_early[:].rearrange("p (c t) -> p c t", t=PACK),
+            dom_raw[:, :, 0 : 2 * P].rearrange("p t c -> p c t"), 1.0, 0.0, MULT, ADD,
+        )
+        qm_early = [
+            placed("qm_bf0", [P, words], BF16, EVEN_CASTS + KIB),
+            tile("qm_bf1", [P, words], BF16),
+            placed("qm_bf2", [P, words], BF16, EVEN_CASTS),
+        ]
+
+        def early_codes(stripe, place=None):
+            dom_bf = dom_second[:] if stripe == 2 else dom_early[:, stripe * words : (stripe + 1) * words]
+            return stripe_codes(stripe, dom_bf, qm_early[stripe][:], place)
+
+        def late_casts(stripe, values=None):
+            if values is None:
+                place = (EVEN_CASTS + 3 * KIB // 2, ODD_CASTS)[stripe % 2]
+                values = placed("late_bf%d" % stripe, [P, 2 * words], BF16, place)[:]
+            first = stripe * P - CUT
+            nc.gpsimd.tensor_scalar(
+                values.rearrange("p (x c t) -> p x c t", x=2, t=PACK),
+                late_raw[:, :, :, first : first + P].rearrange("p x t c -> p x c t"), 1.0, 0.0, MULT, ADD,
+            )
+            return values
+
+        parts = ds_part()
+        idle = bank(2 * PACK - 1, "warm")
+        for repeat in range(3):
+            nc.tensor.matmul_mx(
+                out=idle[:], lhsT=last_codes[0][:, 0:P].bitcast(E5M2), lhsT_scale=last_codes[1][:, 0:P],
+                rhs=c_codes[0][:].bitcast(E2M1), rhs_scale=c_sc[0][:], start=True, stop=True,
+            )
         ds_first = tile("ds_bf0", [P, PACK * HALF], BF16)
         ds_words(nc.vector, ds_first[:], 0, 0, HALF)
         quantize(pw_mx, E4M3, 0, pw_bf[0][:])
-        operands = [stripe_codes(0, stripe_casts(nc.scalar, 0, step_tile(0, None)[:]))]
+        cast(nc.scalar.copy, qm_early[0][:], qm_raw, 0)
+        operands = [early_codes(0, PW_ROWS + 2 * KIB)]
         quantize(ds_mx, E5M2, 0, ds_first[:])
-        pw_bf.append(pw_words(1, "ds_bf0"))
-        ds_second = tile("ds_bf1", [P, PACK * HALF], BF16, place_of="step_bf0")
+        cast(nc.scalar.copy, qm_early[1][:], qm_raw, 1)
+        pw_bf.append(pw_words(1, placed("pw_bf1", [P, PACK * HALF], BF16, PW_ROWS)))
+        cast(nc.scalar.copy, qm_early[2][:], qm_raw, 2)
+        ds_second = placed("ds_bf1", [P, PACK * HALF], BF16, EVEN_CASTS + KIB)
         ds_words(nc.vector, ds_second[:], 1, 0, HALF)
 
-        acc = bank(0, "grad0a")
-        gradient(operands[0], acc[:, 0:HALF], halves[0])
+        acc = product(0, halves[0], 0)
         first = tile("first0", [P, HALF], F32)
-        nc.scalar.copy(first[:], acc[:, 0:HALF])
+        nc.scalar.copy(first[:], acc)
         nc.scalar.activation(window_at(0, halves[0]), first[:], COPY)
 
         quantize(pw_mx, E4M3, HALF, pw_bf[1][:])
         quantize(ds_mx, E5M2, HALF, ds_second[:])
-        acc = bank(1, "grad0b")
-        gradient(operands[0], acc[:, 0:HALF], halves[1])
-        step_bytes = 2 * 2 * PACK * P
-        values = placed("step_bf1", [P, 2 * PACK * P], BF16, 4 * PACK * HALF)
-        operands.append(stripe_codes(1, stripe_casts(nc.vector, 1, values[:])))
-        values = placed("step_bf2", [P, 2 * PACK * P], BF16, 4 * PACK * HALF + step_bytes)
-        casts = stripe_casts(nc.scalar, 2, values[:])
-        second = tile("second0", [P, HALF], F32)
-        nc.vector.tensor_copy(second[:], acc[:, 0:HALF])
+        acc = product(0, halves[1], 1)
+        dom_second = placed("dom_bf2", [P, words], BF16, EVEN_CASTS + 3 * KIB)
+        cast(nc.vector.tensor_copy, dom_second[:], dom_raw, 2)
+        operands.append(early_codes(1))
+        first1 = tile("first1", [P, HALF], F32)
+        nc.vector.tensor_copy(first1[:], product(1, halves[0], 2))
+        nc.scalar.activation(window_at(1, halves[0]), first1[:], COPY)
+        operands.append(early_codes(2))
+        second = placed("second0", [P, HALF], F32, SECOND0)
+        nc.vector.tensor_copy(second[:], acc)
+        fourth = placed("late_bf4", [P, 3 * words], BF16, EVEN_CASTS + KIB // 2)
+        qm_third = fourth[:, 0:words]
+        nc.gpsimd.tensor_scalar(
+            qm_third.rearrange("p (c t) -> p c t", t=PACK),
+            qm_raw[:, :, EARLY * P : (EARLY + 1) * P].rearrange("p t c -> p c t"), 1.0, 0.0, MULT, ADD,
+        )
+        pending = {4: late_casts(4, fourth[:, words : 3 * words])}
+        nc.vector.tensor_copy(window_at(0, halves[1]), second[:])
+        store(0)
 
-        for stripe in range(STRIPES):
-            if stripe > 0:
-                acc = bank((stripe + 1) % 8, "grad%d" % stripe)
-                gradient(operands[stripe], acc[:], slice(0, N))
-                first = tile("first%d" % stripe, [P, HALF], F32, place_of="first0")
-                second = tile("second%d" % stripe, [P, HALF], F32)
+        acc = product(1, halves[1], 1)
+        second = tile("second1", [P, HALF], F32, place_of="first1")
+        nc.scalar.copy(second[:], acc)
+        nc.scalar.activation(window_at(1, halves[1]), second[:], COPY)
+        acc = product(2, slice(0, N), 2)
+        store(1)
+
+        dom_third = placed("dom_bf3", [P, words], BF16, ODD_CASTS + KIB)
+        cast(nc.vector.tensor_copy, dom_third[:], dom_raw, 3)
+        first_at = {2: SECOND0 + KIB // 2 + P}
+        first = placed("first2", [P, HALF], F32, first_at[2])
+        nc.vector.tensor_copy(first[:], acc[:, halves[0]])
+        operands.append(stripe_codes(3, dom_third[:], qm_third, SECOND0 - P))
+
+        for stripe in range(2, STRIPES):
+            if stripe + 3 < STRIPES:
+                pending[stripe + 3] = late_casts(stripe + 3)
+            nc.vector.tensor_copy(window_at(stripe, halves[0]), first[:])
+            last = acc
+            if stripe + 1 < STRIPES:
+                acc = product(stripe + 1, slice(0, N), (stripe + 2) % 8)
+            second = tile("second%d" % stripe, [P, HALF], F32, place_of="qm%d_codes" % (stripe + 1))
+            nc.scalar.copy(second[:], last[:, halves[1]])
+            if stripe + 1 < STRIPES:
+                first_at[stripe + 1] = FIRSTS + stripe * KIB
+                first = placed("first%d" % (stripe + 1), [P, HALF], F32, first_at[stripe + 1])
                 nc.scalar.copy(first[:], acc[:, halves[0]])
-                nc.scalar.copy(second[:], acc[:, halves[1]])
-                nc.scalar.activation(window_at(stripe, halves[0]), first[:], COPY)
-            nc.vector.tensor_copy(window_at(stripe, halves[1]), second[:])
-            nc.sync.dma_start(out=out[stripe * P : (stripe + 1) * P, :], in_=windows[stripe % len(windows)][:])
-            if stripe == 0:
-                operands.append(stripe_codes(2, casts))
-            if stripe + AHEAD < STRIPES:
-                values = placed("step_bf%d" % (stripe + AHEAD), [P, 2 * PACK * P], BF16, 4 * PACK * HALF + stripe % 2 * step_bytes)
-                operands.append(stripe_codes(stripe + AHEAD, stripe_casts(nc.vector, stripe + AHEAD, values[:])))
+            nc.scalar.activation(window_at(stripe, halves[1]), second[:], COPY)
+            store(stripe)
+            if stripe + 2 < STRIPES:
+                values = pending[stripe + 2]
+                operands.append(stripe_codes(stripe + 2, values[:, 0:words], values[:, words : 2 * words], first_at[stripe]))

from contextlib import ExitStack

import concourse.mybir as mybir

N, T, D, R = 512, 2048, 1024, 512
FLOPS = 4 * 2 * D * R * N

F32 = mybir.dt.float32
BF16 = mybir.dt.bfloat16
I32 = mybir.dt.int32
U32 = mybir.dt.uint32
U16 = mybir.dt.uint16
U8 = mybir.dt.uint8
E4M3 = mybir.dt.float8_e4m3fn_x4
E5M2 = mybir.dt.float8_e5m2_x4
E2M1 = mybir.dt.float4_e2m1fn_x4
MULT = mybir.AluOpType.mult
ADD = mybir.AluOpType.add
SUB = mybir.AluOpType.subtract
SIGMOID = mybir.ActivationFunctionType.Sigmoid
COPY = mybir.ActivationFunctionType.Copy

P = 128
PACK = 4
K_PASS = P * PACK
PASSES = D // K_PASS
GROUPS = R // 8
HALF = N // 2
LIST_BAND = 16
PLANE_SHIFT = 16
RUN = 4
WINDOWS = 2

Q_GROUPS_ON_VECTOR = 36
FIRST_GROUPS_ON_VECTOR = 32
PW_ROW_ON_VECTOR_FROM = 4
CUT = 512
STRIPES = D // P
EARLY = 3
KIB = 1024
EVEN_CASTS = 16 * KIB
SECOND0 = EVEN_CASTS + 6 * KIB
ODD_CASTS = SECOND0 - 3 * KIB // 2
PW_ROWS = 0
FIRSTS = 26 * KIB


def tile_attend_gat_sig_c_kernel(tc, qT, c_words, c_scales, doT, rw, qm, dom, offs, out):
    nc = tc.nc
    with ExitStack() as ctx:
        sb = ctx.enter_context(tc.tile_pool(name="sb", bufs=1))
        shared = ctx.enter_context(tc.tile_pool(name="shared", bufs=1))
        ps = ctx.enter_context(tc.psum_pool(name="ps", bufs=1))

        def tile(name, shape, dtype, place_of=None):
            return sb.tile(shape, dtype, name=name, tag=place_of or name, align_bytes=64)

        def placed(name, shape, dtype, offset):
            return shared.tile(shape, dtype, name=name, offset=offset, align_bytes=64)

        def bank(index, name):
            return ps.tile([P, N], F32, name=name, tag="bank%d" % index)

        offsets = sb.tile([P, N // LIST_BAND], U16, name="offsets")
        nc.sync.dma_start(offsets[:], offs)
        pool_words = tile("pool_words", [P, T], I32)
        nc.sync.dma_start(out=pool_words[:], in_=c_words[0].rearrange("p t b -> p (t b)").bitcast(I32))
        gate = tile("gate", [P, 2 * PACK - 1], F32)
        for b in range(2):
            nc.sync.dma_start(
                out=gate[b:P:2, :], in_=rw[0].rearrange("(g x) o -> g (x o)", x=2 * PACK)[:, b : b + 2 * PACK - 1]
            )

        pool_scales = tile("pool_scales", [P, T // 4], I32)
        nc.gpsimd.memset(pool_scales[:], 0)
        scale_rows = c_scales.bitcast(I32)
        for i in range(4):
            nc.sync.dma_start(
                out=pool_scales[i:P:PLANE_SHIFT, :], in_=scale_rows[:, i:16:4, :].rearrange("o q t -> q o t")
            )

        warm_in = tile("warm_in", [P, 1], F32)
        warm_out = tile("warm_out", [P, 1], F32)
        nc.gpsimd.memset(warm_in[:], 0.0)
        nc.scalar.activation(out=warm_out[:], in_=warm_in[:], func=SIGMOID)

        c_sc = [tile("c_sc%d" % o, [P, N], U8) for o in range(PASSES)]
        nc.gpsimd.memset(c_sc[1][:].bitcast(I32), 0)

        pw_mx = (tile("pw_codes", [P, N], U32), placed("pw_scales", [P, N], U8, PW_ROWS + 2 * KIB))
        ds_mx = (tile("ds_codes", [P, N], U32), tile("ds_scales", [P, N], U8))

        windows = [tile("window%d" % w, [P, T], F32) for w in range(WINDOWS)]
        nc.vector.memset(windows[0][:], 0.0)
        nc.vector.memset(windows[1][:], 0.0)
        neg_gate = tile("neg_gate", [P, 2 * PACK - 1], F32)
        nc.gpsimd.tensor_scalar(neg_gate[:], gate[:], -1.0, 0.0, MULT, ADD)
        windows.append(tile("window2", [P, T], F32, place_of="gate"))
        nc.gpsimd.memset(windows[2][:], 0.0)
        windows.append(tile("window3", [P, T], F32))
        nc.vector.memset(windows[3][:], 0.0)

        word_pairs = tile("word_pairs", [P, N], U32)
        nc.vector.tensor_copy(word_pairs[:], pool_words[:].bitcast(U32).indirect(offsets[:]))
        nc.vector.tensor_copy(c_sc[0][:], pool_scales[:].bitcast(U8).indirect(offsets[:]))
        c_codes = [tile("c_codes%d" % o, [P, 2 * N], U8, place_of=("pool_scales", "q_bf0")[o]) for o in range(PASSES)]

        def part_words(o):
            nc.vector.tensor_copy(
                c_codes[o][:].bitcast(U16),
                word_pairs[:].bitcast(U16).rearrange("p (n o) -> p o n", o=PASSES)[:, o],
            )

        part_words(0)

        def load_pass(name, src, o):
            raw = tile("%s%d" % (name, o), [P, PACK, R], F32)
            rows = src[0, o * K_PASS : (o + 1) * K_PASS, :]
            nc.sync.dma_start(out=raw[:], in_=rows.rearrange("(p j) w -> p j w", j=PACK))
            return raw

        def load_queries(raw, src, features):
            for t in range(PACK):
                nc.sync.dma_start(
                    out=raw[:, t, :], in_=src[0, :, features].rearrange("(g t b) w -> t g b w", t=PACK, b=2)[t]
                )

        q_raw = [load_pass("q_raw", qT, o) for o in range(PASSES)]
        first_pass = tile("do_raw0", [P, PACK, R], F32)
        first_rows = doT[0, 0:K_PASS, :].rearrange("(p j) w -> p j w", j=PACK)
        nc.sync.dma_start(out=first_pass[:, 0:2, :], in_=first_rows[:, 0:2, :])
        for first, count in ((0, 64), (64, 4), (96, 4)):
            nc.sync.dma_start(
                out=c_sc[1][first : first + count, :].bitcast(I32),
                in_=c_sc[0][first + PLANE_SHIFT : first + PLANE_SHIFT + count, :].bitcast(I32),
            )
        nc.sync.dma_start(out=first_pass[:, 2:PACK, :], in_=first_rows[:, 2:PACK, :])
        do_raw = [first_pass, load_pass("do_raw", doT, 1)]
        dom_raw = tile("dom_raw", [P, PACK, CUT], F32)
        load_queries(dom_raw, dom, slice(0, CUT))
        qm_raw = tile("qm_raw", [P, PACK, CUT], F32)
        load_queries(qm_raw, qm, slice(0, CUT))
        late_raw = tile("late_raw", [P, 2, PACK, D - CUT], F32)
        load_queries(late_raw[:, 0], dom, slice(CUT, D))
        load_queries(late_raw[:, 1], qm, slice(CUT, D))

        def mx_tiles(name, words):
            return tile(name + "_codes", [P, words], U32), tile(name + "_scales", [P, words], U8)

        def quantize(operand, fmt, first_word, values):
            codes, scales = operand
            words = slice(first_word, first_word + values.shape[1] // PACK)
            nc.vector.quantize_mx(out=codes[:, words].bitcast(fmt), scales=scales[:, words], in_=values)

        def score_pass(name, raw, o, groups_on_vector, operand, fmt, banks):
            if name == "do_bf1":
                values = placed(name, [P, PACK * R], BF16, EVEN_CASTS - 4 * KIB)
            else:
                values = tile(name, [P, PACK * R], BF16)
            dst = values[:].rearrange("p (t g b j) -> p g t j b", t=PACK, b=2, j=PACK)
            src = raw[:].rearrange("p j (g t b) -> p g t j b", t=PACK, b=2)
            codes, scales = operand or mx_tiles(name, R)
            for pair, groups in zip((slice(0, 2), slice(2, PACK)), groups_on_vector):
                nc.vector.tensor_copy(dst[:, 0:groups, pair], src[:, 0:groups, pair])
                if groups < GROUPS:
                    nc.scalar.copy(dst[:, groups:GROUPS, pair], src[:, groups:GROUPS, pair])
            for t in range(PACK):
                quantize((codes, scales), fmt, t * P, values[:, t * K_PASS : (t + 1) * K_PASS])
            if name == "q_bf0":
                part_words(1)
            for t in range(PACK):
                nc.tensor.matmul_mx(
                    out=banks[t][:],
                    lhsT=codes[:, t * P : (t + 1) * P].bitcast(fmt),
                    lhsT_scale=scales[:, t * P : (t + 1) * P],
                    rhs=c_codes[o][:].bitcast(E2M1),
                    rhs_scale=c_sc[o][:],
                    start=(o == 0),
                    stop=(o == PASSES - 1),
                )
            return codes, scales

        a_banks = [bank(t, "a%d" % t) for t in range(PACK)]
        dp_banks = [bank(PACK + t, "dp%d" % t) for t in range(PACK)]
        for o, operand in enumerate((None, None)):
            score_pass("q_bf%d" % o, q_raw[o], o, ((28, 28), (Q_GROUPS_ON_VECTOR,) * 2)[o], operand, E4M3, a_banks)
        for o, operand in enumerate((None, None)):
            last_codes = score_pass("do_bf%d" % o, do_raw[o], o, ((52, 52), (GROUPS, GROUPS))[o], operand, E5M2, dp_banks)
        prob = placed("prob", [P, PACK, N], F32, PW_ROWS)
        for t in range(PACK):
            nc.scalar.activation(out=prob[:, t, :], in_=a_banks[t][:], func=SIGMOID)

        def words_view(values):
            return values.rearrange("p (c i t) -> p c t i", i=RUN, t=PACK)

        def rows_view(rows):
            return rows.rearrange("p t (c i) -> p c t i", i=RUN)

        halves = (slice(0, HALF), slice(HALF, N))
        minus_pw = tile("minus_pw", [P, PACK, N], F32)
        for t in range(PACK):
            nc.scalar.activation(out=minus_pw[:, t, :], in_=prob[:, t, :], func=COPY, scale=neg_gate[:, 2 * t : 2 * t + 1])
        neg_pw = [minus_pw[:, :, slots] for slots in halves]

        def pw_words(h, values):
            nc.scalar.activation(out=words_view(values[:]), in_=rows_view(neg_pw[h]), func=COPY, scale=-1.0)
            return values

        pw_bf = [pw_words(0, placed("pw_bf0", [P, PACK * HALF], BF16, EVEN_CASTS + 7 * KIB // 2))]

        def ds_part():
            rows = tile("part", [P, PACK, N], F32)
            for t in range(PACK):
                nc.vector.scalar_tensor_tensor(rows[:, t, :], prob[:, t, :], 1.0, dp_banks[t][:], SUB, MULT)
            return [rows[:, :, slots] for slots in halves]

        def ds_words(engine, values, h, first, count):
            slots = slice(first, first + count)
            engine.tensor_tensor(
                words_view(values), rows_view(parts[h][:, :, slots]), rows_view(neg_pw[h][:, :, slots]), MULT
            )

        def cast(copy, values, raw, stripe):
            copy(words_view(values), rows_view(raw[:, :, stripe * P : (stripe + 1) * P]))

        def stripe_codes(stripe, dom_bf, qm_bf, place=None):
            both = []
            for k, (name, fmt, values) in enumerate((("dom", E5M2, dom_bf), ("qm", E4M3, qm_bf))):
                if place is None or (stripe, name) in ((0, "dom"), (3, "dom")):
                    operand = mx_tiles("%s%d" % (name, stripe), P)
                else:
                    operand = (
                        tile("%s%d_codes" % (name, stripe), [P, P], U32),
                        placed("%s%d_scales" % (name, stripe), [P, P], U8, place + KIB // 2 + k * P),
                    )
                quantize(operand, fmt, 0, values)
                both.append(operand)
            return both

        def gradient(operands, acc, slots):
            (dom_codes, dom_scales), (qm_codes, qm_scales) = operands
            nc.tensor.matmul_mx(
                out=acc, lhsT=dom_codes[:].bitcast(E5M2), lhsT_scale=dom_scales[:],
                rhs=pw_mx[0][:, slots].bitcast(E4M3), rhs_scale=pw_mx[1][:, slots], start=True, stop=False,
            )
            nc.tensor.matmul_mx(
                out=acc, lhsT=qm_codes[:].bitcast(E4M3), lhsT_scale=qm_scales[:],
                rhs=ds_mx[0][:, slots].bitcast(E5M2), rhs_scale=ds_mx[1][:, slots], start=False, stop=True,
            )

        def window_at(stripe, slots):
            columns = offsets[:, slots.start // LIST_BAND : slots.stop // LIST_BAND]
            return windows[stripe % len(windows)][:].indirect(columns)

        def store(stripe):
            nc.sync.dma_start(out=out[stripe * P : (stripe + 1) * P, :], in_=windows[stripe % len(windows)][:])

        def product(stripe, slots, index):
            acc = bank(index, "grad%d_%d" % (stripe, slots.start))[:, 0 : slots.stop - slots.start]
            gradient(operands[stripe], acc, slots)
            return acc

        words = PACK * P
        dom_early = placed("dom_early", [P, 2 * words], BF16, EVEN_CASTS - EARLY * KIB)
        nc.gpsimd.tensor_scalar(
            dom_early[:].rearrange("p (c t) -> p c t", t=PACK),
            dom_raw[:, :, 0 : 2 * P].rearrange("p t c -> p c t"), 1.0, 0.0, MULT, ADD,
        )
        qm_early = [
            placed("qm_bf0", [P, words], BF16, EVEN_CASTS + KIB),
            tile("qm_bf1", [P, words], BF16),
            placed("qm_bf2", [P, words], BF16, EVEN_CASTS),
        ]

        def early_codes(stripe, place=None):
            dom_bf = dom_second[:] if stripe == 2 else dom_early[:, stripe * words : (stripe + 1) * words]
            return stripe_codes(stripe, dom_bf, qm_early[stripe][:], place)

        def late_casts(stripe, values=None):
            if values is None:
                place = (EVEN_CASTS + 3 * KIB // 2, ODD_CASTS)[stripe % 2]
                values = placed("late_bf%d" % stripe, [P, 2 * words], BF16, place)[:]
            first = stripe * P - CUT
            nc.gpsimd.tensor_scalar(
                values.rearrange("p (x c t) -> p x c t", x=2, t=PACK),
                late_raw[:, :, :, first : first + P].rearrange("p x t c -> p x c t"), 1.0, 0.0, MULT, ADD,
            )
            return values

        parts = ds_part()
        idle = bank(2 * PACK - 1, "warm")
        for repeat in range(3):
            nc.tensor.matmul_mx(
                out=idle[:], lhsT=last_codes[0][:, 0:P].bitcast(E5M2), lhsT_scale=last_codes[1][:, 0:P],
                rhs=c_codes[0][:].bitcast(E2M1), rhs_scale=c_sc[0][:], start=True, stop=True,
            )
        ds_first = tile("ds_bf0", [P, PACK * HALF], BF16)
        ds_words(nc.vector, ds_first[:], 0, 0, HALF)
        quantize(pw_mx, E4M3, 0, pw_bf[0][:])
        cast(nc.scalar.copy, qm_early[0][:], qm_raw, 0)
        operands = [early_codes(0, PW_ROWS + 2 * KIB)]
        quantize(ds_mx, E5M2, 0, ds_first[:])
        cast(nc.scalar.copy, qm_early[1][:], qm_raw, 1)
        pw_bf.append(pw_words(1, placed("pw_bf1", [P, PACK * HALF], BF16, PW_ROWS)))
        cast(nc.scalar.copy, qm_early[2][:], qm_raw, 2)
        ds_second = placed("ds_bf1", [P, PACK * HALF], BF16, EVEN_CASTS + KIB)
        ds_words(nc.vector, ds_second[:], 1, 0, HALF)

        acc = product(0, halves[0], 0)
        first = tile("first0", [P, HALF], F32)
        nc.scalar.copy(first[:], acc)
        nc.scalar.activation(window_at(0, halves[0]), first[:], COPY)

        quantize(pw_mx, E4M3, HALF, pw_bf[1][:])
        quantize(ds_mx, E5M2, HALF, ds_second[:])
        acc = product(0, halves[1], 1)
        dom_second = placed("dom_bf2", [P, words], BF16, EVEN_CASTS + 3 * KIB)
        cast(nc.vector.tensor_copy, dom_second[:], dom_raw, 2)
        operands.append(early_codes(1))
        first1 = tile("first1", [P, HALF], F32)
        nc.vector.tensor_copy(first1[:], product(1, halves[0], 2))
        nc.scalar.activation(window_at(1, halves[0]), first1[:], COPY)
        operands.append(early_codes(2))
        second = placed("second0", [P, HALF], F32, SECOND0)
        nc.vector.tensor_copy(second[:], acc)
        fourth = placed("late_bf4", [P, 3 * words], BF16, EVEN_CASTS + KIB // 2)
        qm_third = fourth[:, 0:words]
        nc.gpsimd.tensor_scalar(
            qm_third.rearrange("p (c t) -> p c t", t=PACK),
            qm_raw[:, :, EARLY * P : (EARLY + 1) * P].rearrange("p t c -> p c t"), 1.0, 0.0, MULT, ADD,
        )
        pending = {4: late_casts(4, fourth[:, words : 3 * words])}
        nc.vector.tensor_copy(window_at(0, halves[1]), second[:])
        store(0)

        acc = product(1, halves[1], 1)
        second = tile("second1", [P, HALF], F32, place_of="first1")
        nc.scalar.copy(second[:], acc)
        nc.scalar.activation(window_at(1, halves[1]), second[:], COPY)
        acc = product(2, slice(0, N), 2)
        store(1)

        dom_third = placed("dom_bf3", [P, words], BF16, ODD_CASTS + KIB)
        cast(nc.vector.tensor_copy, dom_third[:], dom_raw, 3)
        first_at = {2: SECOND0 + KIB // 2 + P}
        first = placed("first2", [P, HALF], F32, first_at[2])
        nc.vector.tensor_copy(first[:], acc[:, halves[0]])
        operands.append(stripe_codes(3, dom_third[:], qm_third, SECOND0 - P))

        for stripe in range(2, STRIPES):
            if stripe + 3 < STRIPES:
                pending[stripe + 3] = late_casts(stripe + 3)
            nc.vector.tensor_copy(window_at(stripe, halves[0]), first[:])
            last = acc
            if stripe + 1 < STRIPES:
                acc = product(stripe + 1, slice(0, N), (stripe + 2) % 8)
            second = tile("second%d" % stripe, [P, HALF], F32, place_of="qm%d_codes" % (stripe + 1))
            nc.scalar.copy(second[:], last[:, halves[1]])
            if stripe + 1 < STRIPES:
                first_at[stripe + 1] = FIRSTS + stripe * KIB
                first = placed("first%d" % (stripe + 1), [P, HALF], F32, first_at[stripe + 1])
                nc.scalar.copy(first[:], acc[:, halves[0]])
            nc.scalar.activation(window_at(stripe, halves[1]), second[:], COPY)
            store(stripe)
            if stripe + 2 < STRIPES:
                values = pending[stripe + 2]
                operands.append(stripe_codes(stripe + 2, values[:, 0:words], values[:, words : 2 * words], first_at[stripe]))
